import numpy as np
import ml_dtypes


def mxq(x, axis, fmt="e4m3"):
    dtype, down = {"e4m3": (ml_dtypes.float8_e4m3fn, 7), "e5m2": (ml_dtypes.float8_e5m2, 14)}[fmt]
    v = np.moveaxis(np.asarray(x, np.float32).astype(ml_dtypes.bfloat16).astype(np.float64), axis, -1)
    blocks = v.reshape(v.shape[:-1] + (-1, 32))
    amax = np.abs(blocks).max(-1, keepdims=True)
    byte = np.maximum(np.where(amax > 0, np.frexp(amax)[1] - 1 + 127, 0) - down, 1)
    scale = np.exp2(byte - 127.0)
    codes = (blocks / scale).astype(np.float32).astype(dtype).astype(np.float64)
    return np.moveaxis((codes * scale).reshape(v.shape), -1, axis)


WIDE = False


def mx_kscale(k):
    if not WIDE:
        return np.ones(k)
    levels = np.array([18, -18])
    if k % 512:
        return np.exp2(np.random.permutation(np.resize(levels, k // 32))).repeat(32)
    a = np.empty((k // 512, 16))
    for p in range(k // 512):
        a[p, :8] = np.random.permutation(np.resize(levels, 8))
        for g in range(8):
            far = levels[np.abs(levels - a[p, g]) >= 10]
            a[p, g + 8] = far[np.random.randint(len(far))]
    return np.exp2(a.ravel()).repeat(32)


def f64(x):
    return np.asarray(x).astype(np.float64)


def striped(idx):
    return np.tile(np.asarray(idx).reshape(-1, 16).T, (8, 1)).astype(np.uint16)


def unstriped(offs):
    return offs[:16].T.reshape(-1).astype(np.int64)

def planes(y):
    n, m = y.shape
    v = y.astype(np.float32).astype(ml_dtypes.bfloat16).astype(np.float64).reshape(n // 32, 32, m)
    top = np.abs(v).max(1)
    byte = np.clip(np.where(top > 0, np.frexp(top)[1] - 1 + 127 - 7, 1), 1, 254)
    codes = (v * np.exp2(127.0 - byte)[:, None, :]).reshape(n, m).astype(np.float32).astype(ml_dtypes.float8_e4m3fn).view(np.uint8)
    words = codes.reshape(n // 512, 128, 4, m).transpose(0, 1, 3, 2)
    return np.ascontiguousarray(words), np.ascontiguousarray(byte.astype(np.uint8).reshape(n // 512, 16, m))


def setup_inputs():
    n = np.random.standard_normal
    uni = np.random.uniform
    idx = np.random.permutation(2048)[:512]
    f_d = mx_kscale(512)
    f_f = mx_kscale(512)
    return {
        "xT": (n((512, 512)) * f_d[:, None]).astype(np.float32),
        "dz": (n((512, 512))).astype(np.float32),
        "cf": (uni(0.75, 1.3, (512, 1))).astype(np.float32),
        "si": np.tile(uni(0.75, 1.3, 512), (128, 1)).astype(np.float32),
        "U": (n((512, 512)) / np.sqrt(512) / f_d[:, None] * f_f[None, :]).astype(np.float32),
        "V": (n((512, 512)) / np.sqrt(512) / f_f[None, :]).astype(np.float32),
        "offs": striped(idx),
    }


def reference(xT, dz, cf, si, U, V, offs):
    idx = unstriped(offs)
    u = mxq(f64(U), 0, "e4m3").T @ mxq(f64(xT), 0, "e4m3")
    dv = f64(cf) * f64(si)[:1] * f64(dz) * u
    de = mxq(f64(V), 1, "e4m3") @ mxq(dv, 0, "e5m2")
    out_0 = np.zeros((512, 2048))
    out_0[:, idx] = de
    return (out_0,) + planes(out_0)

@@ -1,0 +1,286 @@
+from contextlib import ExitStack
+
+import concourse.mybir as mybir
+from concourse.masks import make_identity
+
+F32 = mybir.dt.float32
+BF16 = mybir.dt.bfloat16
+I32 = mybir.dt.int32
+U32 = mybir.dt.uint32
+U16 = mybir.dt.uint16
+U8 = mybir.dt.uint8
+E4M3 = mybir.dt.float8_e4m3fn_x4
+E5M2 = mybir.dt.float8_e5m2_x4
+MULT = mybir.AluOpType.mult
+COPY = mybir.ActivationFunctionType.Copy
+
+P = 128
+PACK = 4
+K = 512
+SAMPLES = 512
+ITEMS = 2048
+HALF = SAMPLES // 2
+CHUNK = 256
+CHUNKS = ITEMS // CHUNK
+SCALAR_WEAVES = 2
+
+FLOPS = 2 * 2 * K * K * SAMPLES
+BYTES = 4 * (4 * K * K + K + SAMPLES) + 2 * P * SAMPLES // 16 + 4 * K * ITEMS + K * ITEMS + 16 * ITEMS
+
+
+def tile_attend_gbpool_E_pl_kernel(tc, xT, dz, cf, si, U, V, offs, out_0, out_1, out_2):
+    nc = tc.nc
+    with ExitStack() as ctx:
+        sb = ctx.enter_context(tc.tile_pool(name="sb", bufs=1))
+        ps = ctx.enter_context(tc.psum_pool(name="ps", bufs=1))
+
+        def bank(number, name):
+            return ps.tile([P, 512], F32, tag="bank_%d" % number, name=name)
+
+        si_sb = sb.tile([P, PACK], F32, name="si_sb")
+        nc.scalar.dma_start(out=si_sb[:], in_=si[0:1, :].rearrange("o (n j) -> (o n) j", j=PACK))
+        cf_sb = sb.tile([P, PACK], F32, name="cf_sb")
+        nc.scalar.dma_start(out=cf_sb[:], in_=cf.rearrange("(p t) o -> p (t o)", t=PACK))
+
+        def load_half(name, source, h):
+            tile = sb.tile([P, PACK, HALF], F32, name="%s_%d" % (name, h))
+            rows = source.rearrange("(p j) c -> p j c", j=PACK)
+            nc.sync.dma_start(out=tile[:], in_=rows[:, :, h * HALF : (h + 1) * HALF])
+            return tile
+
+        v_rows = V.rearrange("(s r) f -> r s f", r=PACK)
+
+        def load_v(r):
+            tile = sb.tile([P, K], F32, name="v_raw_%d" % r)
+            nc.sync.dma_start(out=tile[:], in_=v_rows[r])
+            return tile
+
+        u_raw = [load_half("u_raw", U, h) for h in range(2)]
+        x_raw = [load_half("x_raw", xT, h) for h in range(2)]
+        dz_sb = [load_half("dz", dz, 0)]
+        v_raw = [load_v(0)]
+        dz_sb.append(load_half("dz", dz, 1))
+        offsets = sb.tile([P, SAMPLES // 16], U16, name="offsets")
+        nc.sync.dma_start(offsets[:], offs)
+        v_raw.extend([load_v(r) for r in range(1, PACK)])
+
+        ident = sb.tile([P, P], F32, name="ident")
+        make_identity(nc, ident[:])
+
+        dv_codes = sb.tile([P, HALF + SAMPLES], U32, name="dv_codes", align_bytes=64)
+        dv_scales = sb.tile([P, HALF + SAMPLES], U8, name="dv_scales", align_bytes=64)
+        windows = [sb.tile([P, ITEMS], F32, name="window_%d" % r) for r in range(PACK)]
+        for r in range(PACK - 1):
+            nc.vector.memset(windows[r][:], 0.0)
+        nc.vector.memset(dv_codes[:, 0:HALF], 0)
+        nc.vector.memset(dv_scales[:, 0:HALF], 0)
+
+        si_ps = bank(4, "si_ps")
+        for j in range(PACK):
+            nc.tensor.transpose(si_ps[:, j * P : (j + 1) * P], si_sb[:, j : j + 1].to_broadcast([P, P]), ident[:])
+        cs = sb.tile([P, PACK, SAMPLES], F32, name="cs")
+        for t in range(PACK):
+            nc.scalar.activation(
+                out=cs[:, t, :].rearrange("p (n j) -> p n j", j=PACK),
+                in_=si_ps[:].rearrange("p (j n) -> p n j", j=PACK),
+                func=COPY,
+                scale=cf_sb[:, t : t + 1],
+            )
+
+        u_bf = sb.tile([P, K * PACK], BF16, name="u_bf", align_bytes=64)
+        u_dst = u_bf[:].rearrange("p (t m j) -> p m j t", t=PACK, j=PACK)
+        for h in range(2):
+            nc.vector.tensor_copy(
+                out=u_dst[:, h * 64 : (h + 1) * 64], in_=u_raw[h][:].rearrange("p j (m t) -> p m j t", t=PACK)
+            )
+        u_codes = sb.tile([P, K], U32, name="u_codes", align_bytes=64)
+        u_scales = sb.tile([P, K], U8, name="u_scales", align_bytes=64)
+        nc.vector.quantize_mx(out=u_codes[:].bitcast(E4M3), scales=u_scales[:], in_=u_bf[:])
+
+        v_bf = sb.tile([P, K * PACK], BF16, name="v_bf", align_bytes=64)
+        v_codes = sb.tile([P, K], U32, name="v_codes", align_bytes=64)
+        v_scales = sb.tile([P, K], U8, name="v_scales", align_bytes=64)
+
+        def turn_v(r):
+            rounded = sb.tile([P, K], BF16, tag="v_rounded_%d" % (r % 2), name="v_rounded_%d" % r)
+            nc.scalar.copy(
+                out=rounded[:].rearrange("s (u p e) -> s u p e", u=2, e=2),
+                in_=v_raw[r][:].rearrange("s (p u e) -> s u p e", u=2, e=2),
+            )
+            words = rounded[:].bitcast(F32)
+            turned = bank(2 + r % 2, "v_turned_%d" % r)
+            for u in range(2):
+                nc.tensor.transpose(turned[:, u * P : (u + 1) * P], words[:, u * P : (u + 1) * P], ident[:])
+            nc.scalar.copy(
+                out=v_bf[:, r * K : (r + 1) * K].bitcast(F32).rearrange("p (s u) -> p s u", u=2),
+                in_=turned[:, 0 : 2 * P].rearrange("p (u s) -> p s u", u=2),
+            )
+
+        def quantise_v(first, count):
+            cols = slice(first * P, (first + count) * P)
+            nc.vector.quantize_mx(
+                out=v_codes[:, cols].bitcast(E4M3),
+                scales=v_scales[:, cols],
+                in_=v_bf[:, first * K : (first + count) * K],
+            )
+
+        x_bf = sb.tile([P, SAMPLES * PACK], BF16, name="x_bf", align_bytes=64)
+        x_codes = sb.tile([P, SAMPLES], U32, name="x_codes", align_bytes=64)
+        x_scales = sb.tile([P, SAMPLES], U8, name="x_scales", align_bytes=64)
+        w = [sb.tile([P, PACK * P], F32, name="w_%d" % q) for q in range(PACK)]
+        dv_bf = sb.tile([P, SAMPLES * PACK], BF16, name="dv_bf", align_bytes=64)
+        de = [sb.tile([P, SAMPLES], F32, name="de_%d" % r) for r in range(PACK)]
+
+        def quantise_x(q):
+            h, o = divmod(q, 2)
+            nc.scalar.copy(
+                out=x_bf[:, q * 512 : (q + 1) * 512].rearrange("p (c i j) -> p c j i", i=2, j=PACK),
+                in_=x_raw[h][:, :, o * P : (o + 1) * P].rearrange("p j (c i) -> p c j i", i=2),
+            )
+            nc.vector.quantize_mx(
+                out=x_codes[:, q * P : (q + 1) * P].bitcast(E4M3),
+                scales=x_scales[:, q * P : (q + 1) * P],
+                in_=x_bf[:, q * 512 : (q + 1) * 512],
+            )
+
+        def make_w(q):
+            u_ps = bank(q, "u_%d" % q)
+            for t in range(PACK):
+                nc.tensor.matmul_mx(
+                    out=u_ps[:, t * P : (t + 1) * P],
+                    lhsT=u_codes[:, t * P : (t + 1) * P].bitcast(E4M3),
+                    lhsT_scale=u_scales[:, t * P : (t + 1) * P],
+                    rhs=x_codes[:, q * P : (q + 1) * P].bitcast(E4M3),
+                    rhs_scale=x_scales[:, q * P : (q + 1) * P],
+                    start=True,
+                    stop=True,
+                )
+            nc.vector.tensor_tensor(
+                out=w[q][:].rearrange("p (t i) -> p t i", t=PACK),
+                in0=u_ps[:].rearrange("p (t i) -> p t i", t=PACK),
+                in1=cs[:, :, q * P : (q + 1) * P],
+                op=MULT,
+            )
+
+        def make_dv(q):
+            h, o = divmod(q, 2)
+            nc.vector.tensor_tensor(
+                out=dv_bf[:, q * 512 : (q + 1) * 512].rearrange("p (c i t) -> p c t i", i=2, t=PACK),
+                in0=w[q][:].rearrange("p (t c i) -> p c t i", i=2, t=PACK),
+                in1=dz_sb[h][:, :, o * P : (o + 1) * P].rearrange("p t (c i) -> p c t i", i=2),
+                op=MULT,
+            )
+
+        def quantise_dv(h):
+            cols = slice(HALF + h * HALF, HALF + (h + 1) * HALF)
+            nc.vector.quantize_mx(
+                out=dv_codes[:, cols].bitcast(E5M2),
+                scales=dv_scales[:, cols],
+                in_=dv_bf[:, h * HALF * PACK : (h + 1) * HALF * PACK],
+            )
+
+        def make_de(r, number, first, lo, hi):
+            acc = bank(number, "de_ps_%d_%d" % (r, lo))
+            nc.tensor.matmul_mx(
+                out=acc[:],
+                lhsT=v_codes[:, r * P : (r + 1) * P].bitcast(E4M3),
+                lhsT_scale=v_scales[:, r * P : (r + 1) * P],
+                rhs=dv_codes[:, first : first + SAMPLES].bitcast(E5M2),
+                rhs_scale=dv_scales[:, first : first + SAMPLES],
+                start=True,
+                stop=True,
+            )
+            shift = HALF - first
+            nc.scalar.copy(out=de[r][:, lo:hi], in_=acc[:, lo + shift : hi + shift])
+
+        def scatter(r, lo, hi):
+            nc.vector.tensor_copy(windows[r][:].indirect(offsets[:, lo // 16 : hi // 16]), de[r][:, lo:hi])
+
+        nc.vector.memset(windows[PACK - 1][:, 0 : ITEMS // 2], 0.0)
+        quantise_x(0)
+        nc.vector.memset(windows[PACK - 1][:, ITEMS // 2 : ITEMS], 0.0)
+        quantise_x(1)
+        make_w(0)
+        quantise_x(2)
+        make_w(1)
+        quantise_x(3)
+        make_w(2)
+        turn_v(0)
+        make_dv(0)
+        make_dv(1)
+        make_w(3)
+        turn_v(1)
+        quantise_dv(0)
+        quantise_v(0, 1)
+        turn_v(2)
+        make_de(0, 4, 0, 0, HALF)
+        make_dv(2)
+        make_dv(3)
+        turn_v(3)
+        quantise_v(1, 2)
+        quantise_dv(1)
+        scatter(0, 0, HALF)
+        make_de(0, 5, HALF, HALF, SAMPLES)
+        make_de(1, 6, HALF, 0, SAMPLES)
+        make_de(2, 7, HALF, 0, SAMPLES)
+        quantise_v(3, 1)
+        make_de(3, 0, HALF, 0, SAMPLES)
+        scatter(0, HALF, SAMPLES)
+
+        out_rows = out_0.rearrange("(s r) c -> r s c", r=PACK)
+        pairs = sb.tile([P, ITEMS * PACK], BF16, name="pairs")
+        pair_view = pairs[:].rearrange("p (n a c l) -> p n a c l", a=2, c=CHUNK, l=2)
+
+        def round_plane(r, first, count):
+            a, l = divmod(r, 2)
+            nc.scalar.copy(
+                out=pair_view[:, first : first + count, a, :, l],
+                in_=windows[r][:].rearrange("p (n c) -> p n c", c=CHUNK)[:, first : first + count, :],
+            )
+
+        for r in range(PACK):
+            if r > 0:
+                scatter(r, 0, SAMPLES)
+            nc.sync.dma_start(out=out_rows[r], in_=windows[r][:])
+            if r < PACK - 1:
+                round_plane(r, 0, CHUNKS)
+
+        y_bf = sb.tile([P, ITEMS * PACK], BF16, name="y_bf", align_bytes=64)
+        y_codes = sb.tile([P, ITEMS], U32, name="y_codes", align_bytes=64)
+        y_scales = sb.tile([P, ITEMS // PACK], U8, name="y_scales", align_bytes=64)
+        pair_words = pairs[:].bitcast(F32)
+        y_words = y_bf[:].bitcast(F32)
+        words_out = out_1[0].rearrange("p c l -> p (c l)").bitcast(I32)
+
+        def weave(n):
+            cols = slice(2 * n * CHUNK, 2 * (n + 1) * CHUNK)
+            dst = y_words[:, cols].rearrange("p (c i a) -> p c a i", i=2, a=2)
+            src = pair_words[:, cols].rearrange("p (a c i) -> p c a i", i=2, a=2)
+            if n >= CHUNKS - SCALAR_WEAVES:
+                nc.scalar.copy(out=dst, in_=src)
+            else:
+                nc.vector.tensor_copy(out=dst, in_=src)
+
+        def quantise_y(n):
+            lo, hi = n * CHUNK, (n + 1) * CHUNK
+            group, side = divmod(n, 2)
+            nc.vector.quantize_mx(
+                out=y_codes[:, lo:hi].bitcast(E4M3),
+                scales=y_scales[4 * group : P, side * CHUNK : (side + 1) * CHUNK],
+                in_=y_bf[:, PACK * lo : PACK * hi],
+            )
+            if side == 1:
+                nc.sync.dma_start(out=words_out[:, lo - CHUNK : hi], in_=y_codes[:, lo - CHUNK : hi].bitcast(I32))
+
+        for n in range(CHUNKS):
+            round_plane(PACK - 1, n, 1)
+        for n in range(CHUNKS):
+            weave(n)
+            if n >= 1:
+                quantise_y(n - 1)
+        quantise_y(CHUNKS - 1)
+
+        scales_out = out_2[0].bitcast(I32).rearrange("(q j) (g c) -> q g j c", j=4, g=4)
+        for quad in range(4):
+            queue = nc.scalar if quad % 2 else nc.sync
+            queue.dma_start(out=scales_out[quad], in_=y_scales[32 * quad : 32 * quad + 16, :].bitcast(I32))

@@ -1,7 +1,6 @@
 from contextlib import ExitStack
 
 import concourse.mybir as mybir
-from concourse.masks import make_identity
 
 F32 = mybir.dt.float32
 BF16 = mybir.dt.bfloat16
@@ -38,9 +37,9 @@ def tile_attend_gbpool_E_pl_kernel(tc, xT, dz, cf, si, U, V, offs, out_0, out_1,
             return ps.tile([P, 512], F32, tag="bank_%d" % number, name=name)
 
         si_sb = sb.tile([P, PACK], F32, name="si_sb")
-        nc.scalar.dma_start(out=si_sb[:], in_=si[0:1, :].rearrange("o (n j) -> (o n) j", j=PACK))
+        nc.sync.dma_start(out=si_sb[:], in_=si[0:1, :].rearrange("o (n j) -> (o n) j", j=PACK))
         cf_sb = sb.tile([P, PACK], F32, name="cf_sb")
-        nc.scalar.dma_start(out=cf_sb[:], in_=cf.rearrange("(p t) o -> p (t o)", t=PACK))
+        nc.sync.dma_start(out=cf_sb[:], in_=cf.rearrange("(p t) o -> p (t o)", t=PACK))
 
         def load_half(name, source, h):
             tile = sb.tile([P, PACK, HALF], F32, name="%s_%d" % (name, h))
@@ -65,13 +64,26 @@ def tile_attend_gbpool_E_pl_kernel(tc, xT, dz, cf, si, U, V, offs, out_0, out_1,
         v_raw.extend([load_v(r) for r in range(1, PACK)])
 
         ident = sb.tile([P, P], F32, name="ident")
-        make_identity(nc, ident[:])
+        zeros = sb.tile([P, P], F32, tag="zeros_then_window", name="zeros")
+        nc.gpsimd.memset(zeros[:], 0.0)
+        nc.gpsimd.affine_select(
+            out=ident[:],
+            in_=zeros[:],
+            compare_op=mybir.AluOpType.not_equal,
+            fill=1.0,
+            base=0,
+            pattern=[[-1, P]],
+            channel_multiplier=1,
+        )
 
         dv_codes = sb.tile([P, HALF + SAMPLES], U32, name="dv_codes", align_bytes=64)
         dv_scales = sb.tile([P, HALF + SAMPLES], U8, name="dv_scales", align_bytes=64)
-        windows = [sb.tile([P, ITEMS], F32, name="window_%d" % r) for r in range(PACK)]
-        for r in range(PACK - 1):
-            nc.vector.memset(windows[r][:], 0.0)
+        windows = [
+            sb.tile([P, ITEMS], F32, name="window_0"),
+            sb.tile([P, ITEMS], F32, tag="zeros_then_window", name="window_1"),
+        ]
+        nc.vector.memset(windows[0][:], 0.0)
+        nc.gpsimd.memset(windows[1][:], 0.0)
         nc.vector.memset(dv_codes[:, 0:HALF], 0)
         nc.vector.memset(dv_scales[:, 0:HALF], 0)
 
@@ -124,10 +136,10 @@ def tile_attend_gbpool_E_pl_kernel(tc, xT, dz, cf, si, U, V, offs, out_0, out_1,
                 in_=v_bf[:, first * K : (first + count) * K],
             )
 
-        x_bf = sb.tile([P, SAMPLES * PACK], BF16, name="x_bf", align_bytes=64)
+        x_bf = sb.tile([P, SAMPLES * PACK], BF16, tag="x_then_window", name="x_bf", align_bytes=64)
         x_codes = sb.tile([P, SAMPLES], U32, name="x_codes", align_bytes=64)
         x_scales = sb.tile([P, SAMPLES], U8, name="x_scales", align_bytes=64)
-        w = [sb.tile([P, PACK * P], F32, name="w_%d" % q) for q in range(PACK)]
+        w = [sb.tile([P, PACK, HALF], F32, name="w_%d" % h) for h in range(2)]
         dv_bf = sb.tile([P, SAMPLES * PACK], BF16, name="dv_bf", align_bytes=64)
         de = [sb.tile([P, SAMPLES], F32, name="de_%d" % r) for r in range(PACK)]
 
@@ -156,18 +168,17 @@ def tile_attend_gbpool_E_pl_kernel(tc, xT, dz, cf, si, U, V, offs, out_0, out_1,
                     stop=True,
                 )
             nc.vector.tensor_tensor(
-                out=w[q][:].rearrange("p (t i) -> p t i", t=PACK),
+                out=w[q // 2][:, :, (q % 2) * P : (q % 2 + 1) * P],
                 in0=u_ps[:].rearrange("p (t i) -> p t i", t=PACK),
                 in1=cs[:, :, q * P : (q + 1) * P],
                 op=MULT,
             )
 
-        def make_dv(q):
-            h, o = divmod(q, 2)
+        def make_dv(h):
             nc.vector.tensor_tensor(
-                out=dv_bf[:, q * 512 : (q + 1) * 512].rearrange("p (c i t) -> p c t i", i=2, t=PACK),
-                in0=w[q][:].rearrange("p (t c i) -> p c t i", i=2, t=PACK),
-                in1=dz_sb[h][:, :, o * P : (o + 1) * P].rearrange("p t (c i) -> p c t i", i=2),
+                out=dv_bf[:, h * HALF * PACK : (h + 1) * HALF * PACK].rearrange("p (c i t) -> p c t i", i=2, t=PACK),
+                in0=w[h][:].rearrange("p t (c i) -> p c t i", i=2),
+                in1=dz_sb[h][:].rearrange("p t (c i) -> p c t i", i=2),
                 op=MULT,
             )
 
@@ -196,26 +207,25 @@ def tile_attend_gbpool_E_pl_kernel(tc, xT, dz, cf, si, U, V, offs, out_0, out_1,
         def scatter(r, lo, hi):
             nc.vector.tensor_copy(windows[r][:].indirect(offsets[:, lo // 16 : hi // 16]), de[r][:, lo:hi])
 
-        nc.vector.memset(windows[PACK - 1][:, 0 : ITEMS // 2], 0.0)
         quantise_x(0)
-        nc.vector.memset(windows[PACK - 1][:, ITEMS // 2 : ITEMS], 0.0)
         quantise_x(1)
         make_w(0)
         quantise_x(2)
         make_w(1)
         quantise_x(3)
+        windows.append(sb.tile([P, ITEMS], F32, tag="x_then_window", name="window_2", align_bytes=64))
+        nc.gpsimd.memset(windows[2][:], 0.0)
+        windows.append(windows[0])
         make_w(2)
         turn_v(0)
         make_dv(0)
-        make_dv(1)
         make_w(3)
         turn_v(1)
         quantise_dv(0)
         quantise_v(0, 1)
         turn_v(2)
         make_de(0, 4, 0, 0, HALF)
-        make_dv(2)
-        make_dv(3)
+        make_dv(1)
         turn_v(3)
         quantise_v(1, 2)
         quantise_dv(1)

@@ -11,7 +11,6 @@ U8 = mybir.dt.uint8
 E4M3 = mybir.dt.float8_e4m3fn_x4
 E5M2 = mybir.dt.float8_e5m2_x4
 MULT = mybir.AluOpType.mult
-COPY = mybir.ActivationFunctionType.Copy
 
 P = 128
 PACK = 4
@@ -90,14 +89,10 @@ def tile_attend_gbpool_E_pl_kernel(tc, xT, dz, cf, si, U, V, offs, out_0, out_1,
         si_ps = bank(4, "si_ps")
         for j in range(PACK):
             nc.tensor.transpose(si_ps[:, j * P : (j + 1) * P], si_sb[:, j : j + 1].to_broadcast([P, P]), ident[:])
-        cs = sb.tile([P, PACK, SAMPLES], F32, name="cs")
-        for t in range(PACK):
-            nc.scalar.activation(
-                out=cs[:, t, :].rearrange("p (n j) -> p n j", j=PACK),
-                in_=si_ps[:].rearrange("p (j n) -> p n j", j=PACK),
-                func=COPY,
-                scale=cf_sb[:, t : t + 1],
-            )
+        si_all = sb.tile([P, SAMPLES], F32, name="si_all")
+        nc.scalar.copy(
+            out=si_all[:].rearrange("p (n j) -> p n j", j=PACK), in_=si_ps[:].rearrange("p (j n) -> p n j", j=PACK)
+        )
 
         u_bf = sb.tile([P, K * PACK], BF16, name="u_bf", align_bytes=64)
         u_dst = u_bf[:].rearrange("p (t m j) -> p m j t", t=PACK, j=PACK)
@@ -120,7 +115,7 @@ def tile_attend_gbpool_E_pl_kernel(tc, xT, dz, cf, si, U, V, offs, out_0, out_1,
                 in_=v_raw[r][:].rearrange("s (p u e) -> s u p e", u=2, e=2),
             )
             words = rounded[:].bitcast(F32)
-            turned = bank(2 + r % 2, "v_turned_%d" % r)
+            turned = bank(r % 2, "v_turned_%d" % r)
             for u in range(2):
                 nc.tensor.transpose(turned[:, u * P : (u + 1) * P], words[:, u * P : (u + 1) * P], ident[:])
             nc.scalar.copy(
@@ -143,36 +138,46 @@ def tile_attend_gbpool_E_pl_kernel(tc, xT, dz, cf, si, U, V, offs, out_0, out_1,
         dv_bf = sb.tile([P, SAMPLES * PACK], BF16, name="dv_bf", align_bytes=64)
         de = [sb.tile([P, SAMPLES], F32, name="de_%d" % r) for r in range(PACK)]
 
-        def quantise_x(q):
-            h, o = divmod(q, 2)
-            nc.scalar.copy(
-                out=x_bf[:, q * 512 : (q + 1) * 512].rearrange("p (c i j) -> p c j i", i=2, j=PACK),
-                in_=x_raw[h][:, :, o * P : (o + 1) * P].rearrange("p j (c i) -> p c j i", i=2),
-            )
+        def quantise_x(h):
+            for o, copy in enumerate((nc.scalar.copy, nc.scalar.copy if h else nc.vector.tensor_copy)):
+                q = 2 * h + o
+                copy(
+                    out=x_bf[:, q * 512 : (q + 1) * 512].rearrange("p (c i j) -> p c j i", i=2, j=PACK),
+                    in_=x_raw[h][:, :, o * P : (o + 1) * P].rearrange("p j (c i) -> p c j i", i=2),
+                )
+
+        def codes_x(h):
             nc.vector.quantize_mx(
-                out=x_codes[:, q * P : (q + 1) * P].bitcast(E4M3),
-                scales=x_scales[:, q * P : (q + 1) * P],
-                in_=x_bf[:, q * 512 : (q + 1) * 512],
+                out=x_codes[:, h * HALF : (h + 1) * HALF].bitcast(E4M3),
+                scales=x_scales[:, h * HALF : (h + 1) * HALF],
+                in_=x_bf[:, h * HALF * PACK : (h + 1) * HALF * PACK],
             )
 
-        def make_w(q):
-            u_ps = bank(q, "u_%d" % q)
-            for t in range(PACK):
-                nc.tensor.matmul_mx(
-                    out=u_ps[:, t * P : (t + 1) * P],
-                    lhsT=u_codes[:, t * P : (t + 1) * P].bitcast(E4M3),
-                    lhsT_scale=u_scales[:, t * P : (t + 1) * P],
-                    rhs=x_codes[:, q * P : (q + 1) * P].bitcast(E4M3),
-                    rhs_scale=x_scales[:, q * P : (q + 1) * P],
-                    start=True,
-                    stop=True,
-                )
-            nc.vector.tensor_tensor(
-                out=w[q // 2][:, :, (q % 2) * P : (q % 2 + 1) * P],
-                in0=u_ps[:].rearrange("p (t i) -> p t i", t=PACK),
-                in1=cs[:, :, q * P : (q + 1) * P],
-                op=MULT,
-            )
+        def make_w(h):
+            cols = slice(h * HALF, (h + 1) * HALF)
+            for pair in range(2):
+                u_ps = bank(2 * h + pair, "u_%d_%d" % (h, pair))
+                for o in range(2):
+                    t = 2 * pair + o
+                    nc.tensor.matmul_mx(
+                        out=u_ps[:, o * HALF : (o + 1) * HALF],
+                        lhsT=u_codes[:, t * P : (t + 1) * P].bitcast(E4M3),
+                        lhsT_scale=u_scales[:, t * P : (t + 1) * P],
+                        rhs=x_codes[:, cols].bitcast(E4M3),
+                        rhs_scale=x_scales[:, cols],
+                        start=True,
+                        stop=True,
+                    )
+                for o in range(2):
+                    t = 2 * pair + o
+                    nc.vector.scalar_tensor_tensor(
+                        out=w[h][:, t, :],
+                        in0=u_ps[:, o * HALF : (o + 1) * HALF],
+                        scalar=cf_sb[:, t : t + 1],
+                        in1=si_all[:, cols],
+                        op0=MULT,
+                        op1=MULT,
+                    )
 
         def make_dv(h):
             nc.vector.tensor_tensor(
@@ -208,18 +213,16 @@ def tile_attend_gbpool_E_pl_kernel(tc, xT, dz, cf, si, U, V, offs, out_0, out_1,
             nc.vector.tensor_copy(windows[r][:].indirect(offsets[:, lo // 16 : hi // 16]), de[r][:, lo:hi])
 
         quantise_x(0)
+        codes_x(0)
         quantise_x(1)
         make_w(0)
-        quantise_x(2)
-        make_w(1)
-        quantise_x(3)
+        codes_x(1)
         windows.append(sb.tile([P, ITEMS], F32, tag="x_then_window", name="window_2", align_bytes=64))
         nc.gpsimd.memset(windows[2][:], 0.0)
         windows.append(windows[0])
-        make_w(2)
-        turn_v(0)
         make_dv(0)
-        make_w(3)
+        make_w(1)
+        turn_v(0)
         turn_v(1)
         quantise_dv(0)
         quantise_v(0, 1)
@@ -234,16 +237,16 @@ def tile_attend_gbpool_E_pl_kernel(tc, xT, dz, cf, si, U, V, offs, out_0, out_1,
         make_de(1, 6, HALF, 0, SAMPLES)
         make_de(2, 7, HALF, 0, SAMPLES)
         quantise_v(3, 1)
-        make_de(3, 0, HALF, 0, SAMPLES)
+        make_de(3, 2, HALF, 0, SAMPLES)
         scatter(0, HALF, SAMPLES)
 
         out_rows = out_0.rearrange("(s r) c -> r s c", r=PACK)
         pairs = sb.tile([P, ITEMS * PACK], BF16, name="pairs")
         pair_view = pairs[:].rearrange("p (n a c l) -> p n a c l", a=2, c=CHUNK, l=2)
 
-        def round_plane(r, first, count):
+        def round_plane(r, first, count, copy):
             a, l = divmod(r, 2)
-            nc.scalar.copy(
+            copy(
                 out=pair_view[:, first : first + count, a, :, l],
                 in_=windows[r][:].rearrange("p (n c) -> p n c", c=CHUNK)[:, first : first + count, :],
             )
@@ -253,7 +256,7 @@ def tile_attend_gbpool_E_pl_kernel(tc, xT, dz, cf, si, U, V, offs, out_0, out_1,
                 scatter(r, 0, SAMPLES)
             nc.sync.dma_start(out=out_rows[r], in_=windows[r][:])
             if r < PACK - 1:
-                round_plane(r, 0, CHUNKS)
+                round_plane(r, 0, CHUNKS, nc.scalar.copy)
 
         y_bf = sb.tile([P, ITEMS * PACK], BF16, name="y_bf", align_bytes=64)
         y_codes = sb.tile([P, ITEMS], U32, name="y_codes", align_bytes=64)
@@ -279,11 +282,13 @@ def tile_attend_gbpool_E_pl_kernel(tc, xT, dz, cf, si, U, V, offs, out_0, out_1,
                 scales=y_scales[4 * group : P, side * CHUNK : (side + 1) * CHUNK],
                 in_=y_bf[:, PACK * lo : PACK * hi],
             )
-            if side == 1:
+            if n >= CHUNKS - 2:
+                nc.sync.dma_start(out=words_out[:, lo:hi], in_=y_codes[:, lo:hi].bitcast(I32))
+            elif side == 1:
                 nc.sync.dma_start(out=words_out[:, lo - CHUNK : hi], in_=y_codes[:, lo - CHUNK : hi].bitcast(I32))
 
         for n in range(CHUNKS):
-            round_plane(PACK - 1, n, 1)
+            round_plane(PACK - 1, n, 1, nc.scalar.copy)
         for n in range(CHUNKS):
             weave(n)
             if n >= 1:

@@ -21,6 +21,7 @@ HALF = SAMPLES // 2
 CHUNK = 256
 CHUNKS = ITEMS // CHUNK
 SCALAR_WEAVES = 2
+U_VECTOR = 88
 
 FLOPS = 2 * 2 * K * K * SAMPLES
 BYTES = 4 * (4 * K * K + K + SAMPLES) + 2 * P * SAMPLES // 16 + 4 * K * ITEMS + K * ITEMS + 16 * ITEMS
@@ -53,17 +54,18 @@ def tile_attend_gbpool_E_pl_kernel(tc, xT, dz, cf, si, U, V, offs, out_0, out_1,
             nc.sync.dma_start(out=tile[:], in_=v_rows[r])
             return tile
 
-        u_raw = [load_half("u_raw", U, h) for h in range(2)]
+        u_raw = sb.tile([P, PACK, K], F32, name="u_raw")
+        nc.sync.dma_start(out=u_raw[:], in_=U.rearrange("(p j) c -> p j c", j=PACK))
         x_raw = [load_half("x_raw", xT, h) for h in range(2)]
         dz_sb = [load_half("dz", dz, 0)]
-        v_raw = [load_v(0)]
+        v_raw = [load_v(0), load_v(1)]
         dz_sb.append(load_half("dz", dz, 1))
         offsets = sb.tile([P, SAMPLES // 16], U16, name="offsets")
         nc.sync.dma_start(offsets[:], offs)
-        v_raw.extend([load_v(r) for r in range(1, PACK)])
+        v_raw.extend([load_v(r) for r in range(2, PACK)])
 
         ident = sb.tile([P, P], F32, name="ident")
-        zeros = sb.tile([P, P], F32, tag="zeros_then_window", name="zeros")
+        zeros = sb.tile([P, P], F32, name="zeros")
         nc.gpsimd.memset(zeros[:], 0.0)
         nc.gpsimd.affine_select(
             out=ident[:],
@@ -77,14 +79,12 @@ def tile_attend_gbpool_E_pl_kernel(tc, xT, dz, cf, si, U, V, offs, out_0, out_1,
 
         dv_codes = sb.tile([P, HALF + SAMPLES], U32, name="dv_codes", align_bytes=64)
         dv_scales = sb.tile([P, HALF + SAMPLES], U8, name="dv_scales", align_bytes=64)
-        windows = [
-            sb.tile([P, ITEMS], F32, name="window_0"),
-            sb.tile([P, ITEMS], F32, tag="zeros_then_window", name="window_1"),
-        ]
-        nc.vector.memset(windows[0][:], 0.0)
-        nc.gpsimd.memset(windows[1][:], 0.0)
+        windows = [sb.tile([P, ITEMS], F32, name="window_%d" % r) for r in range(PACK - 1)]
         nc.vector.memset(dv_codes[:, 0:HALF], 0)
         nc.vector.memset(dv_scales[:, 0:HALF], 0)
+        for window in windows:
+            nc.vector.memset(window[:], 0.0)
+        windows.append(windows[0])
 
         si_ps = bank(4, "si_ps")
         for j in range(PACK):
@@ -96,10 +96,9 @@ def tile_attend_gbpool_E_pl_kernel(tc, xT, dz, cf, si, U, V, offs, out_0, out_1,
 
         u_bf = sb.tile([P, K * PACK], BF16, name="u_bf", align_bytes=64)
         u_dst = u_bf[:].rearrange("p (t m j) -> p m j t", t=PACK, j=PACK)
-        for h in range(2):
-            nc.vector.tensor_copy(
-                out=u_dst[:, h * 64 : (h + 1) * 64], in_=u_raw[h][:].rearrange("p j (m t) -> p m j t", t=PACK)
-            )
+        u_src = u_raw[:].rearrange("p j (m t) -> p m j t", t=PACK)
+        nc.vector.tensor_copy(out=u_dst[:, 0:U_VECTOR], in_=u_src[:, 0:U_VECTOR])
+        nc.scalar.copy(out=u_dst[:, U_VECTOR:P], in_=u_src[:, U_VECTOR:P])
         u_codes = sb.tile([P, K], U32, name="u_codes", align_bytes=64)
         u_scales = sb.tile([P, K], U8, name="u_scales", align_bytes=64)
         nc.vector.quantize_mx(out=u_codes[:].bitcast(E4M3), scales=u_scales[:], in_=u_bf[:])
@@ -131,7 +130,7 @@ def tile_attend_gbpool_E_pl_kernel(tc, xT, dz, cf, si, U, V, offs, out_0, out_1,
                 in_=v_bf[:, first * K : (first + count) * K],
             )
 
-        x_bf = sb.tile([P, SAMPLES * PACK], BF16, tag="x_then_window", name="x_bf", align_bytes=64)
+        x_bf = sb.tile([P, SAMPLES * PACK], BF16, name="x_bf", align_bytes=64)
         x_codes = sb.tile([P, SAMPLES], U32, name="x_codes", align_bytes=64)
         x_scales = sb.tile([P, SAMPLES], U8, name="x_scales", align_bytes=64)
         w = [sb.tile([P, PACK, HALF], F32, name="w_%d" % h) for h in range(2)]
@@ -179,20 +178,22 @@ def tile_attend_gbpool_E_pl_kernel(tc, xT, dz, cf, si, U, V, offs, out_0, out_1,
                         op1=MULT,
                     )
 
-        def make_dv(h):
+        def make_dv(h, lo=0, hi=HALF):
+            first = h * HALF
             nc.vector.tensor_tensor(
-                out=dv_bf[:, h * HALF * PACK : (h + 1) * HALF * PACK].rearrange("p (c i t) -> p c t i", i=2, t=PACK),
-                in0=w[h][:].rearrange("p t (c i) -> p c t i", i=2),
-                in1=dz_sb[h][:].rearrange("p t (c i) -> p c t i", i=2),
+                out=dv_bf[:, (first + lo) * PACK : (first + hi) * PACK].rearrange("p (c i t) -> p c t i", i=2, t=PACK),
+                in0=w[h][:, :, lo:hi].rearrange("p t (c i) -> p c t i", i=2),
+                in1=dz_sb[h][:, :, lo:hi].rearrange("p t (c i) -> p c t i", i=2),
                 op=MULT,
             )
 
-        def quantise_dv(h):
-            cols = slice(HALF + h * HALF, HALF + (h + 1) * HALF)
+        def quantise_dv(h, lo=0, hi=HALF):
+            first = h * HALF
+            cols = slice(HALF + first + lo, HALF + first + hi)
             nc.vector.quantize_mx(
                 out=dv_codes[:, cols].bitcast(E5M2),
                 scales=dv_scales[:, cols],
-                in_=dv_bf[:, h * HALF * PACK : (h + 1) * HALF * PACK],
+                in_=dv_bf[:, (first + lo) * PACK : (first + hi) * PACK],
             )
 
         def make_de(r, number, first, lo, hi):
@@ -217,9 +218,6 @@ def tile_attend_gbpool_E_pl_kernel(tc, xT, dz, cf, si, U, V, offs, out_0, out_1,
         quantise_x(1)
         make_w(0)
         codes_x(1)
-        windows.append(sb.tile([P, ITEMS], F32, tag="x_then_window", name="window_2", align_bytes=64))
-        nc.gpsimd.memset(windows[2][:], 0.0)
-        windows.append(windows[0])
         make_dv(0)
         make_w(1)
         turn_v(0)
@@ -228,15 +226,17 @@ def tile_attend_gbpool_E_pl_kernel(tc, xT, dz, cf, si, U, V, offs, out_0, out_1,
         quantise_v(0, 1)
         turn_v(2)
         make_de(0, 4, 0, 0, HALF)
-        make_dv(1)
+        make_dv(1, 0, P)
+        make_dv(1, P, HALF)
+        quantise_dv(1, 0, P)
+        quantise_dv(1, P, HALF)
+        quantise_v(1, 1)
         turn_v(3)
-        quantise_v(1, 2)
-        quantise_dv(1)
         scatter(0, 0, HALF)
         make_de(0, 5, HALF, HALF, SAMPLES)
         make_de(1, 6, HALF, 0, SAMPLES)
+        quantise_v(2, 2)
         make_de(2, 7, HALF, 0, SAMPLES)
-        quantise_v(3, 1)
         make_de(3, 2, HALF, 0, SAMPLES)
         scatter(0, HALF, SAMPLES)
 

@@ -54,18 +54,18 @@ def tile_attend_gbpool_E_pl_kernel(tc, xT, dz, cf, si, U, V, offs, out_0, out_1,
             nc.sync.dma_start(out=tile[:], in_=v_rows[r])
             return tile
 
-        u_raw = sb.tile([P, PACK, K], F32, name="u_raw")
+        u_raw = sb.tile([P, PACK, K], F32, tag="u_then_x", name="u_raw", align_bytes=64)
         nc.sync.dma_start(out=u_raw[:], in_=U.rearrange("(p j) c -> p j c", j=PACK))
         x_raw = [load_half("x_raw", xT, h) for h in range(2)]
         dz_sb = [load_half("dz", dz, 0)]
-        v_raw = [load_v(0), load_v(1)]
+        v_raw = [load_v(0)]
         dz_sb.append(load_half("dz", dz, 1))
         offsets = sb.tile([P, SAMPLES // 16], U16, name="offsets")
         nc.sync.dma_start(offsets[:], offs)
-        v_raw.extend([load_v(r) for r in range(2, PACK)])
+        v_raw.extend([load_v(r) for r in range(1, PACK)])
 
         ident = sb.tile([P, P], F32, name="ident")
-        zeros = sb.tile([P, P], F32, name="zeros")
+        zeros = sb.tile([P, P], F32, tag="zeros_then_window", name="zeros")
         nc.gpsimd.memset(zeros[:], 0.0)
         nc.gpsimd.affine_select(
             out=ident[:],
@@ -79,12 +79,14 @@ def tile_attend_gbpool_E_pl_kernel(tc, xT, dz, cf, si, U, V, offs, out_0, out_1,
 
         dv_codes = sb.tile([P, HALF + SAMPLES], U32, name="dv_codes", align_bytes=64)
         dv_scales = sb.tile([P, HALF + SAMPLES], U8, name="dv_scales", align_bytes=64)
-        windows = [sb.tile([P, ITEMS], F32, name="window_%d" % r) for r in range(PACK - 1)]
+        windows = [
+            sb.tile([P, ITEMS], F32, name="window_0"),
+            sb.tile([P, ITEMS], F32, tag="zeros_then_window", name="window_1"),
+        ]
         nc.vector.memset(dv_codes[:, 0:HALF], 0)
         nc.vector.memset(dv_scales[:, 0:HALF], 0)
-        for window in windows:
-            nc.vector.memset(window[:], 0.0)
-        windows.append(windows[0])
+        nc.vector.memset(windows[0][:], 0.0)
+        nc.gpsimd.memset(windows[1][:], 0.0)
 
         si_ps = bank(4, "si_ps")
         for j in range(PACK):
@@ -94,7 +96,7 @@ def tile_attend_gbpool_E_pl_kernel(tc, xT, dz, cf, si, U, V, offs, out_0, out_1,
             out=si_all[:].rearrange("p (n j) -> p n j", j=PACK), in_=si_ps[:].rearrange("p (j n) -> p n j", j=PACK)
         )
 
-        u_bf = sb.tile([P, K * PACK], BF16, name="u_bf", align_bytes=64)
+        u_bf = sb.tile([P, K * PACK], BF16, tag="x_then_window", name="u_bf", align_bytes=64)
         u_dst = u_bf[:].rearrange("p (t m j) -> p m j t", t=PACK, j=PACK)
         u_src = u_raw[:].rearrange("p j (m t) -> p m j t", t=PACK)
         nc.vector.tensor_copy(out=u_dst[:, 0:U_VECTOR], in_=u_src[:, 0:U_VECTOR])
@@ -104,7 +106,7 @@ def tile_attend_gbpool_E_pl_kernel(tc, xT, dz, cf, si, U, V, offs, out_0, out_1,
         nc.vector.quantize_mx(out=u_codes[:].bitcast(E4M3), scales=u_scales[:], in_=u_bf[:])
 
         v_bf = sb.tile([P, K * PACK], BF16, name="v_bf", align_bytes=64)
-        v_codes = sb.tile([P, K], U32, name="v_codes", align_bytes=64)
+        v_codes = sb.tile([P, K], U32, tag="v_codes", name="v_codes", align_bytes=64)
         v_scales = sb.tile([P, K], U8, name="v_scales", align_bytes=64)
 
         def turn_v(r):
@@ -130,50 +132,54 @@ def tile_attend_gbpool_E_pl_kernel(tc, xT, dz, cf, si, U, V, offs, out_0, out_1,
                 in_=v_bf[:, first * K : (first + count) * K],
             )
 
-        x_bf = sb.tile([P, SAMPLES * PACK], BF16, name="x_bf", align_bytes=64)
+        x_bf = [
+            sb.tile([P, HALF * PACK], BF16, tag=tag, name="x_bf_%d" % h, align_bytes=64)
+            for h, tag in enumerate(("u_then_x", "x_then_window"))
+        ]
         x_codes = sb.tile([P, SAMPLES], U32, name="x_codes", align_bytes=64)
         x_scales = sb.tile([P, SAMPLES], U8, name="x_scales", align_bytes=64)
         w = [sb.tile([P, PACK, HALF], F32, name="w_%d" % h) for h in range(2)]
         dv_bf = sb.tile([P, SAMPLES * PACK], BF16, name="dv_bf", align_bytes=64)
         de = [sb.tile([P, SAMPLES], F32, name="de_%d" % r) for r in range(PACK)]
 
-        def quantise_x(h):
-            for o, copy in enumerate((nc.scalar.copy, nc.scalar.copy if h else nc.vector.tensor_copy)):
-                q = 2 * h + o
-                copy(
-                    out=x_bf[:, q * 512 : (q + 1) * 512].rearrange("p (c i j) -> p c j i", i=2, j=PACK),
-                    in_=x_raw[h][:, :, o * P : (o + 1) * P].rearrange("p j (c i) -> p c j i", i=2),
-                )
-
-        def codes_x(h):
-            nc.vector.quantize_mx(
-                out=x_codes[:, h * HALF : (h + 1) * HALF].bitcast(E4M3),
-                scales=x_scales[:, h * HALF : (h + 1) * HALF],
-                in_=x_bf[:, h * HALF * PACK : (h + 1) * HALF * PACK],
+        def interleave_x(q, copy):
+            h, o = divmod(q, 2)
+            copy(
+                out=x_bf[h][:, o * P * PACK : (o + 1) * P * PACK].rearrange("p (c i j) -> p c j i", i=2, j=PACK),
+                in_=x_raw[h][:, :, o * P : (o + 1) * P].rearrange("p j (c i) -> p c j i", i=2),
             )
 
-        def make_w(h):
-            cols = slice(h * HALF, (h + 1) * HALF)
-            for pair in range(2):
-                u_ps = bank(2 * h + pair, "u_%d_%d" % (h, pair))
-                for o in range(2):
-                    t = 2 * pair + o
+        def quantise_x(lo, hi):
+            nc.vector.quantize_mx(
+                out=x_codes[:, lo:hi].bitcast(E4M3),
+                scales=x_scales[:, lo:hi],
+                in_=x_bf[lo // HALF][:, (lo % HALF) * PACK : (lo % HALF + hi - lo) * PACK],
+            )
+
+        def make_w(lo, hi, first_bank):
+            width = hi - lo
+            per_bank = 512 // width
+            h = lo // HALF
+            for b in range(PACK // per_bank):
+                u_ps = bank(first_bank + b, "u_%d_%d" % (lo, b))
+                for o in range(per_bank):
+                    t = per_bank * b + o
                     nc.tensor.matmul_mx(
-                        out=u_ps[:, o * HALF : (o + 1) * HALF],
+                        out=u_ps[:, o * width : (o + 1) * width],
                         lhsT=u_codes[:, t * P : (t + 1) * P].bitcast(E4M3),
                         lhsT_scale=u_scales[:, t * P : (t + 1) * P],
-                        rhs=x_codes[:, cols].bitcast(E4M3),
-                        rhs_scale=x_scales[:, cols],
+                        rhs=x_codes[:, lo:hi].bitcast(E4M3),
+                        rhs_scale=x_scales[:, lo:hi],
                         start=True,
                         stop=True,
                     )
-                for o in range(2):
-                    t = 2 * pair + o
+                for o in range(per_bank):
+                    t = per_bank * b + o
                     nc.vector.scalar_tensor_tensor(
-                        out=w[h][:, t, :],
-                        in0=u_ps[:, o * HALF : (o + 1) * HALF],
+                        out=w[h][:, t, lo - h * HALF : hi - h * HALF],
+                        in0=u_ps[:, o * width : (o + 1) * width],
                         scalar=cf_sb[:, t : t + 1],
-                        in1=si_all[:, cols],
+                        in1=si_all[:, lo:hi],
                         op0=MULT,
                         op1=MULT,
                     )
@@ -213,13 +219,20 @@ def tile_attend_gbpool_E_pl_kernel(tc, xT, dz, cf, si, U, V, offs, out_0, out_1,
         def scatter(r, lo, hi):
             nc.vector.tensor_copy(windows[r][:].indirect(offsets[:, lo // 16 : hi // 16]), de[r][:, lo:hi])
 
-        quantise_x(0)
-        codes_x(0)
-        quantise_x(1)
-        make_w(0)
-        codes_x(1)
+        interleave_x(0, nc.scalar.copy)
+        quantise_x(0, P)
+        interleave_x(1, nc.vector.tensor_copy)
+        interleave_x(2, nc.vector.tensor_copy)
+        interleave_x(3, nc.scalar.copy)
+        quantise_x(P, HALF)
+        make_w(0, P, 0)
+        make_w(P, HALF, 1)
+        quantise_x(HALF, SAMPLES)
+        windows.append(sb.tile([P, ITEMS], F32, tag="x_then_window", name="window_2", align_bytes=64))
+        nc.gpsimd.memset(windows[2][:], 0.0)
+        windows.append(windows[0])
         make_dv(0)
-        make_w(1)
+        make_w(HALF, SAMPLES, 2)
         turn_v(0)
         turn_v(1)
         quantise_dv(0)
@@ -241,7 +254,7 @@ def tile_attend_gbpool_E_pl_kernel(tc, xT, dz, cf, si, U, V, offs, out_0, out_1,
         scatter(0, HALF, SAMPLES)
 
         out_rows = out_0.rearrange("(s r) c -> r s c", r=PACK)
-        pairs = sb.tile([P, ITEMS * PACK], BF16, name="pairs")
+        pairs = sb.tile([P, ITEMS * PACK], BF16, tag="v_codes", name="pairs", align_bytes=64)
         pair_view = pairs[:].rearrange("p (n a c l) -> p n a c l", a=2, c=CHUNK, l=2)
 
         def round_plane(r, first, count, copy):

@@ -20,8 +20,10 @@ ITEMS = 2048
 HALF = SAMPLES // 2
 CHUNK = 256
 CHUNKS = ITEMS // CHUNK
-SCALAR_WEAVES = 2
+SCALAR_WEAVES = 3
 U_VECTOR = 88
+LANES = (2, 0, 1, 3)
+VECTOR_ROUNDS = 2
 
 FLOPS = 2 * 2 * K * K * SAMPLES
 BYTES = 4 * (4 * K * K + K + SAMPLES) + 2 * P * SAMPLES // 16 + 4 * K * ITEMS + K * ITEMS + 16 * ITEMS
@@ -51,7 +53,7 @@ def tile_attend_gbpool_E_pl_kernel(tc, xT, dz, cf, si, U, V, offs, out_0, out_1,
 
         def load_v(r):
             tile = sb.tile([P, K], F32, name="v_raw_%d" % r)
-            nc.sync.dma_start(out=tile[:], in_=v_rows[r])
+            nc.sync.dma_start(out=tile[:], in_=v_rows[LANES[r]])
             return tile
 
         u_raw = sb.tile([P, PACK, K], F32, tag="u_then_x", name="u_raw", align_bytes=64)
@@ -145,8 +147,8 @@ def tile_attend_gbpool_E_pl_kernel(tc, xT, dz, cf, si, U, V, offs, out_0, out_1,
         def interleave_x(q, copy):
             h, o = divmod(q, 2)
             copy(
-                out=x_bf[h][:, o * P * PACK : (o + 1) * P * PACK].rearrange("p (c i j) -> p c j i", i=2, j=PACK),
-                in_=x_raw[h][:, :, o * P : (o + 1) * P].rearrange("p j (c i) -> p c j i", i=2),
+                out=x_bf[h][:, o * P * PACK : (o + 1) * P * PACK].rearrange("p (c i j) -> p c j i", i=4, j=PACK),
+                in_=x_raw[h][:, :, o * P : (o + 1) * P].rearrange("p j (c i) -> p c j i", i=4),
             )
 
         def quantise_x(lo, hi):
@@ -187,9 +189,9 @@ def tile_attend_gbpool_E_pl_kernel(tc, xT, dz, cf, si, U, V, offs, out_0, out_1,
         def make_dv(h, lo=0, hi=HALF):
             first = h * HALF
             nc.vector.tensor_tensor(
-                out=dv_bf[:, (first + lo) * PACK : (first + hi) * PACK].rearrange("p (c i t) -> p c t i", i=2, t=PACK),
-                in0=w[h][:, :, lo:hi].rearrange("p t (c i) -> p c t i", i=2),
-                in1=dz_sb[h][:, :, lo:hi].rearrange("p t (c i) -> p c t i", i=2),
+                out=dv_bf[:, (first + lo) * PACK : (first + hi) * PACK].rearrange("p (c i t) -> p c t i", i=4, t=PACK),
+                in0=w[h][:, :, lo:hi].rearrange("p t (c i) -> p c t i", i=4),
+                in1=dz_sb[h][:, :, lo:hi].rearrange("p t (c i) -> p c t i", i=4),
                 op=MULT,
             )
 
@@ -239,17 +241,15 @@ def tile_attend_gbpool_E_pl_kernel(tc, xT, dz, cf, si, U, V, offs, out_0, out_1,
         quantise_v(0, 1)
         turn_v(2)
         make_de(0, 4, 0, 0, HALF)
-        make_dv(1, 0, P)
-        make_dv(1, P, HALF)
-        quantise_dv(1, 0, P)
-        quantise_dv(1, P, HALF)
-        quantise_v(1, 1)
+        make_dv(1)
         turn_v(3)
+        quantise_v(1, 2)
+        quantise_dv(1)
         scatter(0, 0, HALF)
         make_de(0, 5, HALF, HALF, SAMPLES)
         make_de(1, 6, HALF, 0, SAMPLES)
-        quantise_v(2, 2)
         make_de(2, 7, HALF, 0, SAMPLES)
+        quantise_v(3, 1)
         make_de(3, 2, HALF, 0, SAMPLES)
         scatter(0, HALF, SAMPLES)
 
@@ -258,7 +258,7 @@ def tile_attend_gbpool_E_pl_kernel(tc, xT, dz, cf, si, U, V, offs, out_0, out_1,
         pair_view = pairs[:].rearrange("p (n a c l) -> p n a c l", a=2, c=CHUNK, l=2)
 
         def round_plane(r, first, count, copy):
-            a, l = divmod(r, 2)
+            a, l = divmod(LANES[r], 2)
             copy(
                 out=pair_view[:, first : first + count, a, :, l],
                 in_=windows[r][:].rearrange("p (n c) -> p n c", c=CHUNK)[:, first : first + count, :],
@@ -267,9 +267,12 @@ def tile_attend_gbpool_E_pl_kernel(tc, xT, dz, cf, si, U, V, offs, out_0, out_1,
         for r in range(PACK):
             if r > 0:
                 scatter(r, 0, SAMPLES)
-            nc.sync.dma_start(out=out_rows[r], in_=windows[r][:])
-            if r < PACK - 1:
+            nc.sync.dma_start(out=out_rows[LANES[r]], in_=windows[r][:])
+            if r < PACK - 2:
                 round_plane(r, 0, CHUNKS, nc.scalar.copy)
+            elif r == PACK - 2:
+                for n in range(0, CHUNKS, 2):
+                    round_plane(r, n, 2, nc.scalar.copy)
 
         y_bf = sb.tile([P, ITEMS * PACK], BF16, name="y_bf", align_bytes=64)
         y_codes = sb.tile([P, ITEMS], U32, name="y_codes", align_bytes=64)
@@ -280,8 +283,8 @@ def tile_attend_gbpool_E_pl_kernel(tc, xT, dz, cf, si, U, V, offs, out_0, out_1,
 
         def weave(n):
             cols = slice(2 * n * CHUNK, 2 * (n + 1) * CHUNK)
-            dst = y_words[:, cols].rearrange("p (c i a) -> p c a i", i=2, a=2)
-            src = pair_words[:, cols].rearrange("p (a c i) -> p c a i", i=2, a=2)
+            dst = y_words[:, cols].rearrange("p (c i a) -> p c a i", i=4, a=2)
+            src = pair_words[:, cols].rearrange("p (a c i) -> p c a i", i=4, a=2)
             if n >= CHUNKS - SCALAR_WEAVES:
                 nc.scalar.copy(out=dst, in_=src)
             else:
@@ -301,7 +304,7 @@ def tile_attend_gbpool_E_pl_kernel(tc, xT, dz, cf, si, U, V, offs, out_0, out_1,
                 nc.sync.dma_start(out=words_out[:, lo - CHUNK : hi], in_=y_codes[:, lo - CHUNK : hi].bitcast(I32))
 
         for n in range(CHUNKS):
-            round_plane(PACK - 1, n, 1, nc.scalar.copy)
+            round_plane(PACK - 1, n, 1, nc.vector.tensor_copy if n < VECTOR_ROUNDS else nc.scalar.copy)
         for n in range(CHUNKS):
             weave(n)
             if n >= 1:

@@ -20,7 +20,7 @@ ITEMS = 2048
 HALF = SAMPLES // 2
 CHUNK = 256
 CHUNKS = ITEMS // CHUNK
-SCALAR_WEAVES = 3
+SCALAR_WEAVES = 2
 U_VECTOR = 88
 LANES = (2, 0, 1, 3)
 VECTOR_ROUNDS = 2
@@ -44,7 +44,7 @@ def tile_attend_gbpool_E_pl_kernel(tc, xT, dz, cf, si, U, V, offs, out_0, out_1,
         nc.sync.dma_start(out=cf_sb[:], in_=cf.rearrange("(p t) o -> p (t o)", t=PACK))
 
         def load_half(name, source, h):
-            tile = sb.tile([P, PACK, HALF], F32, name="%s_%d" % (name, h))
+            tile = sb.tile([P, PACK, HALF], F32, tag="%s_%d" % (name, h), name="%s_%d" % (name, h))
             rows = source.rearrange("(p j) c -> p j c", j=PACK)
             nc.sync.dma_start(out=tile[:], in_=rows[:, :, h * HALF : (h + 1) * HALF])
             return tile
@@ -52,19 +52,19 @@ def tile_attend_gbpool_E_pl_kernel(tc, xT, dz, cf, si, U, V, offs, out_0, out_1,
         v_rows = V.rearrange("(s r) f -> r s f", r=PACK)
 
         def load_v(r):
-            tile = sb.tile([P, K], F32, name="v_raw_%d" % r)
+            tile = sb.tile([P, K], F32, tag="v_raw_%d" % r, name="v_raw_%d" % r)
             nc.sync.dma_start(out=tile[:], in_=v_rows[LANES[r]])
             return tile
 
         u_raw = sb.tile([P, PACK, K], F32, tag="u_then_x", name="u_raw", align_bytes=64)
         nc.sync.dma_start(out=u_raw[:], in_=U.rearrange("(p j) c -> p j c", j=PACK))
         x_raw = [load_half("x_raw", xT, h) for h in range(2)]
+        v_raw = [load_v(0), load_v(1)]
         dz_sb = [load_half("dz", dz, 0)]
-        v_raw = [load_v(0)]
+        v_raw.extend([load_v(2), load_v(3)])
         dz_sb.append(load_half("dz", dz, 1))
         offsets = sb.tile([P, SAMPLES // 16], U16, name="offsets")
         nc.sync.dma_start(offsets[:], offs)
-        v_raw.extend([load_v(r) for r in range(1, PACK)])
 
         ident = sb.tile([P, P], F32, name="ident")
         zeros = sb.tile([P, P], F32, tag="zeros_then_window", name="zeros")
@@ -112,7 +112,7 @@ def tile_attend_gbpool_E_pl_kernel(tc, xT, dz, cf, si, U, V, offs, out_0, out_1,
         v_scales = sb.tile([P, K], U8, name="v_scales", align_bytes=64)
 
         def turn_v(r):
-            rounded = sb.tile([P, K], BF16, tag="v_rounded_%d" % (r % 2), name="v_rounded_%d" % r)
+            rounded = sb.tile([P, K], BF16, tag="v_raw_%d" % (r - 1) if r else "x_raw_1", name="v_rounded_%d" % r)
             nc.scalar.copy(
                 out=rounded[:].rearrange("s (u p e) -> s u p e", u=2, e=2),
                 in_=v_raw[r][:].rearrange("s (p u e) -> s u p e", u=2, e=2),
@@ -233,23 +233,20 @@ def tile_attend_gbpool_E_pl_kernel(tc, xT, dz, cf, si, U, V, offs, out_0, out_1,
         windows.append(sb.tile([P, ITEMS], F32, tag="x_then_window", name="window_2", align_bytes=64))
         nc.gpsimd.memset(windows[2][:], 0.0)
         windows.append(windows[0])
-        make_dv(0)
         make_w(HALF, SAMPLES, 2)
-        turn_v(0)
-        turn_v(1)
+        make_dv(0)
+        for r in range(PACK):
+            turn_v(r)
+        quantise_v(0, 2)
         quantise_dv(0)
-        quantise_v(0, 1)
-        turn_v(2)
         make_de(0, 4, 0, 0, HALF)
         make_dv(1)
-        turn_v(3)
-        quantise_v(1, 2)
+        quantise_v(2, 2)
         quantise_dv(1)
         scatter(0, 0, HALF)
         make_de(0, 5, HALF, HALF, SAMPLES)
         make_de(1, 6, HALF, 0, SAMPLES)
         make_de(2, 7, HALF, 0, SAMPLES)
-        quantise_v(3, 1)
         make_de(3, 2, HALF, 0, SAMPLES)
         scatter(0, HALF, SAMPLES)
 

@@ -261,15 +261,16 @@ def tile_attend_gbpool_E_pl_kernel(tc, xT, dz, cf, si, U, V, offs, out_0, out_1,
                 in_=windows[r][:].rearrange("p (n c) -> p n c", c=CHUNK)[:, first : first + count, :],
             )
 
+        def gpsimd_round(out, in_):
+            nc.gpsimd.tensor_scalar(out, in_, 1.0, -0.0, MULT, mybir.AluOpType.add)
+
         for r in range(PACK):
             if r > 0:
                 scatter(r, 0, SAMPLES)
             nc.sync.dma_start(out=out_rows[LANES[r]], in_=windows[r][:])
-            if r < PACK - 2:
-                round_plane(r, 0, CHUNKS, nc.scalar.copy)
-            elif r == PACK - 2:
-                for n in range(0, CHUNKS, 2):
-                    round_plane(r, n, 2, nc.scalar.copy)
+            if r < PACK - 1:
+                round_plane(r, 0, CHUNKS // 2, nc.scalar.copy)
+                round_plane(r, CHUNKS // 2, CHUNKS // 2, gpsimd_round)
 
         y_bf = sb.tile([P, ITEMS * PACK], BF16, name="y_bf", align_bytes=64)
         y_codes = sb.tile([P, ITEMS], U32, name="y_codes", align_bytes=64)

@@ -20,7 +20,7 @@ ITEMS = 2048
 HALF = SAMPLES // 2
 CHUNK = 256
 CHUNKS = ITEMS // CHUNK
-SCALAR_WEAVES = 2
+SCALAR_WEAVES = 3
 U_VECTOR = 88
 LANES = (2, 0, 1, 3)
 VECTOR_ROUNDS = 2
@@ -311,5 +311,4 @@ def tile_attend_gbpool_E_pl_kernel(tc, xT, dz, cf, si, U, V, offs, out_0, out_1,
 
         scales_out = out_2[0].bitcast(I32).rearrange("(q j) (g c) -> q g j c", j=4, g=4)
         for quad in range(4):
-            queue = nc.scalar if quad % 2 else nc.sync
-            queue.dma_start(out=scales_out[quad], in_=y_scales[32 * quad : 32 * quad + 16, :].bitcast(I32))
+            nc.sync.dma_start(out=scales_out[quad], in_=y_scales[32 * quad : 32 * quad + 16, :].bitcast(I32))

@@ -11,6 +11,8 @@ U8 = mybir.dt.uint8
 E4M3 = mybir.dt.float8_e4m3fn_x4
 E5M2 = mybir.dt.float8_e5m2_x4
 MULT = mybir.AluOpType.mult
+ADD = mybir.AluOpType.add
+COPY = mybir.ActivationFunctionType.Copy
 
 P = 128
 PACK = 4
@@ -38,13 +40,16 @@ def tile_attend_gbpool_E_pl_kernel(tc, xT, dz, cf, si, U, V, offs, out_0, out_1,
         def bank(number, name):
             return ps.tile([P, 512], F32, tag="bank_%d" % number, name=name)
 
+        def buffer(tag, name, shape, dtype):
+            return sb.tile(shape, dtype, tag=tag, name=name, align_bytes=64)
+
         si_sb = sb.tile([P, PACK], F32, name="si_sb")
         nc.sync.dma_start(out=si_sb[:], in_=si[0:1, :].rearrange("o (n j) -> (o n) j", j=PACK))
         cf_sb = sb.tile([P, PACK], F32, name="cf_sb")
         nc.sync.dma_start(out=cf_sb[:], in_=cf.rearrange("(p t) o -> p (t o)", t=PACK))
 
         def load_half(name, source, h):
-            tile = sb.tile([P, PACK, HALF], F32, tag="%s_%d" % (name, h), name="%s_%d" % (name, h))
+            tile = buffer("%s_%d" % (name, h), "%s_%d" % (name, h), [P, PACK, HALF], F32)
             rows = source.rearrange("(p j) c -> p j c", j=PACK)
             nc.sync.dma_start(out=tile[:], in_=rows[:, :, h * HALF : (h + 1) * HALF])
             return tile
@@ -52,22 +57,23 @@ def tile_attend_gbpool_E_pl_kernel(tc, xT, dz, cf, si, U, V, offs, out_0, out_1,
         v_rows = V.rearrange("(s r) f -> r s f", r=PACK)
 
         def load_v(r):
-            tile = sb.tile([P, K], F32, tag="v_raw_%d" % r, name="v_raw_%d" % r)
+            tile = buffer("v_raw_%d" % r, "v_raw_%d" % r, [P, K], F32)
             nc.sync.dma_start(out=tile[:], in_=v_rows[LANES[r]])
             return tile
 
-        u_raw = sb.tile([P, PACK, K], F32, tag="u_then_x", name="u_raw", align_bytes=64)
+        u_raw = buffer("chain", "u_raw", [P, PACK, K], F32)
         nc.sync.dma_start(out=u_raw[:], in_=U.rearrange("(p j) c -> p j c", j=PACK))
-        x_raw = [load_half("x_raw", xT, h) for h in range(2)]
-        v_raw = [load_v(0), load_v(1)]
+        x_raw = [load_half("x_raw", xT, 0)]
         dz_sb = [load_half("dz", dz, 0)]
-        v_raw.extend([load_v(2), load_v(3)])
-        dz_sb.append(load_half("dz", dz, 1))
+        v_raw = [load_v(0), load_v(1)]
+        x_raw.append(load_half("x_raw", xT, 1))
         offsets = sb.tile([P, SAMPLES // 16], U16, name="offsets")
         nc.sync.dma_start(offsets[:], offs)
+        dz_sb.append(load_half("dz", dz, 1))
+        v_raw.extend([load_v(2), load_v(3)])
 
         ident = sb.tile([P, P], F32, name="ident")
-        zeros = sb.tile([P, P], F32, tag="zeros_then_window", name="zeros")
+        zeros = buffer("zeros_then_window", "zeros", [P, P], F32)
         nc.gpsimd.memset(zeros[:], 0.0)
         nc.gpsimd.affine_select(
             out=ident[:],
@@ -79,11 +85,11 @@ def tile_attend_gbpool_E_pl_kernel(tc, xT, dz, cf, si, U, V, offs, out_0, out_1,
             channel_multiplier=1,
         )
 
-        dv_codes = sb.tile([P, HALF + SAMPLES], U32, name="dv_codes", align_bytes=64)
-        dv_scales = sb.tile([P, HALF + SAMPLES], U8, name="dv_scales", align_bytes=64)
+        dv_codes = buffer("dv_codes", "dv_codes", [P, HALF + SAMPLES], U32)
+        dv_scales = buffer("dv_scales", "dv_scales", [P, HALF + SAMPLES], U8)
         windows = [
-            sb.tile([P, ITEMS], F32, name="window_0"),
-            sb.tile([P, ITEMS], F32, tag="zeros_then_window", name="window_1"),
+            buffer("window_0", "window_0", [P, ITEMS], F32),
+            buffer("zeros_then_window", "window_1", [P, ITEMS], F32),
         ]
         nc.vector.memset(dv_codes[:, 0:HALF], 0)
         nc.vector.memset(dv_scales[:, 0:HALF], 0)
@@ -93,119 +99,91 @@ def tile_attend_gbpool_E_pl_kernel(tc, xT, dz, cf, si, U, V, offs, out_0, out_1,
         si_ps = bank(4, "si_ps")
         for j in range(PACK):
             nc.tensor.transpose(si_ps[:, j * P : (j + 1) * P], si_sb[:, j : j + 1].to_broadcast([P, P]), ident[:])
-        si_all = sb.tile([P, SAMPLES], F32, name="si_all")
-        nc.scalar.copy(
-            out=si_all[:].rearrange("p (n j) -> p n j", j=PACK), in_=si_ps[:].rearrange("p (j n) -> p n j", j=PACK)
-        )
+        si_rows = si_ps[:].rearrange("p (j n) -> p n j", j=PACK)
 
-        u_bf = sb.tile([P, K * PACK], BF16, tag="x_then_window", name="u_bf", align_bytes=64)
+        si_all = buffer("si_all", "si_all", [P, SAMPLES], F32)
+        nc.scalar.copy(out=si_all[:].rearrange("p (n j) -> p n j", j=PACK), in_=si_rows)
+
+        u_bf = buffer("u_bf", "u_bf", [P, K * PACK], BF16)
         u_dst = u_bf[:].rearrange("p (t m j) -> p m j t", t=PACK, j=PACK)
         u_src = u_raw[:].rearrange("p j (m t) -> p m j t", t=PACK)
         nc.vector.tensor_copy(out=u_dst[:, 0:U_VECTOR], in_=u_src[:, 0:U_VECTOR])
         nc.scalar.copy(out=u_dst[:, U_VECTOR:P], in_=u_src[:, U_VECTOR:P])
-        u_codes = sb.tile([P, K], U32, name="u_codes", align_bytes=64)
-        u_scales = sb.tile([P, K], U8, name="u_scales", align_bytes=64)
+        u_codes = buffer("u_codes", "u_codes", [P, K], U32)
+        u_scales = buffer("u_scales", "u_scales", [P, K], U8)
         nc.vector.quantize_mx(out=u_codes[:].bitcast(E4M3), scales=u_scales[:], in_=u_bf[:])
 
-        v_bf = sb.tile([P, K * PACK], BF16, name="v_bf", align_bytes=64)
-        v_codes = sb.tile([P, K], U32, tag="v_codes", name="v_codes", align_bytes=64)
-        v_scales = sb.tile([P, K], U8, name="v_scales", align_bytes=64)
+        v_bf = [buffer("v_bf_%d" % r, "v_bf_%d" % r, [P, K], BF16) for r in range(PACK)]
+        v_codes = buffer("v_codes", "v_codes", [P, K], U32)
+        v_scales = buffer("v_scales", "v_scales", [P, K], U8)
 
-        def turn_v(r):
-            rounded = sb.tile([P, K], BF16, tag="v_raw_%d" % (r - 1) if r else "x_raw_1", name="v_rounded_%d" % r)
+        def turn_v(r, rounded):
             nc.scalar.copy(
-                out=rounded[:].rearrange("s (u p e) -> s u p e", u=2, e=2),
+                out=rounded.rearrange("s (u p e) -> s u p e", u=2, e=2),
                 in_=v_raw[r][:].rearrange("s (p u e) -> s u p e", u=2, e=2),
             )
-            words = rounded[:].bitcast(F32)
-            turned = bank(r % 2, "v_turned_%d" % r)
+            words = rounded.bitcast(F32)
+            turned = bank(5 + r % 2, "v_turned_%d" % r)
             for u in range(2):
                 nc.tensor.transpose(turned[:, u * P : (u + 1) * P], words[:, u * P : (u + 1) * P], ident[:])
             nc.scalar.copy(
-                out=v_bf[:, r * K : (r + 1) * K].bitcast(F32).rearrange("p (s u) -> p s u", u=2),
+                out=v_bf[r][:].bitcast(F32).rearrange("p (s u) -> p s u", u=2),
                 in_=turned[:, 0 : 2 * P].rearrange("p (u s) -> p s u", u=2),
             )
 
-        def quantise_v(first, count):
-            cols = slice(first * P, (first + count) * P)
-            nc.vector.quantize_mx(
-                out=v_codes[:, cols].bitcast(E4M3),
-                scales=v_scales[:, cols],
-                in_=v_bf[:, first * K : (first + count) * K],
-            )
+        def quantise_v(r):
+            cols = slice(r * P, (r + 1) * P)
+            nc.vector.quantize_mx(out=v_codes[:, cols].bitcast(E4M3), scales=v_scales[:, cols], in_=v_bf[r][:])
 
-        x_bf = [
-            sb.tile([P, HALF * PACK], BF16, tag=tag, name="x_bf_%d" % h, align_bytes=64)
-            for h, tag in enumerate(("u_then_x", "x_then_window"))
-        ]
-        x_codes = sb.tile([P, SAMPLES], U32, name="x_codes", align_bytes=64)
-        x_scales = sb.tile([P, SAMPLES], U8, name="x_scales", align_bytes=64)
-        w = [sb.tile([P, PACK, HALF], F32, name="w_%d" % h) for h in range(2)]
-        dv_bf = sb.tile([P, SAMPLES * PACK], BF16, name="dv_bf", align_bytes=64)
-        de = [sb.tile([P, SAMPLES], F32, name="de_%d" % r) for r in range(PACK)]
+        x_codes = [buffer("x_codes_%d" % q, "x_codes_%d" % q, [P, P], U32) for q in range(4)]
+        x_scales = [buffer("x_scales_%d" % q, "x_scales_%d" % q, [P, P], U8) for q in range(4)]
+        dv_bf = [buffer("dv_bf_0", "dv_bf_0", [P, HALF * PACK], BF16)[:]]
 
-        def interleave_x(q, copy):
-            h, o = divmod(q, 2)
+        def interleave_x(x_bf, h, o, copy):
             copy(
-                out=x_bf[h][:, o * P * PACK : (o + 1) * P * PACK].rearrange("p (c i j) -> p c j i", i=4, j=PACK),
+                out=x_bf[:, o * P * PACK : (o + 1) * P * PACK].rearrange("p (c i j) -> p c j i", i=4, j=PACK),
                 in_=x_raw[h][:, :, o * P : (o + 1) * P].rearrange("p j (c i) -> p c j i", i=4),
             )
 
-        def quantise_x(lo, hi):
+        def quantise_x(x_bf, h, o):
             nc.vector.quantize_mx(
-                out=x_codes[:, lo:hi].bitcast(E4M3),
-                scales=x_scales[:, lo:hi],
-                in_=x_bf[lo // HALF][:, (lo % HALF) * PACK : (lo % HALF + hi - lo) * PACK],
+                out=x_codes[2 * h + o][:].bitcast(E4M3),
+                scales=x_scales[2 * h + o][:],
+                in_=x_bf[:, o * P * PACK : (o + 1) * P * PACK],
             )
 
-        def make_w(lo, hi, first_bank):
-            width = hi - lo
-            per_bank = 512 // width
-            h = lo // HALF
-            for b in range(PACK // per_bank):
-                u_ps = bank(first_bank + b, "u_%d_%d" % (lo, b))
-                for o in range(per_bank):
-                    t = per_bank * b + o
-                    nc.tensor.matmul_mx(
-                        out=u_ps[:, o * width : (o + 1) * width],
-                        lhsT=u_codes[:, t * P : (t + 1) * P].bitcast(E4M3),
-                        lhsT_scale=u_scales[:, t * P : (t + 1) * P],
-                        rhs=x_codes[:, lo:hi].bitcast(E4M3),
-                        rhs_scale=x_scales[:, lo:hi],
-                        start=True,
-                        stop=True,
-                    )
-                for o in range(per_bank):
-                    t = per_bank * b + o
-                    nc.vector.scalar_tensor_tensor(
-                        out=w[h][:, t, lo - h * HALF : hi - h * HALF],
-                        in0=u_ps[:, o * width : (o + 1) * width],
-                        scalar=cf_sb[:, t : t + 1],
-                        in1=si_all[:, lo:hi],
-                        op0=MULT,
-                        op1=MULT,
-                    )
+        def make_u(h, o):
+            u_ps = bank(2 * h + o, "u_%d_%d" % (h, o))
+            for t in range(PACK):
+                nc.tensor.matmul_mx(
+                    out=u_ps[:, t * P : (t + 1) * P],
+                    lhsT=u_codes[:, t * P : (t + 1) * P].bitcast(E4M3),
+                    lhsT_scale=u_scales[:, t * P : (t + 1) * P],
+                    rhs=x_codes[2 * h + o][:].bitcast(E4M3),
+                    rhs_scale=x_scales[2 * h + o][:],
+                    start=True,
+                    stop=True,
+                )
+            return u_ps
 
-        def make_dv(h, lo=0, hi=HALF):
-            first = h * HALF
+        def make_g(g, h, o, engine):
+            cols = slice(o * P, (o + 1) * P)
+            engine.tensor_tensor(out=g[:, :, cols], in0=dz_sb[h][:, :, cols], in1=cs[:, :, cols], op=MULT)
+
+        def make_dv(u_ps, g, h, o):
             nc.vector.tensor_tensor(
-                out=dv_bf[:, (first + lo) * PACK : (first + hi) * PACK].rearrange("p (c i t) -> p c t i", i=4, t=PACK),
-                in0=w[h][:, :, lo:hi].rearrange("p t (c i) -> p c t i", i=4),
-                in1=dz_sb[h][:, :, lo:hi].rearrange("p t (c i) -> p c t i", i=4),
+                out=dv_bf[h][:, o * P * PACK : (o + 1) * P * PACK].rearrange("p (c i t) -> p c t i", i=4, t=PACK),
+                in0=u_ps[:].rearrange("p (t c i) -> p c t i", t=PACK, i=4),
+                in1=g[:, :, o * P : (o + 1) * P].rearrange("p t (c i) -> p c t i", i=4),
                 op=MULT,
             )
 
-        def quantise_dv(h, lo=0, hi=HALF):
-            first = h * HALF
-            cols = slice(HALF + first + lo, HALF + first + hi)
-            nc.vector.quantize_mx(
-                out=dv_codes[:, cols].bitcast(E5M2),
-                scales=dv_scales[:, cols],
-                in_=dv_bf[:, (first + lo) * PACK : (first + hi) * PACK],
-            )
+        def quantise_dv(h):
+            cols = slice((h + 1) * HALF, (h + 2) * HALF)
+            nc.vector.quantize_mx(out=dv_codes[:, cols].bitcast(E5M2), scales=dv_scales[:, cols], in_=dv_bf[h])
 
-        def make_de(r, number, first, lo, hi):
-            acc = bank(number, "de_ps_%d_%d" % (r, lo))
+        def product(r, number, first):
+            acc = bank(number, "de_ps_%d_%d" % (r, first))
             nc.tensor.matmul_mx(
                 out=acc[:],
                 lhsT=v_codes[:, r * P : (r + 1) * P].bitcast(E4M3),
@@ -215,43 +193,79 @@ def tile_attend_gbpool_E_pl_kernel(tc, xT, dz, cf, si, U, V, offs, out_0, out_1,
                 start=True,
                 stop=True,
             )
-            shift = HALF - first
-            nc.scalar.copy(out=de[r][:, lo:hi], in_=acc[:, lo + shift : hi + shift])
+            return acc
 
-        def scatter(r, lo, hi):
-            nc.vector.tensor_copy(windows[r][:].indirect(offsets[:, lo // 16 : hi // 16]), de[r][:, lo:hi])
+        def copy_out(acc, lo, tag, name):
+            de = buffer(tag, name, [P, SAMPLES - lo], F32)
+            nc.scalar.copy(out=de[:], in_=acc[:, lo:SAMPLES])
+            return de
 
-        interleave_x(0, nc.scalar.copy)
-        quantise_x(0, P)
-        interleave_x(1, nc.vector.tensor_copy)
-        interleave_x(2, nc.vector.tensor_copy)
-        interleave_x(3, nc.scalar.copy)
-        quantise_x(P, HALF)
-        make_w(0, P, 0)
-        make_w(P, HALF, 1)
-        quantise_x(HALF, SAMPLES)
-        windows.append(sb.tile([P, ITEMS], F32, tag="x_then_window", name="window_2", align_bytes=64))
-        nc.gpsimd.memset(windows[2][:], 0.0)
-        windows.append(windows[0])
-        make_w(HALF, SAMPLES, 2)
-        make_dv(0)
-        for r in range(PACK):
-            turn_v(r)
-        quantise_v(0, 2)
+        def scatter(r, lo, hi, de):
+            nc.vector.tensor_copy(windows[r][:].indirect(offsets[:, lo // 16 : hi // 16]), de[:])
+
+        x_bf = buffer("chain", "x_bf_0", [P, HALF * PACK], BF16)
+        interleave_x(x_bf, 0, 0, nc.scalar.copy)
+        interleave_x(x_bf, 0, 1, nc.vector.tensor_copy)
+        quantise_x(x_bf, 0, 0)
+        quantise_x(x_bf, 0, 1)
+        u_ps = [make_u(0, 0), make_u(0, 1)]
+        g_and_v = buffer("chain", "g_0", [P, PACK * HALF + K // 2], F32)
+        g = g_and_v[:, 0 : PACK * HALF].rearrange("p (t i) -> p t i", t=PACK)
+        v_rounded = g_and_v[:, PACK * HALF : PACK * HALF + K // 2].bitcast(BF16)
+        for t in range(PACK):
+            nc.vector.scalar_tensor_tensor(
+                out=g[:, t, :],
+                in0=dz_sb[0][:, t, :],
+                scalar=cf_sb[:, t : t + 1],
+                in1=si_all[:, 0:HALF],
+                op0=MULT,
+                op1=MULT,
+            )
+        make_dv(u_ps[0], g, 0, 0)
+        make_dv(u_ps[1], g, 0, 1)
+        turn_v(0, v_rounded)
+        turn_v(1, v_rounded)
+        cs = buffer("u_bf", "cs", [P, PACK, HALF], F32)
+        for t in range(PACK):
+            nc.scalar.activation(out=cs[:, t, :], in_=si_all[:, HALF:SAMPLES], func=COPY, scale=cf_sb[:, t : t + 1])
+        quantise_v(0)
         quantise_dv(0)
-        make_de(0, 4, 0, 0, HALF)
-        make_dv(1)
-        quantise_v(2, 2)
+        early = [product(0, 7, 0)]
+        quantise_v(1)
+        early.append(product(1, 4, 0))
+        de_early = copy_out(early[0], HALF, "de_a0", "de_a0")
+
+        x_bf = buffer("chain", "x_bf_1", [P, HALF * PACK], BF16)
+        interleave_x(x_bf, 1, 0, nc.vector.tensor_copy)
+        interleave_x(x_bf, 1, 1, nc.scalar.copy)
+        quantise_x(x_bf, 1, 0)
+        quantise_x(x_bf, 1, 1)
+        u_ps = [make_u(1, 0), make_u(1, 1)]
+        g = buffer("chain", "g_1", [P, PACK, HALF], F32)
+        scatter(0, 0, HALF, de_early)
+        make_g(g, 1, 0, nc.gpsimd)
+        make_g(g, 1, 1, nc.gpsimd)
+        dv_bf.append(buffer("de_a0", "dv_bf_1", [P, HALF * PACK], BF16)[:])
+        turn_v(2, buffer("x_codes_2", "v_rounded_2", [P, K], BF16)[:])
+        turn_v(3, buffer("v_raw_2", "v_rounded_3", [P, K], BF16)[:])
+        make_dv(u_ps[0], g, 1, 0)
+        make_dv(u_ps[1], g, 1, 1)
         quantise_dv(1)
-        scatter(0, 0, HALF)
-        make_de(0, 5, HALF, HALF, SAMPLES)
-        make_de(1, 6, HALF, 0, SAMPLES)
-        make_de(2, 7, HALF, 0, SAMPLES)
-        make_de(3, 2, HALF, 0, SAMPLES)
-        scatter(0, HALF, SAMPLES)
+        quantise_v(2)
+        quantise_v(3)
+        de_early = copy_out(early[1], HALF, "chain", "de_b0")
+        windows.append(buffer("v_bf_3", "window_2", [P, ITEMS], F32))
+        for n in range(4):
+            nc.gpsimd.memset(windows[2][:, n * ITEMS // 4 : (n + 1) * ITEMS // 4], 0.0)
+        windows.append(windows[0])
+        scatter(1, 0, HALF, de_early)
+        de = [
+            copy_out(product(r, number, HALF), lo, "de_%d" % r, "de_%d" % r)
+            for r, number, lo in ((0, 7, HALF), (1, 0, HALF), (2, 1, 0), (3, 2, 0))
+        ]
 
         out_rows = out_0.rearrange("(s r) c -> r s c", r=PACK)
-        pairs = sb.tile([P, ITEMS * PACK], BF16, tag="v_codes", name="pairs", align_bytes=64)
+        pairs = buffer("v_codes", "pairs", [P, ITEMS * PACK], BF16)
         pair_view = pairs[:].rearrange("p (n a c l) -> p n a c l", a=2, c=CHUNK, l=2)
 
         def round_plane(r, first, count, copy):
@@ -262,11 +276,10 @@ def tile_attend_gbpool_E_pl_kernel(tc, xT, dz, cf, si, U, V, offs, out_0, out_1,
             )
 
         def gpsimd_round(out, in_):
-            nc.gpsimd.tensor_scalar(out, in_, 1.0, -0.0, MULT, mybir.AluOpType.add)
+            nc.gpsimd.tensor_scalar(out, in_, 1.0, -0.0, MULT, ADD)
 
         for r in range(PACK):
-            if r > 0:
-                scatter(r, 0, SAMPLES)
+            scatter(r, HALF if r < 2 else 0, SAMPLES, de[r])
             nc.sync.dma_start(out=out_rows[LANES[r]], in_=windows[r][:])
             if r < PACK - 1:
                 round_plane(r, 0, CHUNKS // 2, nc.scalar.copy)

@@ -23,7 +23,7 @@ HALF = SAMPLES // 2
 CHUNK = 256
 CHUNKS = ITEMS // CHUNK
 SCALAR_WEAVES = 3
-U_VECTOR = 88
+U_VECTOR = 44
 LANES = (2, 0, 1, 3)
 VECTOR_ROUNDS = 2
 
@@ -43,7 +43,7 @@ def tile_attend_gbpool_E_pl_kernel(tc, xT, dz, cf, si, U, V, offs, out_0, out_1,
         def buffer(tag, name, shape, dtype):
             return sb.tile(shape, dtype, tag=tag, name=name, align_bytes=64)
 
-        si_sb = sb.tile([P, PACK], F32, name="si_sb")
+        si_sb = buffer("x_codes_1", "si_sb", [P, PACK], F32)
         nc.sync.dma_start(out=si_sb[:], in_=si[0:1, :].rearrange("o (n j) -> (o n) j", j=PACK))
         cf_sb = sb.tile([P, PACK], F32, name="cf_sb")
         nc.sync.dma_start(out=cf_sb[:], in_=cf.rearrange("(p t) o -> p (t o)", t=PACK))
@@ -61,15 +61,15 @@ def tile_attend_gbpool_E_pl_kernel(tc, xT, dz, cf, si, U, V, offs, out_0, out_1,
             nc.sync.dma_start(out=tile[:], in_=v_rows[LANES[r]])
             return tile
 
-        u_raw = buffer("chain", "u_raw", [P, PACK, K], F32)
-        nc.sync.dma_start(out=u_raw[:], in_=U.rearrange("(p j) c -> p j c", j=PACK))
+        u_raw = [load_half("u_raw", U, 0), load_half("u_raw", U, 1)]
         x_raw = [load_half("x_raw", xT, 0)]
         dz_sb = [load_half("dz", dz, 0)]
-        v_raw = [load_v(0), load_v(1)]
+        v_raw = [load_v(0)]
+        dz_sb.append(load_half("dz", dz, 1))
+        v_raw.append(load_v(1))
         x_raw.append(load_half("x_raw", xT, 1))
         offsets = sb.tile([P, SAMPLES // 16], U16, name="offsets")
         nc.sync.dma_start(offsets[:], offs)
-        dz_sb.append(load_half("dz", dz, 1))
         v_raw.extend([load_v(2), load_v(3)])
 
         ident = sb.tile([P, P], F32, name="ident")
@@ -96,19 +96,27 @@ def tile_attend_gbpool_E_pl_kernel(tc, xT, dz, cf, si, U, V, offs, out_0, out_1,
         nc.vector.memset(windows[0][:], 0.0)
         nc.gpsimd.memset(windows[1][:], 0.0)
 
-        si_ps = bank(4, "si_ps")
+        si_ps = bank(0, "si_ps")
         for j in range(PACK):
             nc.tensor.transpose(si_ps[:, j * P : (j + 1) * P], si_sb[:, j : j + 1].to_broadcast([P, P]), ident[:])
         si_rows = si_ps[:].rearrange("p (j n) -> p n j", j=PACK)
-
-        si_all = buffer("si_all", "si_all", [P, SAMPLES], F32)
-        nc.scalar.copy(out=si_all[:].rearrange("p (n j) -> p n j", j=PACK), in_=si_rows)
+        si_all = buffer("si_all", "si_all", [P, HALF], F32)
+        nc.scalar.copy(out=si_all[:].rearrange("p (n j) -> p n j", j=PACK), in_=si_rows[:, 0 : HALF // PACK, :])
+        cs = buffer("cs", "cs", [P, PACK, HALF], F32)
+        for t in range(PACK):
+            nc.scalar.activation(
+                out=cs[:, t, :].rearrange("p (n j) -> p n j", j=PACK),
+                in_=si_rows[:, HALF // PACK : SAMPLES // PACK, :],
+                func=COPY,
+                scale=cf_sb[:, t : t + 1],
+            )
 
         u_bf = buffer("u_bf", "u_bf", [P, K * PACK], BF16)
-        u_dst = u_bf[:].rearrange("p (t m j) -> p m j t", t=PACK, j=PACK)
-        u_src = u_raw[:].rearrange("p j (m t) -> p m j t", t=PACK)
-        nc.vector.tensor_copy(out=u_dst[:, 0:U_VECTOR], in_=u_src[:, 0:U_VECTOR])
-        nc.scalar.copy(out=u_dst[:, U_VECTOR:P], in_=u_src[:, U_VECTOR:P])
+        u_dst = u_bf[:].rearrange("p (t h m j) -> p h m j t", t=PACK, h=2, j=PACK)
+        u_src = [u_raw[h][:].rearrange("p j (m t) -> p m j t", t=PACK) for h in range(2)]
+        nc.vector.tensor_copy(out=u_dst[:, 0], in_=u_src[0])
+        nc.vector.tensor_copy(out=u_dst[:, 1, 0:U_VECTOR], in_=u_src[1][:, 0:U_VECTOR])
+        nc.scalar.copy(out=u_dst[:, 1, U_VECTOR : P // 2], in_=u_src[1][:, U_VECTOR : P // 2])
         u_codes = buffer("u_codes", "u_codes", [P, K], U32)
         u_scales = buffer("u_scales", "u_scales", [P, K], U8)
         nc.vector.quantize_mx(out=u_codes[:].bitcast(E4M3), scales=u_scales[:], in_=u_bf[:])
@@ -141,7 +149,7 @@ def tile_attend_gbpool_E_pl_kernel(tc, xT, dz, cf, si, U, V, offs, out_0, out_1,
 
         def interleave_x(x_bf, h, o, copy):
             copy(
-                out=x_bf[:, o * P * PACK : (o + 1) * P * PACK].rearrange("p (c i j) -> p c j i", i=4, j=PACK),
+                out=x_bf.rearrange("p (c i j) -> p c j i", i=4, j=PACK),
                 in_=x_raw[h][:, :, o * P : (o + 1) * P].rearrange("p j (c i) -> p c j i", i=4),
             )
 
@@ -149,7 +157,7 @@ def tile_attend_gbpool_E_pl_kernel(tc, xT, dz, cf, si, U, V, offs, out_0, out_1,
             nc.vector.quantize_mx(
                 out=x_codes[2 * h + o][:].bitcast(E4M3),
                 scales=x_scales[2 * h + o][:],
-                in_=x_bf[:, o * P * PACK : (o + 1) * P * PACK],
+                in_=x_bf,
             )
 
         def make_u(h, o):
@@ -166,15 +174,14 @@ def tile_attend_gbpool_E_pl_kernel(tc, xT, dz, cf, si, U, V, offs, out_0, out_1,
                 )
             return u_ps
 
-        def make_g(g, h, o, engine):
-            cols = slice(o * P, (o + 1) * P)
-            engine.tensor_tensor(out=g[:, :, cols], in0=dz_sb[h][:, :, cols], in1=cs[:, :, cols], op=MULT)
+        def make_g(g, h, o, cs, engine):
+            engine.tensor_tensor(out=g, in0=dz_sb[h][:, :, o * P : (o + 1) * P], in1=cs, op=MULT)
 
         def make_dv(u_ps, g, h, o):
             nc.vector.tensor_tensor(
                 out=dv_bf[h][:, o * P * PACK : (o + 1) * P * PACK].rearrange("p (c i t) -> p c t i", i=4, t=PACK),
                 in0=u_ps[:].rearrange("p (t c i) -> p c t i", t=PACK, i=4),
-                in1=g[:, :, o * P : (o + 1) * P].rearrange("p t (c i) -> p c t i", i=4),
+                in1=g.rearrange("p t (c i) -> p c t i", i=4),
                 op=MULT,
             )
 
@@ -203,57 +210,59 @@ def tile_attend_gbpool_E_pl_kernel(tc, xT, dz, cf, si, U, V, offs, out_0, out_1,
         def scatter(r, lo, hi, de):
             nc.vector.tensor_copy(windows[r][:].indirect(offsets[:, lo // 16 : hi // 16]), de[:])
 
-        x_bf = buffer("chain", "x_bf_0", [P, HALF * PACK], BF16)
-        interleave_x(x_bf, 0, 0, nc.scalar.copy)
-        interleave_x(x_bf, 0, 1, nc.vector.tensor_copy)
-        quantise_x(x_bf, 0, 0)
-        quantise_x(x_bf, 0, 1)
+        x_early = buffer("u_raw_1", "x_early", [P, HALF * PACK], BF16)
+        x_bf = [x_early[:, o * P * PACK : (o + 1) * P * PACK] for o in range(2)]
+        interleave_x(x_bf[0], 0, 0, nc.vector.tensor_copy)
+        interleave_x(x_bf[1], 0, 1, nc.vector.tensor_copy)
+        quantise_x(x_bf[0], 0, 0)
+        quantise_x(x_bf[1], 0, 1)
         u_ps = [make_u(0, 0), make_u(0, 1)]
-        g_and_v = buffer("chain", "g_0", [P, PACK * HALF + K // 2], F32)
-        g = g_and_v[:, 0 : PACK * HALF].rearrange("p (t i) -> p t i", t=PACK)
-        v_rounded = g_and_v[:, PACK * HALF : PACK * HALF + K // 2].bitcast(BF16)
-        for t in range(PACK):
-            nc.vector.scalar_tensor_tensor(
-                out=g[:, t, :],
-                in0=dz_sb[0][:, t, :],
-                scalar=cf_sb[:, t : t + 1],
-                in1=si_all[:, 0:HALF],
-                op0=MULT,
-                op1=MULT,
-            )
-        make_dv(u_ps[0], g, 0, 0)
-        make_dv(u_ps[1], g, 0, 1)
+        g = buffer("x_raw_0", "g_0", [P, PACK, HALF], F32)
+        v_rounded = buffer("u_raw_1", "v_rounded", [P, K], BF16)[:]
+        for o in range(2):
+            cols = slice(o * P, (o + 1) * P)
+            for t in range(PACK):
+                nc.vector.scalar_tensor_tensor(
+                    out=g[:, t, cols],
+                    in0=dz_sb[0][:, t, cols],
+                    scalar=cf_sb[:, t : t + 1],
+                    in1=si_all[:, cols],
+                    op0=MULT,
+                    op1=MULT,
+                )
+        for o in range(2):
+            make_dv(u_ps[o], g[:, :, o * P : (o + 1) * P], 0, o)
+        g_late = [buffer("dz_0", "g_2", [P, PACK, P], F32)[:]]
+        make_g(g_late[0], 1, 0, cs[:, :, 0:P], nc.gpsimd)
         turn_v(0, v_rounded)
         turn_v(1, v_rounded)
-        cs = buffer("u_bf", "cs", [P, PACK, HALF], F32)
-        for t in range(PACK):
-            nc.scalar.activation(out=cs[:, t, :], in_=si_all[:, HALF:SAMPLES], func=COPY, scale=cf_sb[:, t : t + 1])
         quantise_v(0)
         quantise_dv(0)
-        early = [product(0, 7, 0)]
+        early = [product(0, 2, 0)]
         quantise_v(1)
         early.append(product(1, 4, 0))
         de_early = copy_out(early[0], HALF, "de_a0", "de_a0")
 
-        x_bf = buffer("chain", "x_bf_1", [P, HALF * PACK], BF16)
-        interleave_x(x_bf, 1, 0, nc.vector.tensor_copy)
-        interleave_x(x_bf, 1, 1, nc.scalar.copy)
-        quantise_x(x_bf, 1, 0)
-        quantise_x(x_bf, 1, 1)
+        x_late = buffer("x_raw_0", "x_late", [P, HALF * PACK], BF16)
+        x_bf = [x_late[:, o * P * PACK : (o + 1) * P * PACK] for o in range(2)]
+        interleave_x(x_bf[0], 1, 0, nc.vector.tensor_copy)
+        interleave_x(x_bf[1], 1, 1, nc.vector.tensor_copy)
+        quantise_x(x_bf[0], 1, 0)
+        quantise_x(x_bf[1], 1, 1)
         u_ps = [make_u(1, 0), make_u(1, 1)]
-        g = buffer("chain", "g_1", [P, PACK, HALF], F32)
+        g_and_v = buffer("x_raw_0", "g_3", [P, PACK * P + K // 2], F32)
+        g_late.append(g_and_v[:, 0 : PACK * P].rearrange("p (t i) -> p t i", t=PACK))
         scatter(0, 0, HALF, de_early)
-        make_g(g, 1, 0, nc.gpsimd)
-        make_g(g, 1, 1, nc.gpsimd)
-        dv_bf.append(buffer("de_a0", "dv_bf_1", [P, HALF * PACK], BF16)[:])
-        turn_v(2, buffer("x_codes_2", "v_rounded_2", [P, K], BF16)[:])
+        make_g(g_late[1], 1, 1, cs[:, :, P:HALF], nc.gpsimd)
+        dv_bf.append(buffer("dv_bf_1", "dv_bf_1", [P, HALF * PACK], BF16)[:])
+        turn_v(2, g_and_v[:, PACK * P : PACK * P + K // 2].bitcast(BF16))
         turn_v(3, buffer("v_raw_2", "v_rounded_3", [P, K], BF16)[:])
-        make_dv(u_ps[0], g, 1, 0)
-        make_dv(u_ps[1], g, 1, 1)
+        for o in range(2):
+            make_dv(u_ps[o], g_late[o], 1, o)
         quantise_dv(1)
         quantise_v(2)
         quantise_v(3)
-        de_early = copy_out(early[1], HALF, "chain", "de_b0")
+        de_early = copy_out(early[1], HALF, "x_raw_0", "de_b0")
         windows.append(buffer("v_bf_3", "window_2", [P, ITEMS], F32))
         for n in range(4):
             nc.gpsimd.memset(windows[2][:, n * ITEMS // 4 : (n + 1) * ITEMS // 4], 0.0)

@@ -44,9 +44,9 @@ def tile_attend_gbpool_E_pl_kernel(tc, xT, dz, cf, si, U, V, offs, out_0, out_1,
             return sb.tile(shape, dtype, tag=tag, name=name, align_bytes=64)
 
         si_sb = buffer("x_codes_1", "si_sb", [P, PACK], F32)
-        nc.sync.dma_start(out=si_sb[:], in_=si[0:1, :].rearrange("o (n j) -> (o n) j", j=PACK))
+        nc.scalar.dma_start(out=si_sb[:], in_=si[0:1, :].rearrange("o (n j) -> (o n) j", j=PACK))
         cf_sb = sb.tile([P, PACK], F32, name="cf_sb")
-        nc.sync.dma_start(out=cf_sb[:], in_=cf.rearrange("(p t) o -> p (t o)", t=PACK))
+        nc.scalar.dma_start(out=cf_sb[:], in_=cf.rearrange("(p t) o -> p (t o)", t=PACK))
 
         def load_half(name, source, h):
             tile = buffer("%s_%d" % (name, h), "%s_%d" % (name, h), [P, PACK, HALF], F32)

@@ -26,6 +26,7 @@ SCALAR_WEAVES = 3
 U_VECTOR = 44
 LANES = (2, 0, 1, 3)
 VECTOR_ROUNDS = 2
+GPSIMD_ROUNDS = 3
 
 FLOPS = 2 * 2 * K * K * SAMPLES
 BYTES = 4 * (4 * K * K + K + SAMPLES) + 2 * P * SAMPLES // 16 + 4 * K * ITEMS + K * ITEMS + 16 * ITEMS
@@ -73,7 +74,7 @@ def tile_attend_gbpool_E_pl_kernel(tc, xT, dz, cf, si, U, V, offs, out_0, out_1,
         v_raw.extend([load_v(2), load_v(3)])
 
         ident = sb.tile([P, P], F32, name="ident")
-        zeros = buffer("zeros_then_window", "zeros", [P, P], F32)
+        zeros = buffer("zeros", "zeros", [P, P], F32)
         nc.gpsimd.memset(zeros[:], 0.0)
         nc.gpsimd.affine_select(
             out=ident[:],
@@ -87,14 +88,11 @@ def tile_attend_gbpool_E_pl_kernel(tc, xT, dz, cf, si, U, V, offs, out_0, out_1,
 
         dv_codes = buffer("dv_codes", "dv_codes", [P, HALF + SAMPLES], U32)
         dv_scales = buffer("dv_scales", "dv_scales", [P, HALF + SAMPLES], U8)
-        windows = [
-            buffer("window_0", "window_0", [P, ITEMS], F32),
-            buffer("zeros_then_window", "window_1", [P, ITEMS], F32),
-        ]
+        windows = [buffer("window_%d" % r, "window_%d" % r, [P, ITEMS], F32) for r in range(PACK - 1)]
         nc.vector.memset(dv_codes[:, 0:HALF], 0)
         nc.vector.memset(dv_scales[:, 0:HALF], 0)
-        nc.vector.memset(windows[0][:], 0.0)
-        nc.gpsimd.memset(windows[1][:], 0.0)
+        for window in windows:
+            nc.vector.memset(window[:], 0.0)
 
         si_ps = bank(0, "si_ps")
         for j in range(PACK):
@@ -263,9 +261,6 @@ def tile_attend_gbpool_E_pl_kernel(tc, xT, dz, cf, si, U, V, offs, out_0, out_1,
         quantise_v(2)
         quantise_v(3)
         de_early = copy_out(early[1], HALF, "x_raw_0", "de_b0")
-        windows.append(buffer("v_bf_3", "window_2", [P, ITEMS], F32))
-        for n in range(4):
-            nc.gpsimd.memset(windows[2][:, n * ITEMS // 4 : (n + 1) * ITEMS // 4], 0.0)
         windows.append(windows[0])
         scatter(1, 0, HALF, de_early)
         de = [
@@ -290,9 +285,11 @@ def tile_attend_gbpool_E_pl_kernel(tc, xT, dz, cf, si, U, V, offs, out_0, out_1,
         for r in range(PACK):
             scatter(r, HALF if r < 2 else 0, SAMPLES, de[r])
             nc.sync.dma_start(out=out_rows[LANES[r]], in_=windows[r][:])
-            if r < PACK - 1:
-                round_plane(r, 0, CHUNKS // 2, nc.scalar.copy)
-                round_plane(r, CHUNKS // 2, CHUNKS // 2, gpsimd_round)
+            if r == 0:
+                round_plane(r, 0, CHUNKS, nc.scalar.copy)
+            elif r < PACK - 1:
+                round_plane(r, 0, CHUNKS - GPSIMD_ROUNDS, nc.scalar.copy)
+                round_plane(r, CHUNKS - GPSIMD_ROUNDS, GPSIMD_ROUNDS, gpsimd_round)
 
         y_bf = sb.tile([P, ITEMS * PACK], BF16, name="y_bf", align_bytes=64)
         y_codes = sb.tile([P, ITEMS], U32, name="y_codes", align_bytes=64)

@@ -66,9 +66,9 @@ def tile_attend_gbpool_E_pl_kernel(tc, xT, dz, cf, si, U, V, offs, out_0, out_1,
         x_raw = [load_half("x_raw", xT, 0)]
         dz_sb = [load_half("dz", dz, 0)]
         v_raw = [load_v(0)]
-        dz_sb.append(load_half("dz", dz, 1))
         v_raw.append(load_v(1))
         x_raw.append(load_half("x_raw", xT, 1))
+        dz_sb.append(load_half("dz", dz, 1))
         offsets = sb.tile([P, SAMPLES // 16], U16, name="offsets")
         nc.sync.dma_start(offsets[:], offs)
         v_raw.extend([load_v(2), load_v(3)])
@@ -100,11 +100,13 @@ def tile_attend_gbpool_E_pl_kernel(tc, xT, dz, cf, si, U, V, offs, out_0, out_1,
         si_rows = si_ps[:].rearrange("p (j n) -> p n j", j=PACK)
         si_all = buffer("si_all", "si_all", [P, HALF], F32)
         nc.scalar.copy(out=si_all[:].rearrange("p (n j) -> p n j", j=PACK), in_=si_rows[:, 0 : HALF // PACK, :])
-        cs = buffer("cs", "cs", [P, PACK, HALF], F32)
+        si_third = buffer("si_third", "si_third", [P, P], F32)
+        nc.scalar.copy(out=si_third[:].rearrange("p (n j) -> p n j", j=PACK), in_=si_rows[:, 2 * P // PACK : 3 * P // PACK, :])
+        cs = buffer("cs", "cs", [P, PACK, P], F32)
         for t in range(PACK):
             nc.scalar.activation(
                 out=cs[:, t, :].rearrange("p (n j) -> p n j", j=PACK),
-                in_=si_rows[:, HALF // PACK : SAMPLES // PACK, :],
+                in_=si_rows[:, 3 * P // PACK : SAMPLES // PACK, :],
                 func=COPY,
                 scale=cf_sb[:, t : t + 1],
             )
@@ -123,11 +125,13 @@ def tile_attend_gbpool_E_pl_kernel(tc, xT, dz, cf, si, U, V, offs, out_0, out_1,
         v_codes = buffer("v_codes", "v_codes", [P, K], U32)
         v_scales = buffer("v_scales", "v_scales", [P, K], U8)
 
-        def turn_v(r, rounded):
+        def round_v(r, rounded):
             nc.scalar.copy(
                 out=rounded.rearrange("s (u p e) -> s u p e", u=2, e=2),
                 in_=v_raw[r][:].rearrange("s (p u e) -> s u p e", u=2, e=2),
             )
+
+        def turn_v(r, rounded):
             words = rounded.bitcast(F32)
             turned = bank(5 + r % 2, "v_turned_%d" % r)
             for u in range(2):
@@ -172,8 +176,16 @@ def tile_attend_gbpool_E_pl_kernel(tc, xT, dz, cf, si, U, V, offs, out_0, out_1,
                 )
             return u_ps
 
-        def make_g(g, h, o, cs, engine):
-            engine.tensor_tensor(out=g, in0=dz_sb[h][:, :, o * P : (o + 1) * P], in1=cs, op=MULT)
+        def g_on_vector(g, h, o, si_rows):
+            for t in range(PACK):
+                nc.vector.scalar_tensor_tensor(
+                    out=g[:, t, :],
+                    in0=dz_sb[h][:, t, o * P : (o + 1) * P],
+                    scalar=cf_sb[:, t : t + 1],
+                    in1=si_rows,
+                    op0=MULT,
+                    op1=MULT,
+                )
 
         def make_dv(u_ps, g, h, o):
             nc.vector.tensor_tensor(
@@ -216,51 +228,43 @@ def tile_attend_gbpool_E_pl_kernel(tc, xT, dz, cf, si, U, V, offs, out_0, out_1,
         quantise_x(x_bf[1], 0, 1)
         u_ps = [make_u(0, 0), make_u(0, 1)]
         g = buffer("x_raw_0", "g_0", [P, PACK, HALF], F32)
-        v_rounded = buffer("u_raw_1", "v_rounded", [P, K], BF16)[:]
+        v_rounded = buffer("u_raw_1", "v_rounded", [P, 2, K], BF16)
         for o in range(2):
-            cols = slice(o * P, (o + 1) * P)
-            for t in range(PACK):
-                nc.vector.scalar_tensor_tensor(
-                    out=g[:, t, cols],
-                    in0=dz_sb[0][:, t, cols],
-                    scalar=cf_sb[:, t : t + 1],
-                    in1=si_all[:, cols],
-                    op0=MULT,
-                    op1=MULT,
-                )
+            g_on_vector(g[:, :, o * P : (o + 1) * P], 0, o, si_all[:, o * P : (o + 1) * P])
         for o in range(2):
             make_dv(u_ps[o], g[:, :, o * P : (o + 1) * P], 0, o)
-        g_late = [buffer("dz_0", "g_2", [P, PACK, P], F32)[:]]
-        make_g(g_late[0], 1, 0, cs[:, :, 0:P], nc.gpsimd)
-        turn_v(0, v_rounded)
-        turn_v(1, v_rounded)
+        for r in range(2):
+            round_v(r, v_rounded[:, r, :])
+        for r in range(2):
+            turn_v(r, v_rounded[:, r, :])
         quantise_v(0)
         quantise_dv(0)
-        early = [product(0, 2, 0)]
-        quantise_v(1)
-        early.append(product(1, 4, 0))
-        de_early = copy_out(early[0], HALF, "de_a0", "de_a0")
+        de_early = copy_out(product(0, 2, 0), HALF, "de_a0", "de_a0")
 
-        x_late = buffer("x_raw_0", "x_late", [P, HALF * PACK], BF16)
-        x_bf = [x_late[:, o * P * PACK : (o + 1) * P * PACK] for o in range(2)]
+        x_bf = [buffer(tag, "x_late_" + tag, [P, P * PACK], BF16)[:] for tag in ("v_bf_0", "dv_bf_0")]
         interleave_x(x_bf[0], 1, 0, nc.vector.tensor_copy)
         interleave_x(x_bf[1], 1, 1, nc.vector.tensor_copy)
         quantise_x(x_bf[0], 1, 0)
         quantise_x(x_bf[1], 1, 1)
+        quantise_v(1)
         u_ps = [make_u(1, 0), make_u(1, 1)]
-        g_and_v = buffer("x_raw_0", "g_3", [P, PACK * P + K // 2], F32)
-        g_late.append(g_and_v[:, 0 : PACK * P].rearrange("p (t i) -> p t i", t=PACK))
+        early = product(1, 4, 0)
+        g_late = [buffer("v_bf_0", "g_2", [P, PACK, P], F32)[:]]
+        g_on_vector(g_late[0], 1, 0, si_third[:])
         scatter(0, 0, HALF, de_early)
-        make_g(g_late[1], 1, 1, cs[:, :, P:HALF], nc.gpsimd)
+        g_late.append(buffer("si_third", "g_3", [P, PACK, P], F32)[:])
+        nc.gpsimd.tensor_tensor(out=g_late[1], in0=dz_sb[1][:, :, P:HALF], in1=cs[:], op=MULT)
         dv_bf.append(buffer("dv_bf_1", "dv_bf_1", [P, HALF * PACK], BF16)[:])
-        turn_v(2, g_and_v[:, PACK * P : PACK * P + K // 2].bitcast(BF16))
-        turn_v(3, buffer("v_raw_2", "v_rounded_3", [P, K], BF16)[:])
+        for r, tag in ((2, "dv_bf_0"), (3, "v_raw_2")):
+            rounded = buffer(tag, "v_rounded_%d" % r, [P, K], BF16)[:]
+            round_v(r, rounded)
+            turn_v(r, rounded)
         for o in range(2):
             make_dv(u_ps[o], g_late[o], 1, o)
-        quantise_dv(1)
         quantise_v(2)
+        quantise_dv(1)
         quantise_v(3)
-        de_early = copy_out(early[1], HALF, "x_raw_0", "de_b0")
+        de_early = copy_out(early, HALF, "si_third", "de_b0")
         windows.append(windows[0])
         scatter(1, 0, HALF, de_early)
         de = [

@@ -111,15 +111,20 @@ def tile_attend_gbpool_E_pl_kernel(tc, xT, dz, cf, si, U, V, offs, out_0, out_1,
                 scale=cf_sb[:, t : t + 1],
             )
 
-        u_bf = buffer("u_bf", "u_bf", [P, K * PACK], BF16)
-        u_dst = u_bf[:].rearrange("p (t h m j) -> p h m j t", t=PACK, h=2, j=PACK)
-        u_src = [u_raw[h][:].rearrange("p j (m t) -> p m j t", t=PACK) for h in range(2)]
-        nc.vector.tensor_copy(out=u_dst[:, 0], in_=u_src[0])
-        nc.vector.tensor_copy(out=u_dst[:, 1, 0:U_VECTOR], in_=u_src[1][:, 0:U_VECTOR])
-        nc.scalar.copy(out=u_dst[:, 1, U_VECTOR : P // 2], in_=u_src[1][:, U_VECTOR : P // 2])
         u_codes = buffer("u_codes", "u_codes", [P, K], U32)
         u_scales = buffer("u_scales", "u_scales", [P, K], U8)
-        nc.vector.quantize_mx(out=u_codes[:].bitcast(E4M3), scales=u_scales[:], in_=u_bf[:])
+        for h in range(2):
+            u_bf = buffer("u_bf_%d" % h, "u_bf_%d" % h, [P, PACK, P // 2 * PACK], BF16)
+            u_dst = u_bf[:].rearrange("p t (m j) -> p m j t", j=PACK)
+            u_src = u_raw[h][:].rearrange("p j (m t) -> p m j t", t=PACK)
+            if h == 0:
+                nc.vector.tensor_copy(out=u_dst, in_=u_src)
+            else:
+                nc.vector.tensor_copy(out=u_dst[:, 0:U_VECTOR], in_=u_src[:, 0:U_VECTOR])
+                nc.scalar.copy(out=u_dst[:, U_VECTOR : P // 2], in_=u_src[:, U_VECTOR : P // 2])
+            for t in range(PACK):
+                cols = slice(t * P + h * P // 2, t * P + (h + 1) * P // 2)
+                nc.vector.quantize_mx(out=u_codes[:, cols].bitcast(E4M3), scales=u_scales[:, cols], in_=u_bf[:, t, :])
 
         v_bf = [buffer("v_bf_%d" % r, "v_bf_%d" % r, [P, K], BF16) for r in range(PACK)]
         v_codes = buffer("v_codes", "v_codes", [P, K], U32)
@@ -223,7 +228,7 @@ def tile_attend_gbpool_E_pl_kernel(tc, xT, dz, cf, si, U, V, offs, out_0, out_1,
         x_early = buffer("u_raw_1", "x_early", [P, HALF * PACK], BF16)
         x_bf = [x_early[:, o * P * PACK : (o + 1) * P * PACK] for o in range(2)]
         interleave_x(x_bf[0], 0, 0, nc.vector.tensor_copy)
-        interleave_x(x_bf[1], 0, 1, nc.vector.tensor_copy)
+        interleave_x(x_bf[1], 0, 1, nc.scalar.copy)
         quantise_x(x_bf[0], 0, 0)
         quantise_x(x_bf[1], 0, 1)
         u_ps = [make_u(0, 0), make_u(0, 1)]

@@ -27,6 +27,7 @@ U_VECTOR = 44
 LANES = (2, 0, 1, 3)
 VECTOR_ROUNDS = 2
 GPSIMD_ROUNDS = 3
+U_BANKS = (7, 1, 2, 3)
 
 FLOPS = 2 * 2 * K * K * SAMPLES
 BYTES = 4 * (4 * K * K + K + SAMPLES) + 2 * P * SAMPLES // 16 + 4 * K * ITEMS + K * ITEMS + 16 * ITEMS
@@ -168,7 +169,7 @@ def tile_attend_gbpool_E_pl_kernel(tc, xT, dz, cf, si, U, V, offs, out_0, out_1,
             )
 
         def make_u(h, o):
-            u_ps = bank(2 * h + o, "u_%d_%d" % (h, o))
+            u_ps = bank(U_BANKS[2 * h + o], "u_%d_%d" % (h, o))
             for t in range(PACK):
                 nc.tensor.matmul_mx(
                     out=u_ps[:, t * P : (t + 1) * P],
@@ -228,7 +229,7 @@ def tile_attend_gbpool_E_pl_kernel(tc, xT, dz, cf, si, U, V, offs, out_0, out_1,
         x_early = buffer("u_raw_1", "x_early", [P, HALF * PACK], BF16)
         x_bf = [x_early[:, o * P * PACK : (o + 1) * P * PACK] for o in range(2)]
         interleave_x(x_bf[0], 0, 0, nc.vector.tensor_copy)
-        interleave_x(x_bf[1], 0, 1, nc.scalar.copy)
+        interleave_x(x_bf[1], 0, 1, nc.vector.tensor_copy)
         quantise_x(x_bf[0], 0, 0)
         quantise_x(x_bf[1], 0, 1)
         u_ps = [make_u(0, 0), make_u(0, 1)]

@@ -27,6 +27,7 @@ U_VECTOR = 44
 LANES = (2, 0, 1, 3)
 VECTOR_ROUNDS = 2
 GPSIMD_ROUNDS = 3
+PLACES = {"u_raw_1": 0, "x_early": 0, "v_rounded_0_0": 0, "v_rounded_0_1": 512, "v_rounded_1_0": 1024, "v_rounded_1_1": 1536}
 U_BANKS = (7, 1, 2, 3)
 
 FLOPS = 2 * 2 * K * K * SAMPLES
@@ -37,12 +38,15 @@ def tile_attend_gbpool_E_pl_kernel(tc, xT, dz, cf, si, U, V, offs, out_0, out_1,
     nc = tc.nc
     with ExitStack() as ctx:
         sb = ctx.enter_context(tc.tile_pool(name="sb", bufs=1))
+        shared = ctx.enter_context(tc.tile_pool(name="shared", bufs=1))
         ps = ctx.enter_context(tc.psum_pool(name="ps", bufs=1))
 
         def bank(number, name):
             return ps.tile([P, 512], F32, tag="bank_%d" % number, name=name)
 
         def buffer(tag, name, shape, dtype):
+            if name in PLACES:
+                return shared.tile(shape, dtype, name=name, align_bytes=64, offset=PLACES[name])
             return sb.tile(shape, dtype, tag=tag, name=name, align_bytes=64)
 
         si_sb = buffer("x_codes_1", "si_sb", [P, PACK], F32)
@@ -128,32 +132,33 @@ def tile_attend_gbpool_E_pl_kernel(tc, xT, dz, cf, si, U, V, offs, out_0, out_1,
                 nc.vector.quantize_mx(out=u_codes[:, cols].bitcast(E4M3), scales=u_scales[:, cols], in_=u_bf[:, t, :])
 
         v_bf = [buffer("v_bf_%d" % r, "v_bf_%d" % r, [P, K], BF16) for r in range(PACK)]
-        v_codes = buffer("v_codes", "v_codes", [P, K], U32)
+        v_codes = []
         v_scales = buffer("v_scales", "v_scales", [P, K], U8)
 
-        def round_v(r, rounded):
+        def round_v(r, rounded, first):
+            count = rounded.shape[1] // (2 * P)
             nc.scalar.copy(
-                out=rounded.rearrange("s (u p e) -> s u p e", u=2, e=2),
-                in_=v_raw[r][:].rearrange("s (p u e) -> s u p e", u=2, e=2),
+                out=rounded.rearrange("s (u p e) -> s u p e", u=count, e=2),
+                in_=v_raw[r][:].rearrange("s (p u e) -> s u p e", u=2, e=2)[:, first : first + count],
             )
+            return [rounded.bitcast(F32)[:, u * P : (u + 1) * P] for u in range(count)]
 
-        def turn_v(r, rounded):
-            words = rounded.bitcast(F32)
+        def turn_v(r, words):
             turned = bank(5 + r % 2, "v_turned_%d" % r)
             for u in range(2):
-                nc.tensor.transpose(turned[:, u * P : (u + 1) * P], words[:, u * P : (u + 1) * P], ident[:])
+                nc.tensor.transpose(turned[:, u * P : (u + 1) * P], words[u], ident[:])
             nc.scalar.copy(
                 out=v_bf[r][:].bitcast(F32).rearrange("p (s u) -> p s u", u=2),
                 in_=turned[:, 0 : 2 * P].rearrange("p (u s) -> p s u", u=2),
             )
 
-        def quantise_v(r):
-            cols = slice(r * P, (r + 1) * P)
-            nc.vector.quantize_mx(out=v_codes[:, cols].bitcast(E4M3), scales=v_scales[:, cols], in_=v_bf[r][:])
+        def quantise_v(r, tag):
+            v_codes.append(buffer(tag, "v_codes_%d" % r, [P, P], U32)[:])
+            nc.vector.quantize_mx(out=v_codes[r].bitcast(E4M3), scales=v_scales[:, r * P : (r + 1) * P], in_=v_bf[r][:])
 
         x_codes = [buffer("x_codes_%d" % q, "x_codes_%d" % q, [P, P], U32) for q in range(4)]
         x_scales = [buffer("x_scales_%d" % q, "x_scales_%d" % q, [P, P], U8) for q in range(4)]
-        dv_bf = [buffer("dv_bf_0", "dv_bf_0", [P, HALF * PACK], BF16)[:]]
+        dv_bf = [buffer("dv_bf_%d" % q, "dv_bf_%d" % q, [P, P * PACK], BF16)[:] for q in range(4)]
 
         def interleave_x(x_bf, h, o, copy):
             copy(
@@ -195,21 +200,21 @@ def tile_attend_gbpool_E_pl_kernel(tc, xT, dz, cf, si, U, V, offs, out_0, out_1,
 
         def make_dv(u_ps, g, h, o):
             nc.vector.tensor_tensor(
-                out=dv_bf[h][:, o * P * PACK : (o + 1) * P * PACK].rearrange("p (c i t) -> p c t i", i=4, t=PACK),
+                out=dv_bf[2 * h + o].rearrange("p (c i t) -> p c t i", i=4, t=PACK),
                 in0=u_ps[:].rearrange("p (t c i) -> p c t i", t=PACK, i=4),
                 in1=g.rearrange("p t (c i) -> p c t i", i=4),
                 op=MULT,
             )
 
-        def quantise_dv(h):
-            cols = slice((h + 1) * HALF, (h + 2) * HALF)
-            nc.vector.quantize_mx(out=dv_codes[:, cols].bitcast(E5M2), scales=dv_scales[:, cols], in_=dv_bf[h])
+        def quantise_dv(q):
+            cols = slice(HALF + q * P, HALF + (q + 1) * P)
+            nc.vector.quantize_mx(out=dv_codes[:, cols].bitcast(E5M2), scales=dv_scales[:, cols], in_=dv_bf[q])
 
         def product(r, number, first):
             acc = bank(number, "de_ps_%d_%d" % (r, first))
             nc.tensor.matmul_mx(
                 out=acc[:],
-                lhsT=v_codes[:, r * P : (r + 1) * P].bitcast(E4M3),
+                lhsT=v_codes[r].bitcast(E4M3),
                 lhsT_scale=v_scales[:, r * P : (r + 1) * P],
                 rhs=dv_codes[:, first : first + SAMPLES].bitcast(E5M2),
                 rhs_scale=dv_scales[:, first : first + SAMPLES],
@@ -234,42 +239,42 @@ def tile_attend_gbpool_E_pl_kernel(tc, xT, dz, cf, si, U, V, offs, out_0, out_1,
         quantise_x(x_bf[1], 0, 1)
         u_ps = [make_u(0, 0), make_u(0, 1)]
         g = buffer("x_raw_0", "g_0", [P, PACK, HALF], F32)
-        v_rounded = buffer("u_raw_1", "v_rounded", [P, 2, K], BF16)
         for o in range(2):
             g_on_vector(g[:, :, o * P : (o + 1) * P], 0, o, si_all[:, o * P : (o + 1) * P])
         for o in range(2):
             make_dv(u_ps[o], g[:, :, o * P : (o + 1) * P], 0, o)
+        words = [
+            round_v(r, buffer("", "v_rounded_%d_%d" % (r, u), [P, K // 2], BF16)[:], u)[0] for r in range(2) for u in range(2)
+        ]
         for r in range(2):
-            round_v(r, v_rounded[:, r, :])
-        for r in range(2):
-            turn_v(r, v_rounded[:, r, :])
-        quantise_v(0)
+            turn_v(r, words[2 * r : 2 * r + 2])
         quantise_dv(0)
+        quantise_v(0, "v_codes_0")
+        quantise_dv(1)
         de_early = copy_out(product(0, 2, 0), HALF, "de_a0", "de_a0")
 
-        x_bf = [buffer(tag, "x_late_" + tag, [P, P * PACK], BF16)[:] for tag in ("v_bf_0", "dv_bf_0")]
+        x_bf = [buffer(tag, "x_late_" + tag, [P, P * PACK], BF16)[:] for tag in ("x_raw_0", "dv_bf_0")]
         interleave_x(x_bf[0], 1, 0, nc.vector.tensor_copy)
         interleave_x(x_bf[1], 1, 1, nc.vector.tensor_copy)
         quantise_x(x_bf[0], 1, 0)
         quantise_x(x_bf[1], 1, 1)
-        quantise_v(1)
+        quantise_v(1, "v_codes_1")
         u_ps = [make_u(1, 0), make_u(1, 1)]
         early = product(1, 4, 0)
-        g_late = [buffer("v_bf_0", "g_2", [P, PACK, P], F32)[:]]
+        g_late = [buffer("x_raw_0", "g_2", [P, PACK, P], F32)[:]]
         g_on_vector(g_late[0], 1, 0, si_third[:])
         scatter(0, 0, HALF, de_early)
         g_late.append(buffer("si_third", "g_3", [P, PACK, P], F32)[:])
         nc.gpsimd.tensor_tensor(out=g_late[1], in0=dz_sb[1][:, :, P:HALF], in1=cs[:], op=MULT)
-        dv_bf.append(buffer("dv_bf_1", "dv_bf_1", [P, HALF * PACK], BF16)[:])
         for r, tag in ((2, "dv_bf_0"), (3, "v_raw_2")):
             rounded = buffer(tag, "v_rounded_%d" % r, [P, K], BF16)[:]
-            round_v(r, rounded)
-            turn_v(r, rounded)
+            turn_v(r, round_v(r, rounded, 0))
         for o in range(2):
             make_dv(u_ps[o], g_late[o], 1, o)
-        quantise_v(2)
-        quantise_dv(1)
-        quantise_v(3)
+        quantise_dv(2)
+        quantise_dv(3)
+        quantise_v(2, "v_codes_2")
+        quantise_v(3, "v_codes_3")
         de_early = copy_out(early, HALF, "si_third", "de_b0")
         windows.append(windows[0])
         scatter(1, 0, HALF, de_early)
@@ -279,7 +284,7 @@ def tile_attend_gbpool_E_pl_kernel(tc, xT, dz, cf, si, U, V, offs, out_0, out_1,
         ]
 
         out_rows = out_0.rearrange("(s r) c -> r s c", r=PACK)
-        pairs = buffer("v_codes", "pairs", [P, ITEMS * PACK], BF16)
+        pairs = buffer("v_codes_3", "pairs", [P, ITEMS * PACK], BF16)
         pair_view = pairs[:].rearrange("p (n a c l) -> p n a c l", a=2, c=CHUNK, l=2)
 
         def round_plane(r, first, count, copy):

@@ -27,7 +27,7 @@ U_VECTOR = 44
 LANES = (2, 0, 1, 3)
 VECTOR_ROUNDS = 2
 GPSIMD_ROUNDS = 3
-PLACES = {"u_raw_1": 0, "x_early": 0, "v_rounded_0_0": 0, "v_rounded_0_1": 512, "v_rounded_1_0": 1024, "v_rounded_1_1": 1536}
+PLACES = {"u_raw_1": 0, "x_early": 0, "v_rounded_0_0": 0, "v_rounded_0_1": 512, "v_rounded_1_0": 1024, "v_rounded_1_1": 1536, "si_sb": 4096, "x_codes_0": 4096, "x_codes_1": 4608}
 U_BANKS = (7, 1, 2, 3)
 
 FLOPS = 2 * 2 * K * K * SAMPLES
@@ -49,8 +49,8 @@ def tile_attend_gbpool_E_pl_kernel(tc, xT, dz, cf, si, U, V, offs, out_0, out_1,
                 return shared.tile(shape, dtype, name=name, align_bytes=64, offset=PLACES[name])
             return sb.tile(shape, dtype, tag=tag, name=name, align_bytes=64)
 
-        si_sb = buffer("x_codes_1", "si_sb", [P, PACK], F32)
-        nc.scalar.dma_start(out=si_sb[:], in_=si[0:1, :].rearrange("o (n j) -> (o n) j", j=PACK))
+        si_sb = buffer("si_sb", "si_sb", [P, HALF], F32)
+        nc.scalar.dma_start(out=si_sb[:, 0:PACK], in_=si[0:1, :].rearrange("o (n j) -> (o n) j", j=PACK))
         cf_sb = sb.tile([P, PACK], F32, name="cf_sb")
         nc.scalar.dma_start(out=cf_sb[:], in_=cf.rearrange("(p t) o -> p (t o)", t=PACK))
 
@@ -93,7 +93,7 @@ def tile_attend_gbpool_E_pl_kernel(tc, xT, dz, cf, si, U, V, offs, out_0, out_1,
 
         dv_codes = buffer("dv_codes", "dv_codes", [P, HALF + SAMPLES], U32)
         dv_scales = buffer("dv_scales", "dv_scales", [P, HALF + SAMPLES], U8)
-        windows = [buffer("window_%d" % r, "window_%d" % r, [P, ITEMS], F32) for r in range(PACK - 1)]
+        windows = [buffer("window_%d" % r, "window_%d" % r, [P, ITEMS], F32) for r in range(2)]
         nc.vector.memset(dv_codes[:, 0:HALF], 0)
         nc.vector.memset(dv_scales[:, 0:HALF], 0)
         for window in windows:
@@ -276,6 +276,8 @@ def tile_attend_gbpool_E_pl_kernel(tc, xT, dz, cf, si, U, V, offs, out_0, out_1,
         quantise_v(2, "v_codes_2")
         quantise_v(3, "v_codes_3")
         de_early = copy_out(early, HALF, "si_third", "de_b0")
+        windows.append(buffer("v_bf_3", "window_2", [P, ITEMS], F32))
+        nc.gpsimd.memset(windows[2][:], 0.0)
         windows.append(windows[0])
         scatter(1, 0, HALF, de_early)
         de = [

@@ -28,7 +28,7 @@ LANES = (2, 0, 1, 3)
 VECTOR_ROUNDS = 2
 GPSIMD_ROUNDS = 3
 PLACES = {"u_raw_1": 0, "x_early": 0, "v_rounded_0_0": 0, "v_rounded_0_1": 512, "v_rounded_1_0": 1024, "v_rounded_1_1": 1536, "si_sb": 4096, "x_codes_0": 4096, "x_codes_1": 4608}
-U_BANKS = (7, 1, 2, 3)
+U_BANKS = (7, 1, 7, 3)
 
 FLOPS = 2 * 2 * K * K * SAMPLES
 BYTES = 4 * (4 * K * K + K + SAMPLES) + 2 * P * SAMPLES // 16 + 4 * K * ITEMS + K * ITEMS + 16 * ITEMS
@@ -302,9 +302,7 @@ def tile_attend_gbpool_E_pl_kernel(tc, xT, dz, cf, si, U, V, offs, out_0, out_1,
         for r in range(PACK):
             scatter(r, HALF if r < 2 else 0, SAMPLES, de[r])
             nc.sync.dma_start(out=out_rows[LANES[r]], in_=windows[r][:])
-            if r == 0:
-                round_plane(r, 0, CHUNKS, nc.scalar.copy)
-            elif r < PACK - 1:
+            if r < PACK - 1:
                 round_plane(r, 0, CHUNKS - GPSIMD_ROUNDS, nc.scalar.copy)
                 round_plane(r, CHUNKS - GPSIMD_ROUNDS, GPSIMD_ROUNDS, gpsimd_round)
 

@@ -27,6 +27,7 @@ U_VECTOR = 44
 LANES = (2, 0, 1, 3)
 VECTOR_ROUNDS = 2
 GPSIMD_ROUNDS = 3
+STORE_ENDS = [0, 2 * CHUNK, 4 * CHUNK, 6 * CHUNK, ITEMS - CHUNK // 2, ITEMS]
 PLACES = {"u_raw_1": 0, "x_early": 0, "v_rounded_0_0": 0, "v_rounded_0_1": 512, "v_rounded_1_0": 1024, "v_rounded_1_1": 1536, "si_sb": 4096, "x_codes_0": 4096, "x_codes_1": 4608}
 U_BANKS = (7, 1, 7, 3)
 
@@ -275,7 +276,7 @@ def tile_attend_gbpool_E_pl_kernel(tc, xT, dz, cf, si, U, V, offs, out_0, out_1,
         quantise_dv(3)
         quantise_v(2, "v_codes_2")
         quantise_v(3, "v_codes_3")
-        de_early = copy_out(early, HALF, "si_third", "de_b0")
+        de_early = copy_out(early, HALF, "cs", "de_b0")
         windows.append(buffer("v_bf_3", "window_2", [P, ITEMS], F32))
         nc.gpsimd.memset(windows[2][:], 0.0)
         windows.append(windows[0])
@@ -313,35 +314,36 @@ def tile_attend_gbpool_E_pl_kernel(tc, xT, dz, cf, si, U, V, offs, out_0, out_1,
         y_words = y_bf[:].bitcast(F32)
         words_out = out_1[0].rearrange("p c l -> p (c l)").bitcast(I32)
 
-        def weave(n):
-            cols = slice(2 * n * CHUNK, 2 * (n + 1) * CHUNK)
-            dst = y_words[:, cols].rearrange("p (c i a) -> p c a i", i=4, a=2)
-            src = pair_words[:, cols].rearrange("p (a c i) -> p c a i", i=4, a=2)
+        def weave(lo, hi):
+            n = lo // CHUNK
+            dst = y_words[:, 2 * lo : 2 * hi].rearrange("p (c i a) -> p c a i", i=4, a=2)
+            src = pair_words[:, 2 * n * CHUNK : 2 * (n + 1) * CHUNK].rearrange("p (a c i) -> p c a i", i=4, a=2)
+            src = src[:, (lo - n * CHUNK) // 4 : (hi - n * CHUNK) // 4]
             if n >= CHUNKS - SCALAR_WEAVES:
                 nc.scalar.copy(out=dst, in_=src)
             else:
                 nc.vector.tensor_copy(out=dst, in_=src)
 
-        def quantise_y(n):
-            lo, hi = n * CHUNK, (n + 1) * CHUNK
-            group, side = divmod(n, 2)
+        def quantise_y(lo, hi):
+            group, column = divmod(lo, ITEMS // PACK)
             nc.vector.quantize_mx(
                 out=y_codes[:, lo:hi].bitcast(E4M3),
-                scales=y_scales[4 * group : P, side * CHUNK : (side + 1) * CHUNK],
+                scales=y_scales[4 * group : P, column : column + hi - lo],
                 in_=y_bf[:, PACK * lo : PACK * hi],
             )
-            if n >= CHUNKS - 2:
-                nc.sync.dma_start(out=words_out[:, lo:hi], in_=y_codes[:, lo:hi].bitcast(I32))
-            elif side == 1:
-                nc.sync.dma_start(out=words_out[:, lo - CHUNK : hi], in_=y_codes[:, lo - CHUNK : hi].bitcast(I32))
+            if hi in STORE_ENDS:
+                first = STORE_ENDS[STORE_ENDS.index(hi) - 1]
+                nc.sync.dma_start(out=words_out[:, first:hi], in_=y_codes[:, first:hi].bitcast(I32))
 
         for n in range(CHUNKS):
             round_plane(PACK - 1, n, 1, nc.vector.tensor_copy if n < VECTOR_ROUNDS else nc.scalar.copy)
-        for n in range(CHUNKS):
-            weave(n)
+        edges = list(range(0, ITEMS, CHUNK)) + [ITEMS - CHUNK // 2, ITEMS]
+        pieces = list(zip(edges[:-1], edges[1:]))
+        for n, piece in enumerate(pieces):
+            weave(*piece)
             if n >= 1:
-                quantise_y(n - 1)
-        quantise_y(CHUNKS - 1)
+                quantise_y(*pieces[n - 1])
+        quantise_y(*pieces[-1])
 
         scales_out = out_2[0].bitcast(I32).rearrange("(q j) (g c) -> q g j c", j=4, g=4)
         for quad in range(4):

@@ -22,14 +22,29 @@ ITEMS = 2048
 HALF = SAMPLES // 2
 CHUNK = 256
 CHUNKS = ITEMS // CHUNK
-SCALAR_WEAVES = 3
+SCALAR_WEAVES = 1
 U_VECTOR = 44
-LANES = (2, 0, 1, 3)
-VECTOR_ROUNDS = 2
-GPSIMD_ROUNDS = 3
+GPSIMD_CHUNKS = 4
+SCALAR_CHUNKS = 3
+PAD = 32
 STORE_ENDS = [0, 2 * CHUNK, 4 * CHUNK, 6 * CHUNK, ITEMS - CHUNK // 2, ITEMS]
-PLACES = {"u_raw_1": 0, "x_early": 0, "v_rounded_0_0": 0, "v_rounded_0_1": 512, "v_rounded_1_0": 1024, "v_rounded_1_1": 1536, "si_sb": 4096, "x_codes_0": 4096, "x_codes_1": 4608}
-U_BANKS = (7, 1, 7, 3)
+PLACES = {
+    "u_raw_1": 0,
+    "x_early": 0,
+    "window_3": 2048,
+    "si_sb": 10240,
+    "x_codes_0": 10240,
+    "x_codes_1": 10752,
+    "dv_bf_0": 11264,
+    "x_late_1": 11264,
+    "window_1": 12288,
+    "pairs_5": 20480,
+    "de_3": 24576,
+    "de_0b": 26112,
+    "de_2": 26624,
+    "pairs_4": 26624,
+}
+U_BANKS = (1, 2, 3, 4)
 
 FLOPS = 2 * 2 * K * K * SAMPLES
 BYTES = 4 * (4 * K * K + K + SAMPLES) + 2 * P * SAMPLES // 16 + 4 * K * ITEMS + K * ITEMS + 16 * ITEMS
@@ -65,7 +80,7 @@ def tile_attend_gbpool_E_pl_kernel(tc, xT, dz, cf, si, U, V, offs, out_0, out_1,
 
         def load_v(r):
             tile = buffer("v_raw_%d" % r, "v_raw_%d" % r, [P, K], F32)
-            nc.sync.dma_start(out=tile[:], in_=v_rows[LANES[r]])
+            nc.sync.dma_start(out=tile[:], in_=v_rows[r])
             return tile
 
         u_raw = [load_half("u_raw", U, 0), load_half("u_raw", U, 1)]
@@ -73,10 +88,10 @@ def tile_attend_gbpool_E_pl_kernel(tc, xT, dz, cf, si, U, V, offs, out_0, out_1,
         dz_sb = [load_half("dz", dz, 0)]
         v_raw = [load_v(0)]
         v_raw.append(load_v(1))
-        x_raw.append(load_half("x_raw", xT, 1))
-        dz_sb.append(load_half("dz", dz, 1))
         offsets = sb.tile([P, SAMPLES // 16], U16, name="offsets")
         nc.sync.dma_start(offsets[:], offs)
+        x_raw.append(load_half("x_raw", xT, 1))
+        dz_sb.append(load_half("dz", dz, 1))
         v_raw.extend([load_v(2), load_v(3)])
 
         ident = sb.tile([P, P], F32, name="ident")
@@ -92,29 +107,26 @@ def tile_attend_gbpool_E_pl_kernel(tc, xT, dz, cf, si, U, V, offs, out_0, out_1,
             channel_multiplier=1,
         )
 
-        dv_codes = buffer("dv_codes", "dv_codes", [P, HALF + SAMPLES], U32)
-        dv_scales = buffer("dv_scales", "dv_scales", [P, HALF + SAMPLES], U8)
-        windows = [buffer("window_%d" % r, "window_%d" % r, [P, ITEMS], F32) for r in range(2)]
-        nc.vector.memset(dv_codes[:, 0:HALF], 0)
-        nc.vector.memset(dv_scales[:, 0:HALF], 0)
-        for window in windows:
-            nc.vector.memset(window[:], 0.0)
+        dv_codes = buffer("dv_codes", "dv_codes", [P, SAMPLES], U32)
+        dv_scales = buffer("dv_scales", "dv_scales", [P, SAMPLES], U8)
+        windows = {}
+
+        def clear(r, engine):
+            windows[r] = buffer("window_%d" % r, "window_%d" % r, [P, ITEMS], F32)
+            engine.memset(windows[r][:], 0.0)
+
+        clear(0, nc.vector)
+        clear(2, nc.vector)
 
         si_ps = bank(0, "si_ps")
         for j in range(PACK):
             nc.tensor.transpose(si_ps[:, j * P : (j + 1) * P], si_sb[:, j : j + 1].to_broadcast([P, P]), ident[:])
         si_rows = si_ps[:].rearrange("p (j n) -> p n j", j=PACK)
-        si_all = buffer("si_all", "si_all", [P, HALF], F32)
-        nc.scalar.copy(out=si_all[:].rearrange("p (n j) -> p n j", j=PACK), in_=si_rows[:, 0 : HALF // PACK, :])
-        si_third = buffer("si_third", "si_third", [P, P], F32)
-        nc.scalar.copy(out=si_third[:].rearrange("p (n j) -> p n j", j=PACK), in_=si_rows[:, 2 * P // PACK : 3 * P // PACK, :])
-        cs = buffer("cs", "cs", [P, PACK, P], F32)
-        for t in range(PACK):
-            nc.scalar.activation(
-                out=cs[:, t, :].rearrange("p (n j) -> p n j", j=PACK),
-                in_=si_rows[:, 3 * P // PACK : SAMPLES // PACK, :],
-                func=COPY,
-                scale=cf_sb[:, t : t + 1],
+        si_all = [buffer("si_all_%d" % h, "si_all_%d" % h, [P, HALF], F32) for h in range(2)]
+        for h in range(2):
+            nc.scalar.copy(
+                out=si_all[h][:].rearrange("p (n j) -> p n j", j=PACK),
+                in_=si_rows[:, h * HALF // PACK : (h + 1) * HALF // PACK, :],
             )
 
         u_codes = buffer("u_codes", "u_codes", [P, K], U32)
@@ -136,21 +148,14 @@ def tile_attend_gbpool_E_pl_kernel(tc, xT, dz, cf, si, U, V, offs, out_0, out_1,
         v_codes = []
         v_scales = buffer("v_scales", "v_scales", [P, K], U8)
 
-        def round_v(r, rounded, first):
-            count = rounded.shape[1] // (2 * P)
-            nc.scalar.copy(
-                out=rounded.rearrange("s (u p e) -> s u p e", u=count, e=2),
-                in_=v_raw[r][:].rearrange("s (p u e) -> s u p e", u=2, e=2)[:, first : first + count],
-            )
-            return [rounded.bitcast(F32)[:, u * P : (u + 1) * P] for u in range(count)]
-
-        def turn_v(r, words):
+        def turn_v(r):
             turned = bank(5 + r % 2, "v_turned_%d" % r)
-            for u in range(2):
-                nc.tensor.transpose(turned[:, u * P : (u + 1) * P], words[u], ident[:])
+            columns = v_raw[r][:].rearrange("s (p t) -> s t p", t=PACK)
+            for t in range(PACK):
+                nc.tensor.transpose(turned[:, t * P : (t + 1) * P], columns[:, t, :], ident[:])
             nc.scalar.copy(
-                out=v_bf[r][:].bitcast(F32).rearrange("p (s u) -> p s u", u=2),
-                in_=turned[:, 0 : 2 * P].rearrange("p (u s) -> p s u", u=2),
+                out=v_bf[r][:].rearrange("p (s t) -> p s t", t=PACK),
+                in_=turned[:].rearrange("p (t s) -> p s t", t=PACK),
             )
 
         def quantise_v(r, tag):
@@ -188,13 +193,13 @@ def tile_attend_gbpool_E_pl_kernel(tc, xT, dz, cf, si, U, V, offs, out_0, out_1,
                 )
             return u_ps
 
-        def g_on_vector(g, h, o, si_rows):
+        def make_g(g, h):
             for t in range(PACK):
                 nc.vector.scalar_tensor_tensor(
                     out=g[:, t, :],
-                    in0=dz_sb[h][:, t, o * P : (o + 1) * P],
+                    in0=dz_sb[h][:, t, :],
                     scalar=cf_sb[:, t : t + 1],
-                    in1=si_rows,
+                    in1=si_all[h][:],
                     op0=MULT,
                     op1=MULT,
                 )
@@ -208,116 +213,133 @@ def tile_attend_gbpool_E_pl_kernel(tc, xT, dz, cf, si, U, V, offs, out_0, out_1,
             )
 
         def quantise_dv(q):
-            cols = slice(HALF + q * P, HALF + (q + 1) * P)
+            cols = slice(q * P, (q + 1) * P)
             nc.vector.quantize_mx(out=dv_codes[:, cols].bitcast(E5M2), scales=dv_scales[:, cols], in_=dv_bf[q])
 
-        def product(r, number, first):
-            acc = bank(number, "de_ps_%d_%d" % (r, first))
+        def product(r, number, lo, hi):
+            acc = bank(number, "de_ps_%d_%d" % (r, lo))
             nc.tensor.matmul_mx(
-                out=acc[:],
+                out=acc[:, 0 : hi - lo],
                 lhsT=v_codes[r].bitcast(E4M3),
                 lhsT_scale=v_scales[:, r * P : (r + 1) * P],
-                rhs=dv_codes[:, first : first + SAMPLES].bitcast(E5M2),
-                rhs_scale=dv_scales[:, first : first + SAMPLES],
+                rhs=dv_codes[:, lo:hi].bitcast(E5M2),
+                rhs_scale=dv_scales[:, lo:hi],
                 start=True,
                 stop=True,
             )
-            return acc
+            return acc[:, 0 : hi - lo]
 
-        def copy_out(acc, lo, tag, name):
-            de = buffer(tag, name, [P, SAMPLES - lo], F32)
-            nc.scalar.copy(out=de[:], in_=acc[:, lo:SAMPLES])
-            return de
+        def copy_out(acc, tag, name):
+            de = buffer(tag, name, [P, acc.shape[1]], F32)
+            nc.scalar.copy(out=de[:], in_=acc)
+            return de[:]
 
-        def scatter(r, lo, hi, de):
-            nc.vector.tensor_copy(windows[r][:].indirect(offsets[:, lo // 16 : hi // 16]), de[:])
+        def scatter_vector(r, lo, hi, de):
+            nc.vector.tensor_copy(windows[r][:].indirect(offsets[:, lo // 16 : hi // 16]), de)
 
-        x_early = buffer("u_raw_1", "x_early", [P, HALF * PACK], BF16)
+        def scatter_scalar(r, lo, hi, de):
+            nc.scalar.activation(windows[r][:].indirect(offsets[:, lo // 16 : hi // 16]), de, COPY)
+
+        out_rows = out_0.rearrange("(s r) c -> r s c", r=PACK)
+
+        def store_plane(r):
+            nc.sync.dma_start(out=out_rows[r], in_=windows[r][:])
+
+        x_early = buffer("", "x_early", [P, HALF * PACK + PAD], BF16)
         x_bf = [x_early[:, o * P * PACK : (o + 1) * P * PACK] for o in range(2)]
         interleave_x(x_bf[0], 0, 0, nc.vector.tensor_copy)
         interleave_x(x_bf[1], 0, 1, nc.vector.tensor_copy)
         quantise_x(x_bf[0], 0, 0)
         quantise_x(x_bf[1], 0, 1)
+        clear(3, nc.gpsimd)
         u_ps = [make_u(0, 0), make_u(0, 1)]
         g = buffer("x_raw_0", "g_0", [P, PACK, HALF], F32)
-        for o in range(2):
-            g_on_vector(g[:, :, o * P : (o + 1) * P], 0, o, si_all[:, o * P : (o + 1) * P])
+        make_g(g, 0)
         for o in range(2):
             make_dv(u_ps[o], g[:, :, o * P : (o + 1) * P], 0, o)
-        words = [
-            round_v(r, buffer("", "v_rounded_%d_%d" % (r, u), [P, K // 2], BF16)[:], u)[0] for r in range(2) for u in range(2)
-        ]
         for r in range(2):
-            turn_v(r, words[2 * r : 2 * r + 2])
+            turn_v(r)
         quantise_dv(0)
         quantise_v(0, "v_codes_0")
         quantise_dv(1)
-        de_early = copy_out(product(0, 2, 0), HALF, "de_a0", "de_a0")
+        scatter_scalar(0, 0, HALF, copy_out(product(0, 7, 0, HALF), "de_0a", "de_0a"))
 
-        x_bf = [buffer(tag, "x_late_" + tag, [P, P * PACK], BF16)[:] for tag in ("x_raw_0", "dv_bf_0")]
+        x_bf = [
+            buffer("x_raw_0", "x_late_0", [P, P * PACK], BF16)[:],
+            buffer("", "x_late_1", [P, P * PACK + PAD], BF16)[:, 0 : P * PACK],
+        ]
         interleave_x(x_bf[0], 1, 0, nc.vector.tensor_copy)
         interleave_x(x_bf[1], 1, 1, nc.vector.tensor_copy)
         quantise_x(x_bf[0], 1, 0)
         quantise_x(x_bf[1], 1, 1)
         quantise_v(1, "v_codes_1")
+        clear(1, nc.gpsimd)
         u_ps = [make_u(1, 0), make_u(1, 1)]
-        early = product(1, 4, 0)
-        g_late = [buffer("x_raw_0", "g_2", [P, PACK, P], F32)[:]]
-        g_on_vector(g_late[0], 1, 0, si_third[:])
-        scatter(0, 0, HALF, de_early)
-        g_late.append(buffer("si_third", "g_3", [P, PACK, P], F32)[:])
-        nc.gpsimd.tensor_tensor(out=g_late[1], in0=dz_sb[1][:, :, P:HALF], in1=cs[:], op=MULT)
-        for r, tag in ((2, "dv_bf_0"), (3, "v_raw_2")):
-            rounded = buffer(tag, "v_rounded_%d" % r, [P, K], BF16)[:]
-            turn_v(r, round_v(r, rounded, 0))
+        early = product(1, 0, 0, HALF)
+        g = buffer("x_raw_0", "g_1", [P, PACK, HALF], F32)
+        make_g(g, 1)
+        for r in range(2, PACK):
+            turn_v(r)
         for o in range(2):
-            make_dv(u_ps[o], g_late[o], 1, o)
+            make_dv(u_ps[o], g[:, :, o * P : (o + 1) * P], 1, o)
         quantise_dv(2)
-        quantise_dv(3)
         quantise_v(2, "v_codes_2")
+        quantise_dv(3)
         quantise_v(3, "v_codes_3")
-        de_early = copy_out(early, HALF, "cs", "de_b0")
-        windows.append(buffer("v_bf_3", "window_2", [P, ITEMS], F32))
-        nc.gpsimd.memset(windows[2][:], 0.0)
-        windows.append(windows[0])
-        scatter(1, 0, HALF, de_early)
-        de = [
-            copy_out(product(r, number, HALF), lo, "de_%d" % r, "de_%d" % r)
-            for r, number, lo in ((0, 7, HALF), (1, 0, HALF), (2, 1, 0), (3, 2, 0))
-        ]
+        scatter_vector(1, 0, HALF, copy_out(early, "x_raw_0", "de_1a"))
+        de_0b = copy_out(product(0, 1, HALF, SAMPLES), "de_x", "de_0b")
+        de_1b = copy_out(product(1, 2, HALF, SAMPLES), "de_y", "de_1b")
+        scatter_scalar(0, HALF, SAMPLES, de_0b)
+        store_plane(0)
+        scatter_vector(1, HALF, SAMPLES, de_1b)
+        store_plane(1)
+        de_2 = copy_out(product(2, 3, 0, SAMPLES), "de_x", "de_2")
+        de_3 = copy_out(product(3, 4, 0, SAMPLES), "de_y", "de_3")
+        scatter_vector(2, 0, SAMPLES, de_2)
+        store_plane(2)
+        scatter_scalar(3, 0, HALF, de_3[:, 0:HALF])
+        scatter_scalar(3, HALF, SAMPLES, de_3[:, HALF:SAMPLES])
+        store_plane(3)
 
-        out_rows = out_0.rearrange("(s r) c -> r s c", r=PACK)
-        pairs = buffer("v_codes_3", "pairs", [P, ITEMS * PACK], BF16)
-        pair_view = pairs[:].rearrange("p (n a c l) -> p n a c l", a=2, c=CHUNK, l=2)
+        middle = CHUNKS - GPSIMD_CHUNKS - SCALAR_CHUNKS
+        groups = [(0, GPSIMD_CHUNKS, "pairs_low"), (GPSIMD_CHUNKS, middle, "de_x"), (GPSIMD_CHUNKS + middle, SCALAR_CHUNKS, "de_y")]
+        pairs = []
+        for first, count, tag in groups:
+            tile = buffer(tag, "pairs_%d" % first, [P, count * CHUNK * PACK], BF16)
+            pairs.extend((tile, n) for n in range(count))
 
         def round_plane(r, first, count, copy):
-            a, l = divmod(LANES[r], 2)
+            a, l = divmod(r, 2)
+            tile, n = pairs[first]
             copy(
-                out=pair_view[:, first : first + count, a, :, l],
+                out=tile[:].rearrange("p (n a c l) -> p n a c l", a=2, c=CHUNK, l=2)[:, n : n + count, a, :, l],
                 in_=windows[r][:].rearrange("p (n c) -> p n c", c=CHUNK)[:, first : first + count, :],
             )
 
         def gpsimd_round(out, in_):
             nc.gpsimd.tensor_scalar(out, in_, 1.0, -0.0, MULT, ADD)
 
+        for r in range(2):
+            round_plane(r, 0, GPSIMD_CHUNKS, gpsimd_round)
         for r in range(PACK):
-            scatter(r, HALF if r < 2 else 0, SAMPLES, de[r])
-            nc.sync.dma_start(out=out_rows[LANES[r]], in_=windows[r][:])
-            if r < PACK - 1:
-                round_plane(r, 0, CHUNKS - GPSIMD_ROUNDS, nc.scalar.copy)
-                round_plane(r, CHUNKS - GPSIMD_ROUNDS, GPSIMD_ROUNDS, gpsimd_round)
+            if r >= 2:
+                round_plane(r, 0, GPSIMD_CHUNKS, nc.vector.tensor_copy)
+            round_plane(r, GPSIMD_CHUNKS, middle, nc.vector.tensor_copy)
+        for n in range(CHUNKS - SCALAR_CHUNKS, CHUNKS):
+            for r in range(PACK):
+                round_plane(r, n, 1, nc.scalar.copy)
 
         y_bf = sb.tile([P, ITEMS * PACK], BF16, name="y_bf", align_bytes=64)
         y_codes = sb.tile([P, ITEMS], U32, name="y_codes", align_bytes=64)
         y_scales = sb.tile([P, ITEMS // PACK], U8, name="y_scales", align_bytes=64)
-        pair_words = pairs[:].bitcast(F32)
         y_words = y_bf[:].bitcast(F32)
         words_out = out_1[0].rearrange("p c l -> p (c l)").bitcast(I32)
 
         def weave(lo, hi):
             n = lo // CHUNK
             dst = y_words[:, 2 * lo : 2 * hi].rearrange("p (c i a) -> p c a i", i=4, a=2)
-            src = pair_words[:, 2 * n * CHUNK : 2 * (n + 1) * CHUNK].rearrange("p (a c i) -> p c a i", i=4, a=2)
+            tile, m = pairs[n]
+            src = tile[:].bitcast(F32)[:, 2 * m * CHUNK : 2 * (m + 1) * CHUNK].rearrange("p (a c i) -> p c a i", i=4, a=2)
             src = src[:, (lo - n * CHUNK) // 4 : (hi - n * CHUNK) // 4]
             if n >= CHUNKS - SCALAR_WEAVES:
                 nc.scalar.copy(out=dst, in_=src)
@@ -335,8 +357,6 @@ def tile_attend_gbpool_E_pl_kernel(tc, xT, dz, cf, si, U, V, offs, out_0, out_1,
                 first = STORE_ENDS[STORE_ENDS.index(hi) - 1]
                 nc.sync.dma_start(out=words_out[:, first:hi], in_=y_codes[:, first:hi].bitcast(I32))
 
-        for n in range(CHUNKS):
-            round_plane(PACK - 1, n, 1, nc.vector.tensor_copy if n < VECTOR_ROUNDS else nc.scalar.copy)
         edges = list(range(0, ITEMS, CHUNK)) + [ITEMS - CHUNK // 2, ITEMS]
         pieces = list(zip(edges[:-1], edges[1:]))
         for n, piece in enumerate(pieces):

@@ -26,18 +26,24 @@ SCALAR_WEAVES = 1
 U_VECTOR = 44
 GPSIMD_CHUNKS = 4
 SCALAR_CHUNKS = 3
-PAD = 32
 STORE_ENDS = [0, 2 * CHUNK, 4 * CHUNK, 6 * CHUNK, ITEMS - CHUNK // 2, ITEMS]
 PLACES = {
     "u_raw_1": 0,
     "x_early": 0,
-    "window_3": 2048,
     "si_sb": 10240,
     "x_codes_0": 10240,
     "x_codes_1": 10752,
     "dv_bf_0": 11264,
     "x_late_1": 11264,
-    "window_1": 12288,
+    "v_bf_3": 12288,
+    "x_raw_0": 28672,
+    "g_0": 28672,
+    "x_late_0": 28672,
+    "g_1": 28672,
+    "de_1a": 28672,
+    "v_codes_2": 29696,
+    "v_codes_3": 30208,
+    "window_3": 12288,
     "pairs_5": 20480,
     "de_3": 24576,
     "de_0b": 26112,
@@ -115,8 +121,8 @@ def tile_attend_gbpool_E_pl_kernel(tc, xT, dz, cf, si, U, V, offs, out_0, out_1,
             windows[r] = buffer("window_%d" % r, "window_%d" % r, [P, ITEMS], F32)
             engine.memset(windows[r][:], 0.0)
 
-        clear(0, nc.vector)
-        clear(2, nc.vector)
+        for r in range(PACK - 1):
+            clear(r, nc.vector)
 
         si_ps = bank(0, "si_ps")
         for j in range(PACK):
@@ -245,15 +251,14 @@ def tile_attend_gbpool_E_pl_kernel(tc, xT, dz, cf, si, U, V, offs, out_0, out_1,
         def store_plane(r):
             nc.sync.dma_start(out=out_rows[r], in_=windows[r][:])
 
-        x_early = buffer("", "x_early", [P, HALF * PACK + PAD], BF16)
+        x_early = buffer("", "x_early", [P, HALF * PACK], BF16)
         x_bf = [x_early[:, o * P * PACK : (o + 1) * P * PACK] for o in range(2)]
         interleave_x(x_bf[0], 0, 0, nc.vector.tensor_copy)
         interleave_x(x_bf[1], 0, 1, nc.vector.tensor_copy)
         quantise_x(x_bf[0], 0, 0)
         quantise_x(x_bf[1], 0, 1)
-        clear(3, nc.gpsimd)
         u_ps = [make_u(0, 0), make_u(0, 1)]
-        g = buffer("x_raw_0", "g_0", [P, PACK, HALF], F32)
+        g = buffer("", "g_0", [P, PACK, HALF], F32)
         make_g(g, 0)
         for o in range(2):
             make_dv(u_ps[o], g[:, :, o * P : (o + 1) * P], 0, o)
@@ -265,18 +270,17 @@ def tile_attend_gbpool_E_pl_kernel(tc, xT, dz, cf, si, U, V, offs, out_0, out_1,
         scatter_scalar(0, 0, HALF, copy_out(product(0, 7, 0, HALF), "de_0a", "de_0a"))
 
         x_bf = [
-            buffer("x_raw_0", "x_late_0", [P, P * PACK], BF16)[:],
-            buffer("", "x_late_1", [P, P * PACK + PAD], BF16)[:, 0 : P * PACK],
+            buffer("", "x_late_0", [P, P * PACK], BF16)[:],
+            buffer("", "x_late_1", [P, P * PACK], BF16)[:],
         ]
         interleave_x(x_bf[0], 1, 0, nc.vector.tensor_copy)
         interleave_x(x_bf[1], 1, 1, nc.vector.tensor_copy)
         quantise_x(x_bf[0], 1, 0)
         quantise_x(x_bf[1], 1, 1)
         quantise_v(1, "v_codes_1")
-        clear(1, nc.gpsimd)
         u_ps = [make_u(1, 0), make_u(1, 1)]
         early = product(1, 0, 0, HALF)
-        g = buffer("x_raw_0", "g_1", [P, PACK, HALF], F32)
+        g = buffer("", "g_1", [P, PACK, HALF], F32)
         make_g(g, 1)
         for r in range(2, PACK):
             turn_v(r)
@@ -286,6 +290,7 @@ def tile_attend_gbpool_E_pl_kernel(tc, xT, dz, cf, si, U, V, offs, out_0, out_1,
         quantise_v(2, "v_codes_2")
         quantise_dv(3)
         quantise_v(3, "v_codes_3")
+        clear(3, nc.gpsimd)
         scatter_vector(1, 0, HALF, copy_out(early, "x_raw_0", "de_1a"))
         de_0b = copy_out(product(0, 1, HALF, SAMPLES), "de_x", "de_0b")
         de_1b = copy_out(product(1, 2, HALF, SAMPLES), "de_y", "de_1b")

@@ -22,35 +22,48 @@ ITEMS = 2048
 HALF = SAMPLES // 2
 CHUNK = 256
 CHUNKS = ITEMS // CHUNK
-SCALAR_WEAVES = 1
 U_VECTOR = 44
-GPSIMD_CHUNKS = 4
-SCALAR_CHUNKS = 3
+GPSIMD_TO = 4 * CHUNK
+TURNED_FROM = GPSIMD_TO + CHUNK
+TURNED_EDGES = list(range(TURNED_FROM, ITEMS + 1, CHUNK))
+PAIR_BANKS = ((0, 5, 6), (1, 2, 7))
+LAG = 2
 STORE_ENDS = [0, 2 * CHUNK, 4 * CHUNK, 6 * CHUNK, ITEMS - CHUNK // 2, ITEMS]
 PLACES = {
-    "u_raw_1": 0,
-    "x_early": 0,
-    "si_sb": 10240,
-    "x_codes_0": 10240,
-    "x_codes_1": 10752,
-    "dv_bf_0": 11264,
-    "x_late_1": 11264,
-    "v_bf_3": 12288,
-    "x_raw_0": 28672,
-    "g_0": 28672,
-    "x_late_0": 28672,
-    "g_1": 28672,
+    "window_3": 0,
+    "x_early": 8128,
+    "u_raw_1": 8192,
+    "v_rounded_0_0": 8192,
+    "v_rounded_0_1": 8704,
+    "v_rounded_1_0": 9216,
+    "v_rounded_1_1": 9728,
+    "v_rounded_2": 14336,
+    "dv_bf_0": 14848,
+    "x_late_1": 14848,
+    "v_rounded_3": 15360,
+    "v_raw_3": 28672,
     "de_1a": 28672,
-    "v_codes_2": 29696,
-    "v_codes_3": 30208,
-    "window_3": 12288,
-    "pairs_5": 20480,
-    "de_3": 24576,
-    "de_0b": 26112,
-    "de_2": 26624,
-    "pairs_4": 26624,
+    "si_sb": 12288,
+    "x_codes_0": 12288,
+    "x_codes_1": 12800,
+    "dv_bf_1": 13312,
+    "v_codes_1": 13312,
+    "z_0_0": 16384,
+    "de_3": 17344,
+    "z_0_1": 17408,
+    "z_0_2": 18432,
+    "de_2": 19456,
+    "pairs_1": 19456,
+    "x_raw_0": 24576,
+    "g_0": 24576,
+    "x_late_0": 24576,
+    "g_1": 24576,
+    "v_codes_2": 24576,
+    "v_codes_3": 25088,
 }
+PAD = 32
 U_BANKS = (1, 2, 3, 4)
+V_BANKS = (5, 6, 6, 1)
 
 FLOPS = 2 * 2 * K * K * SAMPLES
 BYTES = 4 * (4 * K * K + K + SAMPLES) + 2 * P * SAMPLES // 16 + 4 * K * ITEMS + K * ITEMS + 16 * ITEMS
@@ -125,43 +138,48 @@ def tile_attend_gbpool_E_pl_kernel(tc, xT, dz, cf, si, U, V, offs, out_0, out_1,
             clear(r, nc.vector)
 
         si_ps = bank(0, "si_ps")
+        si_columns = si_ps[:].rearrange("p (n j) -> p j n", j=PACK)
         for j in range(PACK):
-            nc.tensor.transpose(si_ps[:, j * P : (j + 1) * P], si_sb[:, j : j + 1].to_broadcast([P, P]), ident[:])
-        si_rows = si_ps[:].rearrange("p (j n) -> p n j", j=PACK)
-        si_all = [buffer("si_all_%d" % h, "si_all_%d" % h, [P, HALF], F32) for h in range(2)]
-        for h in range(2):
-            nc.scalar.copy(
-                out=si_all[h][:].rearrange("p (n j) -> p n j", j=PACK),
-                in_=si_rows[:, h * HALF // PACK : (h + 1) * HALF // PACK, :],
-            )
+            nc.tensor.transpose(si_columns[:, j, :], si_sb[:, j : j + 1].to_broadcast([P, P]), ident[:])
 
         u_codes = buffer("u_codes", "u_codes", [P, K], U32)
         u_scales = buffer("u_scales", "u_scales", [P, K], U8)
+        u_bf = [buffer("u_bf_%d" % h, "u_bf_%d" % h, [P, PACK, P // 2 * PACK], BF16) for h in range(2)]
         for h in range(2):
-            u_bf = buffer("u_bf_%d" % h, "u_bf_%d" % h, [P, PACK, P // 2 * PACK], BF16)
-            u_dst = u_bf[:].rearrange("p t (m j) -> p m j t", j=PACK)
+            u_dst = u_bf[h][:].rearrange("p t (m j) -> p m j t", j=PACK)
             u_src = u_raw[h][:].rearrange("p j (m t) -> p m j t", t=PACK)
             if h == 0:
                 nc.vector.tensor_copy(out=u_dst, in_=u_src)
             else:
                 nc.vector.tensor_copy(out=u_dst[:, 0:U_VECTOR], in_=u_src[:, 0:U_VECTOR])
                 nc.scalar.copy(out=u_dst[:, U_VECTOR : P // 2], in_=u_src[:, U_VECTOR : P // 2])
+        for h in range(2):
             for t in range(PACK):
                 cols = slice(t * P + h * P // 2, t * P + (h + 1) * P // 2)
-                nc.vector.quantize_mx(out=u_codes[:, cols].bitcast(E4M3), scales=u_scales[:, cols], in_=u_bf[:, t, :])
+                nc.vector.quantize_mx(out=u_codes[:, cols].bitcast(E4M3), scales=u_scales[:, cols], in_=u_bf[h][:, t, :])
 
         v_bf = [buffer("v_bf_%d" % r, "v_bf_%d" % r, [P, K], BF16) for r in range(PACK)]
         v_codes = []
         v_scales = buffer("v_scales", "v_scales", [P, K], U8)
 
-        def turn_v(r):
-            turned = bank(5 + r % 2, "v_turned_%d" % r)
-            columns = v_raw[r][:].rearrange("s (p t) -> s t p", t=PACK)
-            for t in range(PACK):
-                nc.tensor.transpose(turned[:, t * P : (t + 1) * P], columns[:, t, :], ident[:])
+        def gpsimd_round(out, in_):
+            nc.gpsimd.tensor_scalar(out, in_, 1.0, -0.0, MULT, ADD)
+
+        def round_v(r, rounded, first, copy):
+            count = rounded.shape[1] // (2 * P)
+            copy(
+                out=rounded.rearrange("s (u p e) -> s u p e", u=count, e=2),
+                in_=v_raw[r][:].rearrange("s (p u e) -> s u p e", u=2, e=2)[:, first : first + count],
+            )
+            return [rounded.bitcast(F32)[:, u * P : (u + 1) * P] for u in range(count)]
+
+        def turn_v(r, words):
+            turned = bank(V_BANKS[r], "v_turned_%d" % r)
+            for u in range(2):
+                nc.tensor.transpose(turned[:, u * P : (u + 1) * P], words[u], ident[:])
             nc.scalar.copy(
-                out=v_bf[r][:].rearrange("p (s t) -> p s t", t=PACK),
-                in_=turned[:].rearrange("p (t s) -> p s t", t=PACK),
+                out=v_bf[r][:].bitcast(F32).rearrange("p (s u) -> p s u", u=2),
+                in_=turned[:, 0 : 2 * P].rearrange("p (u s) -> p s u", u=2),
             )
 
         def quantise_v(r, tag):
@@ -200,12 +218,13 @@ def tile_attend_gbpool_E_pl_kernel(tc, xT, dz, cf, si, U, V, offs, out_0, out_1,
             return u_ps
 
         def make_g(g, h):
-            for t in range(PACK):
+            steps = [(t, 0, HALF) for t in range(2)] + [(t, lo, lo + P) for lo in (0, P) for t in range(2, PACK)]
+            for t, lo, hi in steps:
                 nc.vector.scalar_tensor_tensor(
-                    out=g[:, t, :],
-                    in0=dz_sb[h][:, t, :],
+                    out=g[:, t, lo:hi],
+                    in0=dz_sb[h][:, t, lo:hi],
                     scalar=cf_sb[:, t : t + 1],
-                    in1=si_all[h][:],
+                    in1=si_ps[:, h * HALF + lo : h * HALF + hi],
                     op0=MULT,
                     op1=MULT,
                 )
@@ -235,9 +254,9 @@ def tile_attend_gbpool_E_pl_kernel(tc, xT, dz, cf, si, U, V, offs, out_0, out_1,
             )
             return acc[:, 0 : hi - lo]
 
-        def copy_out(acc, tag, name):
+        def copy_out(acc, tag, name, copy=nc.scalar.copy):
             de = buffer(tag, name, [P, acc.shape[1]], F32)
-            nc.scalar.copy(out=de[:], in_=acc)
+            copy(out=de[:], in_=acc)
             return de[:]
 
         def scatter_vector(r, lo, hi, de):
@@ -251,22 +270,28 @@ def tile_attend_gbpool_E_pl_kernel(tc, xT, dz, cf, si, U, V, offs, out_0, out_1,
         def store_plane(r):
             nc.sync.dma_start(out=out_rows[r], in_=windows[r][:])
 
-        x_early = buffer("", "x_early", [P, HALF * PACK], BF16)
-        x_bf = [x_early[:, o * P * PACK : (o + 1) * P * PACK] for o in range(2)]
+        x_early = buffer("", "x_early", [P, PAD + HALF * PACK], BF16)
+        x_bf = [x_early[:, PAD + o * P * PACK : PAD + (o + 1) * P * PACK] for o in range(2)]
         interleave_x(x_bf[0], 0, 0, nc.vector.tensor_copy)
         interleave_x(x_bf[1], 0, 1, nc.vector.tensor_copy)
         quantise_x(x_bf[0], 0, 0)
         quantise_x(x_bf[1], 0, 1)
+        clear(3, nc.gpsimd)
         u_ps = [make_u(0, 0), make_u(0, 1)]
         g = buffer("", "g_0", [P, PACK, HALF], F32)
         make_g(g, 0)
         for o in range(2):
             make_dv(u_ps[o], g[:, :, o * P : (o + 1) * P], 0, o)
+        words = [
+            round_v(r, buffer("", "v_rounded_%d_%d" % (r, u), [P, K // 2], BF16)[:], u, nc.scalar.copy)[0]
+            for r in range(2)
+            for u in range(2)
+        ]
         for r in range(2):
-            turn_v(r)
+            turn_v(r, words[2 * r : 2 * r + 2])
         quantise_dv(0)
-        quantise_v(0, "v_codes_0")
         quantise_dv(1)
+        quantise_v(0, "v_codes_0")
         scatter_scalar(0, 0, HALF, copy_out(product(0, 7, 0, HALF), "de_0a", "de_0a"))
 
         x_bf = [
@@ -276,80 +301,44 @@ def tile_attend_gbpool_E_pl_kernel(tc, xT, dz, cf, si, U, V, offs, out_0, out_1,
         interleave_x(x_bf[0], 1, 0, nc.vector.tensor_copy)
         interleave_x(x_bf[1], 1, 1, nc.vector.tensor_copy)
         quantise_x(x_bf[0], 1, 0)
+        quantise_v(1, "")
         quantise_x(x_bf[1], 1, 1)
-        quantise_v(1, "v_codes_1")
         u_ps = [make_u(1, 0), make_u(1, 1)]
-        early = product(1, 0, 0, HALF)
+        early = product(1, 5, 0, HALF)
         g = buffer("", "g_1", [P, PACK, HALF], F32)
         make_g(g, 1)
         for r in range(2, PACK):
-            turn_v(r)
+            rounded = buffer("", "v_rounded_%d" % r, [P, K], BF16)[:]
+            turn_v(r, round_v(r, rounded, 0, gpsimd_round))
+        scatter_scalar(1, 0, HALF, copy_out(early, "", "de_1a"))
         for o in range(2):
             make_dv(u_ps[o], g[:, :, o * P : (o + 1) * P], 1, o)
         quantise_dv(2)
-        quantise_v(2, "v_codes_2")
+        quantise_v(2, "")
         quantise_dv(3)
-        quantise_v(3, "v_codes_3")
-        clear(3, nc.gpsimd)
-        scatter_vector(1, 0, HALF, copy_out(early, "x_raw_0", "de_1a"))
-        de_0b = copy_out(product(0, 1, HALF, SAMPLES), "de_x", "de_0b")
-        de_1b = copy_out(product(1, 2, HALF, SAMPLES), "de_y", "de_1b")
-        scatter_scalar(0, HALF, SAMPLES, de_0b)
+        quantise_v(3, "")
+        de_0b = buffer("de_0b", "de_0b", [P, HALF], F32)
+        for o, number in enumerate((2, 0)):
+            nc.vector.tensor_copy(out=de_0b[:, o * P : (o + 1) * P], in_=product(0, number, HALF + o * P, HALF + (o + 1) * P))
+        de_1b = copy_out(product(1, 7, HALF, SAMPLES), "de_1b", "de_1b", nc.vector.tensor_copy)
+        scatter_vector(0, HALF, SAMPLES, de_0b[:])
         store_plane(0)
+        de_2 = copy_out(product(2, 3, 0, SAMPLES), "", "de_2")
+        de_3 = copy_out(product(3, 4, 0, SAMPLES), "", "de_3")
         scatter_vector(1, HALF, SAMPLES, de_1b)
         store_plane(1)
-        de_2 = copy_out(product(2, 3, 0, SAMPLES), "de_x", "de_2")
-        de_3 = copy_out(product(3, 4, 0, SAMPLES), "de_y", "de_3")
-        scatter_vector(2, 0, SAMPLES, de_2)
+        scatter_scalar(2, 0, HALF, de_2[:, 0:HALF])
+        scatter_vector(2, HALF, SAMPLES, de_2[:, HALF:SAMPLES])
         store_plane(2)
         scatter_scalar(3, 0, HALF, de_3[:, 0:HALF])
         scatter_scalar(3, HALF, SAMPLES, de_3[:, HALF:SAMPLES])
         store_plane(3)
-
-        middle = CHUNKS - GPSIMD_CHUNKS - SCALAR_CHUNKS
-        groups = [(0, GPSIMD_CHUNKS, "pairs_low"), (GPSIMD_CHUNKS, middle, "de_x"), (GPSIMD_CHUNKS + middle, SCALAR_CHUNKS, "de_y")]
-        pairs = []
-        for first, count, tag in groups:
-            tile = buffer(tag, "pairs_%d" % first, [P, count * CHUNK * PACK], BF16)
-            pairs.extend((tile, n) for n in range(count))
-
-        def round_plane(r, first, count, copy):
-            a, l = divmod(r, 2)
-            tile, n = pairs[first]
-            copy(
-                out=tile[:].rearrange("p (n a c l) -> p n a c l", a=2, c=CHUNK, l=2)[:, n : n + count, a, :, l],
-                in_=windows[r][:].rearrange("p (n c) -> p n c", c=CHUNK)[:, first : first + count, :],
-            )
-
-        def gpsimd_round(out, in_):
-            nc.gpsimd.tensor_scalar(out, in_, 1.0, -0.0, MULT, ADD)
-
-        for r in range(2):
-            round_plane(r, 0, GPSIMD_CHUNKS, gpsimd_round)
-        for r in range(PACK):
-            if r >= 2:
-                round_plane(r, 0, GPSIMD_CHUNKS, nc.vector.tensor_copy)
-            round_plane(r, GPSIMD_CHUNKS, middle, nc.vector.tensor_copy)
-        for n in range(CHUNKS - SCALAR_CHUNKS, CHUNKS):
-            for r in range(PACK):
-                round_plane(r, n, 1, nc.scalar.copy)
 
         y_bf = sb.tile([P, ITEMS * PACK], BF16, name="y_bf", align_bytes=64)
         y_codes = sb.tile([P, ITEMS], U32, name="y_codes", align_bytes=64)
         y_scales = sb.tile([P, ITEMS // PACK], U8, name="y_scales", align_bytes=64)
         y_words = y_bf[:].bitcast(F32)
         words_out = out_1[0].rearrange("p c l -> p (c l)").bitcast(I32)
-
-        def weave(lo, hi):
-            n = lo // CHUNK
-            dst = y_words[:, 2 * lo : 2 * hi].rearrange("p (c i a) -> p c a i", i=4, a=2)
-            tile, m = pairs[n]
-            src = tile[:].bitcast(F32)[:, 2 * m * CHUNK : 2 * (m + 1) * CHUNK].rearrange("p (a c i) -> p c a i", i=4, a=2)
-            src = src[:, (lo - n * CHUNK) // 4 : (hi - n * CHUNK) // 4]
-            if n >= CHUNKS - SCALAR_WEAVES:
-                nc.scalar.copy(out=dst, in_=src)
-            else:
-                nc.vector.tensor_copy(out=dst, in_=src)
 
         def quantise_y(lo, hi):
             group, column = divmod(lo, ITEMS // PACK)
@@ -362,13 +351,88 @@ def tile_attend_gbpool_E_pl_kernel(tc, xT, dz, cf, si, U, V, offs, out_0, out_1,
                 first = STORE_ENDS[STORE_ENDS.index(hi) - 1]
                 nc.sync.dma_start(out=words_out[:, first:hi], in_=y_codes[:, first:hi].bitcast(I32))
 
-        edges = list(range(0, ITEMS, CHUNK)) + [ITEMS - CHUNK // 2, ITEMS]
-        pieces = list(zip(edges[:-1], edges[1:]))
-        for n, piece in enumerate(pieces):
+        spans = [(0, GPSIMD_TO, CHUNK), (GPSIMD_TO, TURNED_FROM, TURNED_FROM - GPSIMD_TO)]
+        pairs = [buffer("pairs_%d" % n, "pairs_%d" % n, [P, (hi - lo) * PACK], BF16) for n, (lo, hi, width) in enumerate(spans)]
+
+        def round_plane(r, n, copy):
+            a, l = divmod(r, 2)
+            lo, hi, width = spans[n]
+            copy(
+                out=pairs[n][:].rearrange("p (n a c l) -> p n a c l", a=2, c=width, l=2)[:, :, a, :, l],
+                in_=windows[r][:, lo:hi].rearrange("p (n c) -> p n c", c=width),
+            )
+
+        def weave(n, lo, hi):
+            first = lo - spans[n][0]
+            nc.vector.tensor_copy(
+                out=y_words[:, 2 * lo : 2 * hi].rearrange("p (c i a) -> p c a i", i=4, a=2),
+                in_=pairs[n][:].bitcast(F32)[:, 2 * first : 2 * (first + hi - lo)].rearrange("p (a c i) -> p c a i", i=4, a=2),
+            )
+
+        for r in range(2):
+            round_plane(r, 0, gpsimd_round)
+        for r in range(PACK):
+            if r >= 2:
+                round_plane(r, 0, nc.vector.tensor_copy)
+            round_plane(r, 1, nc.vector.tensor_copy)
+
+        pieces = list(zip(TURNED_EDGES[:-1], TURNED_EDGES[1:]))
+
+        def turn_pair(a, n):
+            lo, hi = pieces[n]
+            turned = bank(PAIR_BANKS[a][n], "pair_%d_%d" % (a, n))
+            for b in range((hi - lo) // P):
+                for l in range(2):
+                    nc.tensor.transpose(
+                        turned[:, (2 * b + l) * P : (2 * b + l + 1) * P],
+                        windows[2 * a + l][:, lo + b * P : lo + (b + 1) * P],
+                        ident[:],
+                    )
+            return turned[:, 0 : 2 * (hi - lo)]
+
+        def round_pair(a, n, turned):
+            lo, hi = pieces[n]
+            z = buffer("z_%d_%d" % (a, n), "z_%d_%d" % (a, n), [P, 2 * (hi - lo)], BF16)
+            nc.scalar.copy(
+                out=z[:].rearrange("c (b p l) -> c b p l", p=P, l=2),
+                in_=turned.rearrange("c (b l p) -> c b p l", p=P, l=2),
+            )
+            return z[:].bitcast(F32)
+
+        def turn_back(a, n, z, back):
+            lo, hi = pieces[n]
+            for b in range((hi - lo) // P):
+                nc.tensor.transpose(back[:, (2 * b + a) * P : (2 * b + a + 1) * P], z[:, b * P : (b + 1) * P], ident[:])
+
+        def weave_out(back, first, lo, hi):
+            nc.scalar.copy(
+                out=y_words[:, 2 * lo : 2 * hi].rearrange("p (b c a) -> p b c a", c=P, a=2),
+                in_=back[:, 2 * (lo - first) : 2 * (hi - first)].rearrange("p (b a c) -> p b c a", c=P, a=2),
+            )
+
+        turned = [[turn_pair(a, n) for n in range(len(pieces))] for a in range(2)]
+        low = [round_pair(0, n, turned[0][n]) for n in range(len(pieces))]
+        backs = []
+        for n in range(len(pieces) + LAG):
+            if n < len(pieces):
+                high = round_pair(1, n, turned[1][n])
+                backs.append(bank(PAIR_BANKS[0][n], "back_%d" % n))
+                turn_back(0, n, low[n], backs[n])
+                turn_back(1, n, high, backs[n])
+            if n >= LAG:
+                lo, hi = pieces[n - LAG]
+                cuts = [lo, hi] if hi < ITEMS else [lo, hi - P, hi]
+                for cut_lo, cut_hi in zip(cuts[:-1], cuts[1:]):
+                    weave_out(backs[n - LAG], lo, cut_lo, cut_hi)
+
+        woven = [(0, lo, lo + CHUNK) for lo in range(0, GPSIMD_TO, CHUNK)] + [(1, GPSIMD_TO, TURNED_FROM)]
+        for n, piece in enumerate(woven):
             weave(*piece)
             if n >= 1:
-                quantise_y(*pieces[n - 1])
-        quantise_y(*pieces[-1])
+                quantise_y(*woven[n - 1][1:])
+        quantise_y(*woven[-1][1:])
+        for lo, hi in pieces[:-1] + [(ITEMS - CHUNK, ITEMS - P), (ITEMS - P, ITEMS)]:
+            quantise_y(lo, hi)
 
         scales_out = out_2[0].bitcast(I32).rearrange("(q j) (g c) -> q g j c", j=4, g=4)
         for quad in range(4):

from contextlib import ExitStack

import concourse.mybir as mybir

F32 = mybir.dt.float32
BF16 = mybir.dt.bfloat16
I32 = mybir.dt.int32
U32 = mybir.dt.uint32
U16 = mybir.dt.uint16
U8 = mybir.dt.uint8
E4M3 = mybir.dt.float8_e4m3fn_x4
E5M2 = mybir.dt.float8_e5m2_x4
MULT = mybir.AluOpType.mult
ADD = mybir.AluOpType.add
COPY = mybir.ActivationFunctionType.Copy

P = 128
PACK = 4
K = 512
SAMPLES = 512
ITEMS = 2048
HALF = SAMPLES // 2
CHUNK = 256
CHUNKS = ITEMS // CHUNK
U_VECTOR = 44
GPSIMD_TO = 4 * CHUNK
TURNED_FROM = GPSIMD_TO + CHUNK
TURNED_EDGES = list(range(TURNED_FROM, ITEMS + 1, CHUNK))
PAIR_BANKS = ((0, 5, 6), (1, 2, 7))
LAG = 2
STORE_ENDS = [0, 2 * CHUNK, 4 * CHUNK, 6 * CHUNK, ITEMS - CHUNK // 2, ITEMS]
PLACES = {
    "window_3": 0,
    "x_early": 8128,
    "u_raw_1": 8192,
    "v_rounded_0_0": 8192,
    "v_rounded_0_1": 8704,
    "v_rounded_1_0": 9216,
    "v_rounded_1_1": 9728,
    "v_rounded_2": 14336,
    "dv_bf_0": 14848,
    "x_late_1": 14848,
    "v_rounded_3": 15360,
    "v_raw_3": 28672,
    "de_1a": 28672,
    "si_sb": 12288,
    "x_codes_0": 12288,
    "x_codes_1": 12800,
    "dv_bf_1": 13312,
    "v_codes_1": 13312,
    "z_0_0": 16384,
    "de_3": 17344,
    "z_0_1": 17408,
    "z_0_2": 18432,
    "de_2": 19456,
    "pairs_1": 19456,
    "x_raw_0": 24576,
    "g_0": 24576,
    "x_late_0": 24576,
    "g_1": 24576,
    "v_codes_2": 24576,
    "v_codes_3": 25088,
}
PAD = 32
U_BANKS = (1, 2, 3, 4)
V_BANKS = (5, 6, 6, 1)

FLOPS = 2 * 2 * K * K * SAMPLES
BYTES = 4 * (4 * K * K + K + SAMPLES) + 2 * P * SAMPLES // 16 + 4 * K * ITEMS + K * ITEMS + 16 * ITEMS


def tile_attend_gbpool_E_pl_kernel(tc, xT, dz, cf, si, U, V, offs, out_0, out_1, out_2):
    nc = tc.nc
    with ExitStack() as ctx:
        sb = ctx.enter_context(tc.tile_pool(name="sb", bufs=1))
        shared = ctx.enter_context(tc.tile_pool(name="shared", bufs=1))
        ps = ctx.enter_context(tc.psum_pool(name="ps", bufs=1))

        def bank(number, name):
            return ps.tile([P, 512], F32, tag="bank_%d" % number, name=name)

        def buffer(tag, name, shape, dtype):
            if name in PLACES:
                return shared.tile(shape, dtype, name=name, align_bytes=64, offset=PLACES[name])
            return sb.tile(shape, dtype, tag=tag, name=name, align_bytes=64)

        si_sb = buffer("si_sb", "si_sb", [P, HALF], F32)
        nc.scalar.dma_start(out=si_sb[:, 0:PACK], in_=si[0:1, :].rearrange("o (n j) -> (o n) j", j=PACK))
        cf_sb = sb.tile([P, PACK], F32, name="cf_sb")
        nc.scalar.dma_start(out=cf_sb[:], in_=cf.rearrange("(p t) o -> p (t o)", t=PACK))

        def load_half(name, source, h):
            tile = buffer("%s_%d" % (name, h), "%s_%d" % (name, h), [P, PACK, HALF], F32)
            rows = source.rearrange("(p j) c -> p j c", j=PACK)
            nc.sync.dma_start(out=tile[:], in_=rows[:, :, h * HALF : (h + 1) * HALF])
            return tile

        v_rows = V.rearrange("(s r) f -> r s f", r=PACK)

        def load_v(r):
            tile = buffer("v_raw_%d" % r, "v_raw_%d" % r, [P, K], F32)
            nc.sync.dma_start(out=tile[:], in_=v_rows[r])
            return tile

        u_raw = [load_half("u_raw", U, 0), load_half("u_raw", U, 1)]
        x_raw = [load_half("x_raw", xT, 0)]
        dz_sb = [load_half("dz", dz, 0)]
        v_raw = [load_v(0)]
        v_raw.append(load_v(1))
        offsets = sb.tile([P, SAMPLES // 16], U16, name="offsets")
        nc.sync.dma_start(offsets[:], offs)
        x_raw.append(load_half("x_raw", xT, 1))
        dz_sb.append(load_half("dz", dz, 1))
        v_raw.extend([load_v(2), load_v(3)])

        ident = sb.tile([P, P], F32, name="ident")
        zeros = buffer("zeros", "zeros", [P, P], F32)
        nc.gpsimd.memset(zeros[:], 0.0)
        nc.gpsimd.affine_select(
            out=ident[:],
            in_=zeros[:],
            compare_op=mybir.AluOpType.not_equal,
            fill=1.0,
            base=0,
            pattern=[[-1, P]],
            channel_multiplier=1,
        )

        dv_codes = buffer("dv_codes", "dv_codes", [P, SAMPLES], U32)
        dv_scales = buffer("dv_scales", "dv_scales", [P, SAMPLES], U8)
        windows = {}

        def clear(r, engine):
            windows[r] = buffer("window_%d" % r, "window_%d" % r, [P, ITEMS], F32)
            engine.memset(windows[r][:], 0.0)

        for r in range(PACK - 1):
            clear(r, nc.vector)

        si_ps = bank(0, "si_ps")
        si_columns = si_ps[:].rearrange("p (n j) -> p j n", j=PACK)
        for j in range(PACK):
            nc.tensor.transpose(si_columns[:, j, :], si_sb[:, j : j + 1].to_broadcast([P, P]), ident[:])

        u_codes = buffer("u_codes", "u_codes", [P, K], U32)
        u_scales = buffer("u_scales", "u_scales", [P, K], U8)
        u_bf = [buffer("u_bf_%d" % h, "u_bf_%d" % h, [P, PACK, P // 2 * PACK], BF16) for h in range(2)]
        for h in range(2):
            u_dst = u_bf[h][:].rearrange("p t (m j) -> p m j t", j=PACK)
            u_src = u_raw[h][:].rearrange("p j (m t) -> p m j t", t=PACK)
            if h == 0:
                nc.vector.tensor_copy(out=u_dst, in_=u_src)
            else:
                nc.vector.tensor_copy(out=u_dst[:, 0:U_VECTOR], in_=u_src[:, 0:U_VECTOR])
                nc.scalar.copy(out=u_dst[:, U_VECTOR : P // 2], in_=u_src[:, U_VECTOR : P // 2])
        for h in range(2):
            for t in range(PACK):
                cols = slice(t * P + h * P // 2, t * P + (h + 1) * P // 2)
                nc.vector.quantize_mx(out=u_codes[:, cols].bitcast(E4M3), scales=u_scales[:, cols], in_=u_bf[h][:, t, :])

        v_bf = [buffer("v_bf_%d" % r, "v_bf_%d" % r, [P, K], BF16) for r in range(PACK)]
        v_codes = []
        v_scales = buffer("v_scales", "v_scales", [P, K], U8)

        def gpsimd_round(out, in_):
            nc.gpsimd.tensor_scalar(out, in_, 1.0, -0.0, MULT, ADD)

        def round_v(r, rounded, first, copy):
            count = rounded.shape[1] // (2 * P)
            copy(
                out=rounded.rearrange("s (u p e) -> s u p e", u=count, e=2),
                in_=v_raw[r][:].rearrange("s (p u e) -> s u p e", u=2, e=2)[:, first : first + count],
            )
            return [rounded.bitcast(F32)[:, u * P : (u + 1) * P] for u in range(count)]

        def turn_v(r, words):
            turned = bank(V_BANKS[r], "v_turned_%d" % r)
            for u in range(2):
                nc.tensor.transpose(turned[:, u * P : (u + 1) * P], words[u], ident[:])
            nc.scalar.copy(
                out=v_bf[r][:].bitcast(F32).rearrange("p (s u) -> p s u", u=2),
                in_=turned[:, 0 : 2 * P].rearrange("p (u s) -> p s u", u=2),
            )

        def quantise_v(r, tag):
            v_codes.append(buffer(tag, "v_codes_%d" % r, [P, P], U32)[:])
            nc.vector.quantize_mx(out=v_codes[r].bitcast(E4M3), scales=v_scales[:, r * P : (r + 1) * P], in_=v_bf[r][:])

        x_codes = [buffer("x_codes_%d" % q, "x_codes_%d" % q, [P, P], U32) for q in range(4)]
        x_scales = [buffer("x_scales_%d" % q, "x_scales_%d" % q, [P, P], U8) for q in range(4)]
        dv_bf = [buffer("dv_bf_%d" % q, "dv_bf_%d" % q, [P, P * PACK], BF16)[:] for q in range(4)]

        def interleave_x(x_bf, h, o, copy):
            copy(
                out=x_bf.rearrange("p (c i j) -> p c j i", i=4, j=PACK),
                in_=x_raw[h][:, :, o * P : (o + 1) * P].rearrange("p j (c i) -> p c j i", i=4),
            )

        def quantise_x(x_bf, h, o):
            nc.vector.quantize_mx(
                out=x_codes[2 * h + o][:].bitcast(E4M3),
                scales=x_scales[2 * h + o][:],
                in_=x_bf,
            )

        def make_u(h, o):
            u_ps = bank(U_BANKS[2 * h + o], "u_%d_%d" % (h, o))
            for t in range(PACK):
                nc.tensor.matmul_mx(
                    out=u_ps[:, t * P : (t + 1) * P],
                    lhsT=u_codes[:, t * P : (t + 1) * P].bitcast(E4M3),
                    lhsT_scale=u_scales[:, t * P : (t + 1) * P],
                    rhs=x_codes[2 * h + o][:].bitcast(E4M3),
                    rhs_scale=x_scales[2 * h + o][:],
                    start=True,
                    stop=True,
                )
            return u_ps

        def make_g(g, h):
            steps = [(t, 0, HALF) for t in range(2)] + [(t, lo, lo + P) for lo in (0, P) for t in range(2, PACK)]
            for t, lo, hi in steps:
                nc.vector.scalar_tensor_tensor(
                    out=g[:, t, lo:hi],
                    in0=dz_sb[h][:, t, lo:hi],
                    scalar=cf_sb[:, t : t + 1],
                    in1=si_ps[:, h * HALF + lo : h * HALF + hi],
                    op0=MULT,
                    op1=MULT,
                )

        def make_dv(u_ps, g, h, o):
            nc.vector.tensor_tensor(
                out=dv_bf[2 * h + o].rearrange("p (c i t) -> p c t i", i=4, t=PACK),
                in0=u_ps[:].rearrange("p (t c i) -> p c t i", t=PACK, i=4),
                in1=g.rearrange("p t (c i) -> p c t i", i=4),
                op=MULT,
            )

        def quantise_dv(q):
            cols = slice(q * P, (q + 1) * P)
            nc.vector.quantize_mx(out=dv_codes[:, cols].bitcast(E5M2), scales=dv_scales[:, cols], in_=dv_bf[q])

        def product(r, number, lo, hi):
            acc = bank(number, "de_ps_%d_%d" % (r, lo))
            nc.tensor.matmul_mx(
                out=acc[:, 0 : hi - lo],
                lhsT=v_codes[r].bitcast(E4M3),
                lhsT_scale=v_scales[:, r * P : (r + 1) * P],
                rhs=dv_codes[:, lo:hi].bitcast(E5M2),
                rhs_scale=dv_scales[:, lo:hi],
                start=True,
                stop=True,
            )
            return acc[:, 0 : hi - lo]

        def copy_out(acc, tag, name, copy=nc.scalar.copy):
            de = buffer(tag, name, [P, acc.shape[1]], F32)
            copy(out=de[:], in_=acc)
            return de[:]

        def scatter_vector(r, lo, hi, de):
            nc.vector.tensor_copy(windows[r][:].indirect(offsets[:, lo // 16 : hi // 16]), de)

        def scatter_scalar(r, lo, hi, de):
            nc.scalar.activation(windows[r][:].indirect(offsets[:, lo // 16 : hi // 16]), de, COPY)

        out_rows = out_0.rearrange("(s r) c -> r s c", r=PACK)

        def store_plane(r):
            nc.sync.dma_start(out=out_rows[r], in_=windows[r][:])

        x_early = buffer("", "x_early", [P, PAD + HALF * PACK], BF16)
        x_bf = [x_early[:, PAD + o * P * PACK : PAD + (o + 1) * P * PACK] for o in range(2)]
        interleave_x(x_bf[0], 0, 0, nc.vector.tensor_copy)
        interleave_x(x_bf[1], 0, 1, nc.vector.tensor_copy)
        quantise_x(x_bf[0], 0, 0)
        quantise_x(x_bf[1], 0, 1)
        clear(3, nc.gpsimd)
        u_ps = [make_u(0, 0), make_u(0, 1)]
        g = buffer("", "g_0", [P, PACK, HALF], F32)
        make_g(g, 0)
        for o in range(2):
            make_dv(u_ps[o], g[:, :, o * P : (o + 1) * P], 0, o)
        words = [
            round_v(r, buffer("", "v_rounded_%d_%d" % (r, u), [P, K // 2], BF16)[:], u, nc.scalar.copy)[0]
            for r in range(2)
            for u in range(2)
        ]
        for r in range(2):
            turn_v(r, words[2 * r : 2 * r + 2])
        quantise_dv(0)
        quantise_dv(1)
        quantise_v(0, "v_codes_0")
        scatter_scalar(0, 0, HALF, copy_out(product(0, 7, 0, HALF), "de_0a", "de_0a"))

        x_bf = [
            buffer("", "x_late_0", [P, P * PACK], BF16)[:],
            buffer("", "x_late_1", [P, P * PACK], BF16)[:],
        ]
        interleave_x(x_bf[0], 1, 0, nc.vector.tensor_copy)
        interleave_x(x_bf[1], 1, 1, nc.vector.tensor_copy)
        quantise_x(x_bf[0], 1, 0)
        quantise_v(1, "")
        quantise_x(x_bf[1], 1, 1)
        u_ps = [make_u(1, 0), make_u(1, 1)]
        early = product(1, 5, 0, HALF)
        g = buffer("", "g_1", [P, PACK, HALF], F32)
        make_g(g, 1)
        for r in range(2, PACK):
            rounded = buffer("", "v_rounded_%d" % r, [P, K], BF16)[:]
            turn_v(r, round_v(r, rounded, 0, gpsimd_round))
        scatter_scalar(1, 0, HALF, copy_out(early, "", "de_1a"))
        for o in range(2):
            make_dv(u_ps[o], g[:, :, o * P : (o + 1) * P], 1, o)
        quantise_dv(2)
        quantise_v(2, "")
        quantise_dv(3)
        quantise_v(3, "")
        de_0b = buffer("de_0b", "de_0b", [P, HALF], F32)
        for o, number in enumerate((2, 0)):
            nc.vector.tensor_copy(out=de_0b[:, o * P : (o + 1) * P], in_=product(0, number, HALF + o * P, HALF + (o + 1) * P))
        de_1b = copy_out(product(1, 7, HALF, SAMPLES), "de_1b", "de_1b", nc.vector.tensor_copy)
        scatter_vector(0, HALF, SAMPLES, de_0b[:])
        store_plane(0)
        de_2 = copy_out(product(2, 3, 0, SAMPLES), "", "de_2")
        de_3 = copy_out(product(3, 4, 0, SAMPLES), "", "de_3")
        scatter_vector(1, HALF, SAMPLES, de_1b)
        store_plane(1)
        scatter_scalar(2, 0, HALF, de_2[:, 0:HALF])
        scatter_vector(2, HALF, SAMPLES, de_2[:, HALF:SAMPLES])
        store_plane(2)
        scatter_scalar(3, 0, HALF, de_3[:, 0:HALF])
        scatter_scalar(3, HALF, SAMPLES, de_3[:, HALF:SAMPLES])
        store_plane(3)

        y_bf = sb.tile([P, ITEMS * PACK], BF16, name="y_bf", align_bytes=64)
        y_codes = sb.tile([P, ITEMS], U32, name="y_codes", align_bytes=64)
        y_scales = sb.tile([P, ITEMS // PACK], U8, name="y_scales", align_bytes=64)
        y_words = y_bf[:].bitcast(F32)
        words_out = out_1[0].rearrange("p c l -> p (c l)").bitcast(I32)

        def quantise_y(lo, hi):
            group, column = divmod(lo, ITEMS // PACK)
            nc.vector.quantize_mx(
                out=y_codes[:, lo:hi].bitcast(E4M3),
                scales=y_scales[4 * group : P, column : column + hi - lo],
                in_=y_bf[:, PACK * lo : PACK * hi],
            )
            if hi in STORE_ENDS:
                first = STORE_ENDS[STORE_ENDS.index(hi) - 1]
                nc.sync.dma_start(out=words_out[:, first:hi], in_=y_codes[:, first:hi].bitcast(I32))

        spans = [(0, GPSIMD_TO, CHUNK), (GPSIMD_TO, TURNED_FROM, TURNED_FROM - GPSIMD_TO)]
        pairs = [buffer("pairs_%d" % n, "pairs_%d" % n, [P, (hi - lo) * PACK], BF16) for n, (lo, hi, width) in enumerate(spans)]

        def round_plane(r, n, copy):
            a, l = divmod(r, 2)
            lo, hi, width = spans[n]
            copy(
                out=pairs[n][:].rearrange("p (n a c l) -> p n a c l", a=2, c=width, l=2)[:, :, a, :, l],
                in_=windows[r][:, lo:hi].rearrange("p (n c) -> p n c", c=width),
            )

        def weave(n, lo, hi):
            first = lo - spans[n][0]
            nc.vector.tensor_copy(
                out=y_words[:, 2 * lo : 2 * hi].rearrange("p (c i a) -> p c a i", i=4, a=2),
                in_=pairs[n][:].bitcast(F32)[:, 2 * first : 2 * (first + hi - lo)].rearrange("p (a c i) -> p c a i", i=4, a=2),
            )

        for r in range(2):
            round_plane(r, 0, gpsimd_round)
        for r in range(PACK):
            if r >= 2:
                round_plane(r, 0, nc.vector.tensor_copy)
            round_plane(r, 1, nc.vector.tensor_copy)

        pieces = list(zip(TURNED_EDGES[:-1], TURNED_EDGES[1:]))

        def turn_pair(a, n):
            lo, hi = pieces[n]
            turned = bank(PAIR_BANKS[a][n], "pair_%d_%d" % (a, n))
            for b in range((hi - lo) // P):
                for l in range(2):
                    nc.tensor.transpose(
                        turned[:, (2 * b + l) * P : (2 * b + l + 1) * P],
                        windows[2 * a + l][:, lo + b * P : lo + (b + 1) * P],
                        ident[:],
                    )
            return turned[:, 0 : 2 * (hi - lo)]

        def round_pair(a, n, turned):
            lo, hi = pieces[n]
            z = buffer("z_%d_%d" % (a, n), "z_%d_%d" % (a, n), [P, 2 * (hi - lo)], BF16)
            nc.scalar.copy(
                out=z[:].rearrange("c (b p l) -> c b p l", p=P, l=2),
                in_=turned.rearrange("c (b l p) -> c b p l", p=P, l=2),
            )
            return z[:].bitcast(F32)

        def turn_back(a, n, z, back):
            lo, hi = pieces[n]
            for b in range((hi - lo) // P):
                nc.tensor.transpose(back[:, (2 * b + a) * P : (2 * b + a + 1) * P], z[:, b * P : (b + 1) * P], ident[:])

        def weave_out(back, first, lo, hi):
            nc.scalar.copy(
                out=y_words[:, 2 * lo : 2 * hi].rearrange("p (b c a) -> p b c a", c=P, a=2),
                in_=back[:, 2 * (lo - first) : 2 * (hi - first)].rearrange("p (b a c) -> p b c a", c=P, a=2),
            )

        turned = [[turn_pair(a, n) for n in range(len(pieces))] for a in range(2)]
        low = [round_pair(0, n, turned[0][n]) for n in range(len(pieces))]
        backs = []
        for n in range(len(pieces) + LAG):
            if n < len(pieces):
                high = round_pair(1, n, turned[1][n])
                backs.append(bank(PAIR_BANKS[0][n], "back_%d" % n))
                turn_back(0, n, low[n], backs[n])
                turn_back(1, n, high, backs[n])
            if n >= LAG:
                lo, hi = pieces[n - LAG]
                cuts = [lo, hi] if hi < ITEMS else [lo, hi - P, hi]
                for cut_lo, cut_hi in zip(cuts[:-1], cuts[1:]):
                    weave_out(backs[n - LAG], lo, cut_lo, cut_hi)

        woven = [(0, lo, lo + CHUNK) for lo in range(0, GPSIMD_TO, CHUNK)] + [(1, GPSIMD_TO, TURNED_FROM)]
        for n, piece in enumerate(woven):
            weave(*piece)
            if n >= 1:
                quantise_y(*woven[n - 1][1:])
        quantise_y(*woven[-1][1:])
        for lo, hi in pieces[:-1] + [(ITEMS - CHUNK, ITEMS - P), (ITEMS - P, ITEMS)]:
            quantise_y(lo, hi)

        scales_out = out_2[0].bitcast(I32).rearrange("(q j) (g c) -> q g j c", j=4, g=4)
        for quad in range(4):
            nc.sync.dma_start(out=scales_out[quad], in_=y_scales[32 * quad : 32 * quad + 16, :].bitcast(I32))
